import numpy as np, ml_dtypes
CORES = [16,18,20,22]
N = 4
import mx_ref
BF = ml_dtypes.bfloat16
def gentries(a):
    return np.ascontiguousarray(a.reshape(8, 16, -1).transpose(0, 2, 1)).reshape(8, -1)
def gtable(e):
    e = np.asarray(e); return np.ascontiguousarray(e.reshape(8, -1, 16).transpose(0, 2, 1)).reshape(128, -1).astype(np.int32)
def gcols(t, e):
    v = np.concatenate([t.reshape(8, 16, -1, 4), np.zeros((8, 16, 1, 4), BF)], axis=2)
    return np.ascontiguousarray(np.stack([v[g][:, e[g]] for g in range(8)])).reshape(128, -1)
def tile(rs):
    return np.stack(rs, axis=2).reshape(128, -1).astype(BF)
def cut(t, i, w=512):
    return t[:, w * i:w * i + w]
def pick(q, e):
    c = np.concatenate([q[0].reshape(128, -1, 4), np.zeros((128, 1, 4), np.uint8)], axis=1); s = np.concatenate([q[1], np.ones((16, 1), np.uint8)], axis=1)
    return (np.ascontiguousarray(c[:, e].reshape(128, -1)), np.ascontiguousarray(s[:, e]))
def join(*qs):
    return (np.concatenate([q[0] for q in qs], axis=1), np.concatenate([q[1] for q in qs], axis=1))
def put(q, e, v):
    c, s = q[0].reshape(128, -1, 4).copy(), q[1].copy(); c[:, e] = v[0].reshape(128, -1, 4); s[:, e] = v[1]
    return (c.reshape(128, -1), s)
def pk(c, s):
    return (np.ascontiguousarray(c), mx_ref.live(s))
def emit(q):
    return q[0], q[1]
def packed(v, rng):
    q = [mx_ref.quantize(np.ascontiguousarray(v[r])) for r in range(N)]
    return np.stack([a for a, b in q]), np.stack([mx_ref.plane(b, rng) for a, b in q])
def values_of_codes():
    e, c = np.zeros((128, 128, 4), np.float32), np.zeros((128, 2, 4), np.uint8)
    e[np.arange(128), np.arange(128), 0] = 1
    c[:127, :, 0] = np.arange(256).reshape(2, 128).T[:127]
    return mx_ref.matmul(mx_ref.quantize(e.reshape(128, 512).astype(BF)), (c.reshape(128, 8), np.full((16, 2), 127, np.uint8))).T.reshape(-1).astype(np.float64)
CODE_VALUE, SCALE_VALUE = values_of_codes(), 2.0 ** (np.arange(256) - 127.0)
def decode(q):
    return (CODE_VALUE[q[0]].reshape(16, 8, -1, 4) * SCALE_VALUE[q[1]][:, None, :, None] + 0.0).reshape(128, -1).astype(np.float32)
def f(rng, *shape):
    return mx_ref.flush((rng.standard_normal(shape, dtype=np.float32) * np.exp2(rng.integers(-2, 3, shape[:-1] + (1,)))).astype(BF))
def wide(rng, *shape, cols=0):
    v = rng.standard_normal(shape, dtype=np.float32) * np.exp2(rng.integers(-12, 13, shape)).astype(np.float32)
    if cols: v *= np.repeat(np.exp2(rng.integers(-cols, cols + 1, shape[:-2] + (1, shape[-1] // 4))) * (rng.random(shape[:-2] + (1, shape[-1] // 4)) > 0.0625), 4, axis=-1).astype(np.float32)
    return mx_ref.flush(v.astype(BF))
C, V, K, R = 384, 48, 128, 3
STEP = [1, 2, 1]
def big(v):
    v = v.astype(np.float32)
    v[np.abs(v) < np.float32(2.0 ** -16)] = 0
    return v.astype(BF)
def lists(a):
    return np.stack([gtable(a[r]) for r in range(N)])
def numbers_of(rng):
    return {"x": big(f(rng, N, 128, 4 * C)), "e": big(f(rng, N, 128, 16 * V)), "ex": lists(rng.integers(0, V, (N, 8, 4 * V))), "at": lists(rng.integers(0, V, (N, 8, C))), "u": np.array(f(rng, N, 128, 512)), "v": np.array(f(rng, N, 128, 512))}
def layers(rng):
    return big(f(rng, N, 128, 2048)).reshape(N, 8, 16, 4, 8, 16, 4)
def weights(rng, w):
    c, p = packed(np.ascontiguousarray(w).reshape(N, 128, 2048), rng)
    return {"wc": c, "ws": p}
def signs(rng):
    return np.stack([rng.permutation(8) % 2 * 2.0 - 1.0 for r in range(N)])
def setup_inputs(rng):
    return {**numbers_of(rng), **weights(rng, layers(rng))}
def setup_inputs_ties(rng):
    d = numbers_of(rng)
    o = rng.permutation(N)
    x, e = d["x"].reshape(N, 8, 16, C, 4), d["e"].reshape(N, 8, 16, 4 * V, 4)
    for r in range(N):
        k = np.zeros(C, int) if r == o[0] else rng.permutation(C) % 3
        a = x[r][:, :8, :3].copy()
        a[:, :, 2] = 0
        x[r][:, :8] = a[:, :, k]
        e[r][:, :8] = a[:, :, rng.permutation(4 * V) % 3]
    x[o[1]] = 0
    at = gentries(d["at"][o[1]]).copy()
    for g in rng.permutation(8)[:4]: at[g] = rng.integers(V)
    d["at"][o[1]] = gtable(at)
    u = d["u"].reshape(N, 8, 16, 128, 4)
    u[:, :, 8:, ::16] = 0
    d["x"], d["e"], d["u"] = x.reshape(N, 128, 4 * C), e.reshape(N, 128, 16 * V), u.reshape(N, 128, 512)
    w = layers(rng)
    w[:, :, 8:, :, :, :8] = 0
    return {**d, **weights(rng, w)}
def setup_inputs_near(rng):
    d = numbers_of(rng)
    m = C + 4 * V
    x = np.zeros((N, 8, 16, m, 4), np.float32)
    at = np.zeros((N, 8, C), int)
    u = d["u"].reshape(N, 128, 128, 4)
    u[:, :, ::16] = 0
    o, c = rng.permutation(N) % 4, signs(rng)
    x[:, :, 10:] = rng.integers(4, 8, (N, 8, 6, m, 4)) * 2.0 ** -20
    for r in range(N):
        if o[r] < 2:
            s = ((np.arange(m) + rng.integers(0, C, (8, 1))) % C + 1) // 2
            g = ((s[:, :, None] >> np.arange(8)) & 1) * np.exp2(np.arange(8) - 23.0)
            x[r, :, :2, :, 0] = c[r][:, None, None]
            x[r, :, 8] = g[:, :, :4]
            x[r, :, 9] = g[:, :, 4:]
            at[r] = np.argsort(rng.random((8, V)), axis=1)[:, np.arange(C) // 8]
        else:
            x[r, :, :2, :, 0] = rng.integers(8, 14, (8, 2, m)) * 2.0 ** -31
            at[r] = rng.integers(0, 4, (8, C))
        k = 1.0 if o[r] == 0 else 2.0 ** -30
        for h in range(0, 128, 16):
            u[r, h, h, 0] = k
            u[r, h + 8:h + 10, h] = k
            if o[r] >= 2:
                u[r, h, h, 0] = 9 * 2.0 ** -33
                u[r, h + 1, h, 0] = 8 * 2.0 ** -33
    x = x.astype(BF)
    d["x"], d["e"] = np.ascontiguousarray(x[:, :, :, :C]).reshape(N, 128, 4 * C), np.ascontiguousarray(x[:, :, :, C:]).reshape(N, 128, 16 * V)
    d["at"], d["u"] = lists(at), u.reshape(N, 128, 512)
    w = layers(rng)
    w[:, :, :10] = 0
    w[:, :, :, :, :, :10] = 0
    return {**d, **weights(rng, w)}
def setup_inputs_huge(rng):
    d = numbers_of(rng)
    m = C + 4 * V
    c = rng.integers(0, 2, (N, m)) * 2.0 - 1.0
    c[:, :C] = np.stack([rng.permutation(C) % 2 * 2.0 - 1.0 for r in range(N)])
    c[rng.permutation(N) < N // 2] = -1
    x = ((0.6 + 0.2 * rng.random((N, 128, m, 4))) * np.where(c < 0, -2.0 ** 30, 2.0 ** 28)[:, None, :, None]).astype(np.float32).astype(BF)
    d["x"], d["e"] = np.ascontiguousarray(x[:, :, :C]).reshape(N, 128, 4 * C), np.ascontiguousarray(x[:, :, C:]).reshape(N, 128, 16 * V)
    u = d["u"].reshape(N, 128, 128, 4)
    a = 2.0 ** 30 * (1 - 0.25 * rng.random((N, 128, 8, 4))) * signs(rng)[:, None, :, None]
    u[:, :, ::16] = a.astype(np.float32).astype(BF)
    d["u"] = u.reshape(N, 128, 512)
    w = np.zeros((N, 128, 4, 128, 4), np.float32)
    i = np.arange(128)
    for b in range(4): w[:, i, b, i, b] = 16
    return {**d, **weights(rng, w.astype(BF))}
def setup_inputs_crowd(rng):
    d = setup_inputs(rng)
    at, ex = rng.integers(0, V, (N, 8, C)), rng.integers(0, V, (N, 8, 4 * V))
    for r in range(N):
        for g, i in enumerate(rng.permutation(8)):
            a, b = rng.permutation(V)[:2]
            if i < 4:
                at[r, g] = np.where(rng.permutation(C) < C - i, a, b)
                ex[r, g, 4 * a:4 * a + 4] = a
                ex[r, g, 4 * b:4 * b + 4] = b
            if i == 4: ex[r, g] = a
            if i == 5:
                at[r, g] = rng.integers(K // 4, V, C)
                ex[r, g] = rng.integers(K // 4, V, 4 * V)
            if i == 6:
                at[r, g] = rng.integers(0, K // 4, C)
                ex[r, g] = rng.integers(0, K // 4, 4 * V)
            if i == 7:
                at[r, g] = rng.permutation(C) % V
                ex[r, g] = (np.arange(4 * V) // 4 + 1) % V
    d["ex"], d["at"] = lists(ex), lists(at)
    return d
def setup_inputs_spread(rng):
    d = setup_inputs(rng)
    d["x"], d["e"] = big(wide(rng, N, 128, 4 * C, cols=6)), big(wide(rng, N, 128, 16 * V, cols=6))
    return d
def check_inputs(d):
    b = []
    for k in ("x", "e", "u", "v"):
        a = np.abs(d[k].astype(np.float32))
        if not (np.isfinite(a).all() and ((a == 0) | (a >= 2.0 ** -30) & (a <= 2.0 ** 30)).all()): b.append("a value of " + k)
    for k in ("ex", "at"):
        if ((d[k] < 0) | (d[k] >= V)).any(): b.append("an entry of " + k)
    none, least, most = [emit(mx_ref.quantize(np.full((128, 16), k, np.float32).astype(BF)))[1][0, 0] for k in (0.0, 2.0 ** -30, 2.0 ** 30)]
    for r in range(N):
        if ((d["wc"][r] == 0x7F) | (d["wc"][r] == 0xFF)).any(): b.append("wc: a code that is no number")
        s = mx_ref.live(d["ws"][r])
        if ((s != none) & ((s < least) | (s > most))).any(): b.append("ws: a scale out of range")
    return b
def reference(x, e, ex, at, u, v, wc, ws):
    qu = [mx_ref.quantize(u[r]) for r in range(N)]
    lay = [pk(wc[r], ws[r]) for r in range(N)]
    now, mem = [x[r] for r in range(N)], [e[r] for r in range(N)]
    to, node = [gentries(ex[r]) for r in range(N)], [gentries(at[r]) for r in range(N)]
    rot = [np.zeros((8, V), np.int64) for r in range(N)]
    came_by = [None] * N
    num, group = np.arange(C), np.arange(8)[:, None]
    for t in range(R):
        sent = []
        for r in range(N):
            s = mx_ref.matmul(qu[r], mx_ref.quantize(now[r]))[::16] + np.float32(0.0)
            n, a, b = node[r], s[:, :, None], s[:, None, :]
            first = (n[:, :, None] == n[:, None, :]) & ((a > b) | (a == b) & (num[:, None] < num))
            k = np.sum(first, axis=1)
            way = 4 * n + (rot[r][group, n] + k) % 4
            o = np.lexsort((k, way))
            w = np.take_along_axis(way, o, axis=1)
            follows = np.zeros((8, C), bool)
            follows[:, 1:] = w[:, 1:] == w[:, :-1]
            pred = np.zeros((8, C), np.int64)
            np.put_along_axis(pred, o, np.where(follows, np.roll(o, 1, axis=1), C + w), axis=1)
            last = np.tile(C + np.arange(4 * V), (8, 1))
            g, i = np.nonzero(np.concatenate([~follows[:, 1:], np.ones((8, 1), bool)], axis=1))
            last[g, w[g, i]] = o[g, i]
            p = gcols(np.concatenate([now[r], mem[r]], axis=1), pred)
            z = ((now[r].astype(np.float32) + p.astype(np.float32)) * np.float32(0.5)).astype(BF)
            q = mx_ref.quantize(z)
            h = tile([np.maximum(mx_ref.matmul(pick(lay[r], np.arange(128 * b, 128 * b + 128)), q), np.float32(0.0)) * np.float32(0.03125) + z[:, b::4].astype(np.float32) for b in range(4)])
            mem[r] = gcols(np.concatenate([h, mem[r]], axis=1), last)
            rot[r] = (rot[r] + np.sum(n[:, :, None] == np.arange(V), axis=1)) % 4
            stack = np.lexsort((k, way, to[r][group, way]))
            now[r] = gcols(h, stack)
            came_by[r] = np.take_along_axis(way, stack, axis=1)
            node[r] = to[r][group, came_by[r]]
            sent.append(mx_ref.quantize(np.ascontiguousarray(cut(mem[r], 0, 4 * K))))
        came = decode(join(*sent)).astype(BF)
        for r in range(N): mem[r] = np.concatenate([cut(came, r ^ STEP[t], 4 * K), mem[r][:, 4 * K:]], axis=1)
    y, ot = np.zeros((N, 128, C), np.float32), np.zeros((N, 8, C), np.float32)
    oc, osc = np.zeros((N, 128, 16 * V), np.uint8), np.zeros((N, 16, 4 * V), np.uint8)
    for r in range(N):
        y[r] = mx_ref.matmul(mx_ref.quantize(v[r]), mx_ref.quantize(now[r]))
        ot[r] = came_by[r]
        oc[r], osc[r] = emit(mx_ref.quantize(np.ascontiguousarray(mem[r])))
    return {"y": y, "ot": ot, "oc": oc, "osc": osc}

@@ -1,0 +1,652 @@
+import numpy as np
+from concourse.mybir import dt, AluOpType, ActivationFunctionType
+
+A = AluOpType
+F = ActivationFunctionType
+C, V, K, ROUNDS = 384, 48, 128, 3
+E = 4 * V
+STEP = [1, 2, 1]
+NB = C // 16
+BIG = 2.0 ** 80
+F32, BF, I32, U16, F16 = "float32", "bfloat16", "int32", "uint16", "float16"
+CODE, PLANE = "float8_e4m3fn_x4", "uint8"
+ACT_ROWS = (0, 2, 4, 6, 8, 10, 12, 14, 16, 18, 20)
+SIG, GAP, PASSES, SEED, PLAN = (500, 2500, 9000), 40, 4500, 2, {}
+
+
+def _sb(n, d):
+    return ("sbuf", [128, n], d)
+
+
+SCRATCH = {
+    "ati": _sb(24, I32), "exi": _sb(12, I32), "ub": _sb(512, BF), "vb": _sb(512, BF),
+    "wq": _sb(512, CODE), "wp": _sb(512, PLANE), "uq": _sb(128, CODE), "up": _sb(128, PLANE),
+    "uq2": _sb(128, CODE), "up2": _sb(128, PLANE), "vq": _sb(128, CODE), "vp": _sb(128, PLANE),
+    "num": _sb(640, F32), "numb": _sb(2176, F32), "t512": _sb(64, F32), "e4096": _sb(E, F32),
+    "pi": _sb(8, I32), "pm": _sb(8, F32), "i16": _sb(416, BF), "dm": _sb(C, BF), "a1": _sb(C, BF), "keep": _sb(416, BF),
+    "cc": _sb(C, BF), "cc2": _sb(C, BF), "half": _sb(64, BF), "ones": _sb(512, BF), "c1": _sb(512, BF), "gb": _sb(512, BF),
+    "eb": _sb(2048, BF), "zb": _sb(1024, BF), "gq": _sb(128, CODE), "gp": _sb(128, PLANE), "eq": _sb(512, CODE),
+    "ep": _sb(512, PLANE), "zq0": _sb(256, CODE), "zp0": _sb(256, PLANE),
+    "ci": _sb(256, I32), "cf": _sb(256, F32), "cu": _sb(128, U16), "uo": _sb(8, U16),
+    "krep": _sb(C, F32), "ksort": _sb(C, F32), "lt": _sb(C * 3, BF), "cs": _sb(C * 3, F32), "nrp": _sb(C, BF),
+    "ff": _sb(416, F16), "tr": _sb(800, F16), "trs": _sb(800, F16),
+    "junk": _sb(23 * C, BF), "th": _sb(64, F32), "acc": _sb(64, F32), "su": _sb(128, U16),
+    "xrep": _sb(E, F32), "to4": _sb(E, F32), "sig": _sb(E, F32), "sig2": _sb(E, F32), "sigw": _sb(12, F32),
+    "s0rep": _sb(C, F32), "wa": _sb(C, F32), "wb": _sb(C, F32),
+    "li": _sb(3 * 256, I32), "lf": _sb(3 * 128, F32), "lu": _sb(3 * 128, U16), "land": _sb(4 * 96, F32), "ro": _sb(48, I32),
+    "landn": _sb(3 * 8, F32), "crep": _sb(E, F32), "csrt": _sb(E, F32), "pf": _sb(208, F32), "g1": _sb(272, F32),
+    "g2": _sb(2 * 704, F32), "vrep": _sb(E, F32), "vw": _sb(3 * 576, F32), "vk": _sb(C, BF), "vs": _sb(C, F32),
+    "vg": _sb(2 * 768, F32), "d0": _sb(3 * 448, BF), "ml": _sb(3 * 24 * 24, U16), "tab": _sb(3 * 576, F32),
+    "ssb": _sb(400, F32), "sa": _sb(C, F32), "yy": _sb(C, F32), "ut": _sb(6 * 1536, BF), "utq": _sb(6 * C, CODE),
+    "utp": _sb(6 * C, PLANE), "sg": _sb(23 * C, BF), "rs": _sb(24, F32), "ds": _sb(C, F16), "pw": _sb(96, F32),
+    "pu": _sb(96, U16), "w1": _sb(C, F16), "w2": _sb(C, F16), "w3": _sb(C, F16), "w4": _sb(C, F16),
+    "srep": _sb(C, F32), "lrep": _sb(E, F32), "lrep2": _sb(E, F32), "land2": _sb(3 * 40, F32), "du": _sb(3 * 40, U16),
+    "xt": _sb(1536, BF), "xq": _sb(C, CODE), "xp": _sb(C, PLANE), "zt": _sb(1536, BF), "zq": _sb(C, CODE), "zp": _sb(C, PLANE),
+    "xmh": _sb(4 * 576, BF), "hm": _sb(4 * 576, BF), "rr": _sb(4 * 576, F32), "zl": _sb(768, BF), "xth": _sb(1536, BF),
+    "mt": _sb(768, BF), "mq": _sb(E, CODE), "mp": _sb(E, PLANE), "ysb": _sb(C, F32),
+    "bq0": _sb(K, CODE), "bp0": _sb(K, PLANE), "bq1": _sb(K, CODE), "bp1": _sb(K, PLANE), "bq2": _sb(K, CODE), "bp2": _sb(K, PLANE),
+    "aq0": _sb(K, CODE), "ap0": _sb(K, PLANE), "aq1": _sb(K, CODE), "ap1": _sb(K, PLANE), "aq2": _sb(K, CODE), "ap2": _sb(K, PLANE),
+    "ps": ("psum", [128, 4096], F32),
+}
+SEMAPHORES = ["dve", "act", "pe", "pool", "arr0", "arr1", "arr2", "out0", "out1", "out2"] + ["d%d" % i for i in range(80)]
+TWO = (BF, F16, U16)
+
+
+def _overlap(a, b):
+    if a[0] != b[0]:
+        return False
+    if a[0] == "ps":
+        return a[1] // 512 == b[1] // 512
+    if a[1] >= b[2] or b[1] >= a[2]:
+        return False
+    if a[3] == b[3] and a[3] > 1:
+        return (a[1] - b[1]) % a[3] == 0
+    return True
+
+
+def build(g, core, T, topo, rank):
+    ops = []
+    Q = {"dve": g.vector, "act": g.scalar, "pe": g.tensor, "pool": g, "sp": g.sync}
+
+    def r(name, a=0, b=None, s=1):
+        return (name, a, SCRATCH[name][1][1] if b is None else b, s)
+
+    def ind(win, off):
+        return ("ind", win, off)
+
+    def ap(x):
+        if x[0] == "ind":
+            return ap(x[1]).indirect(ap(x[2]))
+        if x[3] == 1:
+            return T[x[0]][:, x[1]:x[2]]
+        return T[x[0]][:, x[1]:x[2]:x[3]]
+
+    def regs(xs):
+        o = []
+        for x in xs:
+            if isinstance(x, tuple):
+                o += [x[1], x[2]] if x[0] == "ind" else [x]
+        return o
+
+    def cnt(x):
+        if x[0] == "ind":
+            return 16 * (x[2][2] - x[2][1])
+        return len(range(x[1], x[2], x[3]))
+
+    def val(x):
+        return ap(x) if isinstance(x, tuple) else x
+
+    def two(*xs):
+        return all(SCRATCH[x[0]][2] in TWO for x in xs)
+
+    def add(eng, fn, rd, wr, dur, lat=0, kind="c", chain=False, sem=None, early=0):
+        ops.append({"eng": eng, "fn": fn, "rd": regs(rd), "wr": regs(wr), "dur": dur, "lat": lat, "kind": kind,
+                    "chain": chain, "sem": sem, "early": early})
+
+    def vcost(out, ins, per):
+        if out[0] == "ind":
+            return 60 + 3.8 * cnt(out)
+        if ins[0][0] == "ind":
+            return 60 + 1.56 * cnt(out)
+        return max(64, per * cnt(out)) + 10
+
+    def cp(out, in_):
+        per = 1 if out[0] == "ind" or in_[0] == "ind" or not two(out, in_) else .5
+        add("dve", lambda: g.vector.tensor_copy(ap(out), ap(in_)), [in_] + ([out[2]] if out[0] == "ind" else []),
+            [out[1] if out[0] == "ind" else out], vcost(out, [in_], per))
+
+    def tt(out, a, b, op):
+        per = 1 if "ps" in (a[0], b[0]) else 2
+        add("dve", lambda: g.vector.tensor_tensor(ap(out), ap(a), ap(b), op), [a, b], [out], vcost(out, [a], per))
+
+    def ts(out, a, s1, op0, s2=None, op1=None):
+        per = 1 if a[0] == "ind" or not two(out, a) else .5
+        if op1 is None:
+            fn = lambda: g.vector.tensor_scalar(ap(out), ap(a), val(s1), None, op0)
+        else:
+            fn = lambda: g.vector.tensor_scalar(ap(out), ap(a), val(s1), val(s2), op0, op1)
+        add("dve", fn, [a, s1, s2], [out], vcost(out, [a], per))
+
+    def scan(out, d0, d1, op0, op1, init=0.0):
+        add("dve", lambda: g.vector.tensor_tensor_scan(ap(out), ap(d0), ap(d1), val(init), op0, op1), [d0, d1, init], [out],
+            vcost(out, [d0], .5 if two(out, d0, d1) else 1))
+
+    def mset(out, c):
+        add("dve", lambda: g.vector.memset(ap(out), c), [], [out], vcost(out, [out], .5 if two(out) else 1))
+
+    def quant(q, p, in_):
+        add("dve", lambda: g.vector.quantize_mx(ap(q), ap(p), ap(in_)), [in_], [q, p], 25 + .265 * cnt(in_))
+
+    def act(out, in_, func=F.Copy, bias=None, scale=None, acc=None):
+        def fn():
+            kw = {}
+            if bias is not None:
+                kw["bias"] = val(bias)
+            if scale is not None:
+                kw["scale"] = scale
+            if acc is not None:
+                kw["accum_out"] = ap(acc)
+            return g.scalar.activation(ap(out), ap(in_), func, **kw)
+        d = 78 + 1.56 * cnt(out) if in_[0] == "ind" else 60 + cnt(out)
+        add("act", fn, [in_, bias], [out, acc], d + (24 if acc else 0))
+
+    def mm(bank, n, lq, lp, rq, rp, start=True, stop=True):
+        o = r("ps", 512 * bank, 512 * bank + n)
+        add("pe", lambda: g.tensor.matmul_mx(ap(o), ap(lq), ap(lp), ap(rq), ap(rp), start, stop), [lq, lp, rq, rp], [o],
+            .7 * (n + 16), lat=80, chain=not start)
+
+    def ps(bank, n):
+        return r("ps", 512 * bank, 512 * bank + n)
+
+    def iota(out, pat, base=0, cm=0, early=0):
+        if SCRATCH[out[0]][2] == I32:
+            fn = lambda: g.iota(ap(out), pat, base, cm)
+        else:
+            fn = lambda: g.iota(ap(out), pat, base, cm, allow_small_or_imprecise_dtypes=True)
+        add("pool", fn, [], [out], 160 + 2 * cnt(out), early=early)
+
+    def sel(out, in_, pat, op, base, cm, fill=0.0):
+        add("pool", lambda: g.affine_select(ap(out), ap(in_), pat, op, fill, base, cm), [in_], [out], 200 + 2 * cnt(out))
+
+    def pcp(out, in_):
+        sel(out, in_, [[0, cnt(out)]], A.is_ge, 0, 0)
+
+    def dma(o, i, rd, wr, eng="sp", lat=2400):
+        add(eng, lambda: Q[eng].dma_start(o(), i()), rd, wr, 70, lat=lat, kind="dma")
+
+    def u8(x):
+        return ap(x).bitcast(dt.uint8)
+
+    def spread(dst, src):
+        dma(lambda: ap(dst), lambda: T[src[0]][0:128:16, src[1]:src[2]], [src], [dst])
+
+    num, numc = r("num"), r("num", 0, C)
+    dma(lambda: T.ati[:], lambda: T.at[:], [], [r("ati")])
+    dma(lambda: T.xt[:], lambda: T.x[:], [], [r("xt")], eng="act", lat=3000)
+    dma(lambda: T.exi[:], lambda: T.ex[:], [], [r("exi")])
+    dma(lambda: T.ub[:], lambda: T.u[:], [], [r("ub")])
+    dma(lambda: T.mt[:], lambda: T.e[:], [], [r("mt")])
+    dma(lambda: u8(r("wq")), lambda: T.wc[:], [], [r("wq")])
+    dma(lambda: T.wp[:], lambda: T.ws[:], [], [r("wp")])
+    dma(lambda: T.vb[:], lambda: T.v[:], [], [r("vb")])
+    iota(r("pi", 0, 1), [[0, 1]], 0, 1, early=4e4)
+    iota(r("ci", 0, 24), [[16, 24]], early=3e4)
+    iota(r("t512"), [[512, 64]], early=2e4)
+    iota(numc, [[1, C]], early=1e4)
+    iota(r("num", C, 640), [[1, 640 - C]], C)
+    iota(r("i16"), [[0, NB + 2], [1, 16]], early=5e3)
+    iota(r("numb"), [[1, 2176]])
+    iota(r("e4096"), [[4096, E]])
+    ts(r("pi", 2, 3), r("pi", 0, 1), 15, A.bitwise_and)
+    cp(r("pm", 0, 1), r("pi", 2, 3))
+    pm, keep = r("pm", 0, 1), r("keep", 0, C)
+    ts(r("dm"), r("i16", 0, C), pm, A.is_equal)
+    ts(r("a1"), r("i16", 0, C), pm, A.not_equal, BIG, A.mult)
+    ts(r("keep"), r("i16"), 0.0, A.is_gt)
+    act(r("cc2"), r("a1"), bias=BIG / 2, scale=-1.0)
+    sel(r("cc"), r("cc2"), [[0, NB], [1, 16]], A.is_gt, 0, 0, BIG / 2)
+    mset(r("half"), BIG / 2)
+    cp(r("uo"), r("ci", 0, 8))
+    jw = r("cf", 0, 24)
+    ts(jw, r("ci", 0, 24), pm, A.add)
+    j12, ga = r("cf", 0, 12), r("cf", 132, 156)
+
+    def turn(out, x, w, t1, t2, t3):
+        ts(t2, x, float(65536 // w + 1), A.mult)
+        ts(t1, t2, 16, A.arith_shift_right)
+        ts(t3, t1, -float(16 * w - 1) / 16, A.mult)
+        tt(t3, x, t3, A.add)
+        ts(out, t3, 16.0, A.mult)
+
+    turn(ga, jw, 24, r("ci", 24, 48), r("ci", 48, 72), r("cf", 200, 224))
+    turn(r("cu", 24, 48), ga, 24, r("ci", 72, 96), r("ci", 96, 120), r("cf", 224, 248))
+    turn(r("cu", 48, 60), j12, 12, r("ci", 120, 132), r("ci", 132, 144), r("cf", 48, 60))
+    cp(r("cu", 0, 24), ga)
+    g1216, px16 = r("cu", 48, 60), r("cu", 48, 92)
+    ts(r("ci", 144, 156), r("ci", 120, 132), 2, A.arith_shift_right)
+    ts(r("ci", 156, 168), r("ci", 120, 132), -48.0, A.mult, float(E), A.add)
+    tt(r("ci", 156, 168), r("ci", 156, 168), r("ci", 144, 156), A.add)
+    ts(r("cf", 84, 96), j12, 4.0, A.mult)
+    tt(r("cf", 84, 96), r("cf", 84, 96), r("ci", 156, 168), A.add)
+    cp(r("cu", 60, 72), r("cf", 84, 96))
+    ts(r("cu", 72, 84), r("cf", 84, 96), 1.0, A.add)
+    turn(r("cf", 192, 196), r("cf", 0, 4), 4, r("ci", 204, 208), r("ci", 208, 212), r("cf", 196, 200))
+    ts(r("cu", 84, 88), r("cf", 192, 196), float(E), A.add)
+    ts(r("cu", 88, 92), r("cf", 192, 196), float(E + 1), A.add)
+    csrc, e384, jw4, c4n = r("cf", 96, 120), r("cf", 120, 132), r("cf", 24, 48), r("ci", 212, 236)
+    ts(csrc, ga, 4.0, A.mult, -1536.0, A.add)
+    ts(e384, j12, float(C), A.add)
+    ts(jw4, jw, 4.0, A.add)
+    cp(r("ci", 168, 180), j12)
+    ts(r("ci", 192, 204), r("ci", 168, 180), 3, A.bitwise_and)
+    ts(r("ro", 0, 12), r("ci", 192, 204), -1.0, A.mult, 3.0, A.add)
+    for k in range(2):
+        tt(r("ci", 212 + 12 * k, 224 + 12 * k), r("ci", 168, 180), r("ro", 0, 12), A.add)
+    iota(r("ones"), [[0, 512]], 1)
+    sel(r("c1"), r("ones"), [[-16, 8], [0, 64]], A.is_ge, 0, 1)
+    sel(r("gb"), r("c1"), [[16, 8], [0, 64]], A.is_ge, 15, -1)
+    quant(r("gq"), r("gp"), r("gb"))
+    for k in range(6):
+        lo = 64 * min(k, 4)
+        iota(r("ut", 1536 * k + 4 * lo, 1536 * k + 4 * (64 * k + 48)), [[0, 4 * (64 * k + 48 - lo)]])
+    iota(r("zb"), [[0, 1024]])
+    quant(r("zq0"), r("zp0"), r("zb"))
+    for k in range(1, 6):
+        w = 64 * min(k, 4)
+        dq, dp = r("utq", C * k, C * k + w), r("utp", C * k, C * k + w)
+        dma(lambda dq=dq: u8(dq), lambda w=w: u8(r("zq0", 0, w)), [r("zq0")], [dq])
+        dma(lambda dp=dp: ap(dp), lambda w=w: ap(r("zp0", 0, w)), [r("zp0")], [dp])
+    for t in range(ROUNDS):
+        iota(r("tab", 576 * t, 576 * t + 576), [[0, 576]])
+        iota(r("vw", 576 * t, 576 * t + 576), [[0, 576]])
+        iota(r("d0", 448 * t + C, 448 * t + 448), [[0, 64]])
+    for b in range(4):
+        sel(r("eb", 512 * b, 512 * b + 512), r("ones"), [[-1, 512]], A.is_equal, b, 4)
+        iota(r("rr", 576 * b + C, 576 * b + 576), [[0, E]])
+    quant(r("eq"), r("ep"), r("eb"))
+    mset(r("ssb", C, 400), -BIG)
+    mset(r("rs", 23, 24), 0.0)
+    mset(r("pf", 0, 1), 0.0)
+    iota(r("g1"), [[0, 272]], C)
+    quant(r("uq"), r("up"), r("ub"))
+    add("dve", lambda: g.vector.tensor_copy(T.uq2[:].bitcast(dt.uint32), T.uq[:].bitcast(dt.uint32).indirect(T.uo[:, 0:8])),
+        [r("uq"), r("uo")], [r("uq2")], 260)
+    add("act", lambda: g.scalar.activation(T.up2[:], T.up[:].indirect(T.uo[:, 0:8]), F.Copy), [r("up"), r("uo")], [r("up2")], 280)
+    quant(r("vq"), r("vp"), r("vb"))
+
+    at16, rk16, st16, s016, ex16, ln16, sg16 = (r("su", 0, 24), r("su", 24, 48), r("su", 48, 52), r("su", 52, 76),
+                                                r("su", 76, 88), r("su", 88, 104), r("su", 104, 116))
+    cp(at16, r("ati"))
+    tt(r("krep"), ind(r("t512"), at16), numc, A.add)
+    act(r("nrp"), ind(numc, at16))
+    ts(r("th", 0, 4), r("cf", 0, 4), -1.0, A.mult, 0.5, A.add)
+    for m in range(4):
+        act(r("junk", C * m, C * m + C), r("nrp"), F.Sign, bias=r("th", m, m + 1), acc=r("acc", m, m + 1))
+    ts(st16, r("acc", 0, 4), -0.5, A.mult, C / 2, A.add)
+    ts(r("th", 4, 8), r("acc", 0, 4), -0.5, A.mult, C / 2 - 1, A.add)
+    for q in range(3):
+        ts(r("lt", C * q, C * q + C), r("nrp"), r("cf", q, q + 1), A.is_equal)
+        scan(r("cs", C * q, C * q + C), r("ones", 0, C), r("lt", C * q, C * q + C), A.mult, A.add, r("th", 4 + q, 5 + q))
+    ts(r("li", 0, 24), r("ati"), 4, A.arith_shift_right)
+    ts(r("th", 8, 32), r("li", 0, 24), float(C), A.mult)
+    tt(r("th", 8, 32), r("th", 8, 32), jw, A.add)
+    cp(r("pu", 0, 24), r("th", 8, 32))
+    ts(r("vk"), ind(r("i16", 0, 64), at16), pm, A.is_equal)
+    mset(r("ff", 0, 16), 0.0)
+    mset(r("ff", 400, 416), 0.0)
+    tt(r("ff", 16, 400), ind(r("cs"), r("pu", 0, 24)), r("vk"), A.mult)
+    for o, a, n in ((0, 16, C), (C, 0, 416)):
+        x, y = r("tr", o, o + n), r("ff", a, a + n)
+        add("dve", lambda x=x, y=y: g.vector.transpose(ap(x), ap(y)), [y], [x], 10 + n / 2)
+        scan(r("trs", o, o + n), r("keep", 0, n), x, A.mult, A.add)
+    ts(r("pi", 4, 5), r("pi", 0, 1), 4, A.arith_shift_right, 1, A.bitwise_and)
+    cp(r("pm", 2, 3), r("pi", 4, 5))
+    ts(r("pm", 4, 5), r("pm", 2, 3), -1.0, A.mult, 1.0, A.add)
+    ts(r("pw", 0, 24, 2), r("trs", 15, C, 32), r("pm", 4, 5), A.mult)
+    ts(r("pw", 1, 24, 2), r("trs", C + 47, 800, 32), r("pm", 4, 5), A.mult)
+    ts(r("pw", 24, 48, 2), r("trs", C + 31, 768, 32), r("pm", 2, 3), A.mult)
+    ts(r("pw", 25, 48, 2), r("trs", 31, C, 32), r("pm", 2, 3), A.mult)
+    tt(r("pw", 48, 72), r("pw", 0, 24), r("pw", 24, 48), A.add)
+    cp(rk16, r("pw", 48, 72))
+    cp(ind(r("ksort"), rk16), r("krep"))
+    tt(r("wa"), r("ksort"), r("dm"), A.mult)
+    ops[-1]["early"] = 15000
+    scan(r("wb"), keep, r("wa"), A.mult, A.add)
+    cp(ex16, r("exi"))
+    tt(r("xrep"), ind(r("t512"), ex16), r("num", 0, E), A.add)
+    act(r("to4"), ind(numc, ex16), scale=4096.0)
+    ts(r("cf", 160, 172), r("exi"), 512.0, A.mult)
+    tt(r("cf", 160, 172), r("cf", 160, 172), j12, A.add)
+    ts(r("cf", 172, 176), r("cf", 0, 4), 512.0, A.mult)
+    ts(r("cf", 176, 192), r("cf", 160, 176), -1.0, A.mult, 0.5, A.add)
+    for m in range(16):
+        act(r("sg", C * m, C * m + E), r("xrep"), F.Sign, bias=r("cf", 176 + m, 177 + m), acc=r("acc", 32 + m, 33 + m))
+    ts(ln16, r("acc", 32, 48), -0.5, A.mult, E / 2, A.add)
+    cp(ind(r("sig"), r("su", 88, 100)), r("num", 0, E))
+    act(r("sig2"), ind(r("sig"), g1216))
+    spread(r("sigw"), r("sig2"))
+    cp(sg16, r("sigw"))
+
+    def expand(i):
+        o = 704 * (i % 2)
+        if i == 3:
+            act(r("g2", o, o + E), ind(r("g1"), g1216))
+        else:
+            act(r("g2", o, o + 704), ind(r("g1"), px16))
+            for k in range(2):
+                spread(r("landn", 8 * i + 4 * k, 8 * i + 4 * k + 4), r("g2", o + 576 + 64 * k, o + 640 + 64 * k))
+        for k in range(3):
+            if (i, k) not in ((0, 0), (3, 1), (3, 2)):
+                spread(r("land", 96 * i + 12 * k, 96 * i + 12 * k + 12), r("g2", o + E * k, o + E * k + E))
+
+    act(r("g1", E, 256), ind(num, st16))
+    expand(0)
+
+    def lists(t):
+        def li(k, n=12):
+            return r("li", 256 * t + 12 * k, 256 * t + 12 * k + n)
+
+        def lu(a, n):
+            return r("lu", 128 * t + a, 128 * t + a + n)
+        keyw, basew = r("lf", 128 * t, 128 * t + 24), r("lf", 128 * t + 24, 128 * t + 48)
+        node = li(10, 24)
+        if t == 0:
+            cp(keyw, r("wb", 15, C, 16))
+            cp(li(12, 24), r("wb", 15, C, 16))
+            ts(node, li(12, 24), 9, A.arith_shift_right)
+            ts(li(18, 24), li(12, 24), 511, A.bitwise_and)
+            cp(s016, li(18, 24))
+            act(r("s0rep"), ind(numc, s016))
+        else:
+            ts(node, r("li", 256 * t - 112, 256 * t - 88), 12, A.arith_shift_right)
+            ts(keyw, node, 512.0, A.mult)
+        ts(basew, node, 4.0, A.mult)
+        o = 24 if t == 0 else 0
+        tt(r("lf", 128 * t + o, 128 * t + 48), r("lf", 128 * t + o, 128 * t + 48), r("cf", o, 48), A.add)
+        cp(li(8, 24), r("ksort" if t == 0 else "vs", 15, C, 16))
+        ts(li(16, 24), li(8, 24), 9 if t == 0 else 12, A.arith_shift_right)
+        ts(r("lf", 128 * t + 48, 128 * t + 72), li(16, 24), 512.0, A.mult)
+        for m in range(NB - 1):
+            o = 576 * t + 24 * m
+            ts(r("ml", o, o + 23 - m), r("lf", 128 * t + m + 1, 128 * t + 24), r("lf", 128 * t + 48 + m, 128 * t + 49 + m),
+               A.subtract, float(C), A.min)
+        sn = r("landn", 8 * t, 8 * t + 4)
+        pcp(r("d0", 448 * t, 448 * t + C), r("cc"))
+        tt(li(20, 4), sn, r("landn", 8 * t + 4, 8 * t + 8), A.subtract)
+        ts(li(20, 4), li(20, 4), 1000.0, A.mult)
+        tt(li(20, 4), li(20, 4), r("cf", 120, 124), A.add)
+        tt(li(20, 4), li(20, 4), sn, A.max)
+        cp(lu(108, 4), li(20, 4))
+        cp(ind(r("d0", 448 * t, 448 * t + 448), lu(108, 4)), r("half"))
+        st, en, base = (r("land", 96 * t + 12, 96 * t + 24), r("land", 96 * t + 24, 96 * t + 36),
+                        r("land", 96 * t + 96, 96 * t + 108))
+        rot, nxt = r("ro", 12 * t, 12 * t + 12), r("ro", 12 * t + 12, 12 * t + 24)
+        tt(li(1), en, st, A.subtract)
+        tt(li(2), li(1), rot, A.add)
+        ts(li(3), li(2), 2, A.arith_shift_right)
+        ts(nxt, li(2), 3, A.bitwise_and)
+        tt(li(4, 24), r("land", 96 * t + 12, 96 * t + 36), c4n, A.add)
+        tt(li(4, 24), li(4, 24), r("ro", 12 * t, 12 * t + 24), A.subtract)
+        cp(lu(24, 24), li(4, 24))
+        cp(ind(r("tab", 576 * t, 576 * t + 576), lu(24, 12)), r("num", C, C + E))
+        cp(lu(48, 12), li(3))
+        act(r("crep"), ind(numc, lu(48, 12)))
+        act(r("csrt"), ind(r("crep"), sg16))
+        scan(r("pf", 1, 1 + E), r("ones", 0, E), r("csrt"), A.mult, A.add)
+        act(r("g1", 0, 256), ind(r("pf", 0, 1 + E), ln16))
+        expand(t + 1)
+        ts(li(6), li(3), -1000.0, A.mult)
+        tt(li(6), li(6), e384, A.add)
+        tt(li(6), li(6), base, A.max)
+        ts(li(7), base, -4.0, A.mult, 1540.0, A.add)
+        tt(li(7), li(7), li(4), A.add)
+        cp(lu(60, 24), li(6, 24))
+        tt(r("vrep"), ind(r("numb"), lu(72, 12)), r("to4") if t < 2 else r("e4096"), A.add)
+        cp(ind(r("vw", 576 * t, 576 * t + 576), lu(60, 12)), r("vrep"))
+        act(r("vk"), r("vw", 576 * t, 576 * t + C), F.Relu, bias=1.0, scale=-1.0)
+        scan(r("vs"), r("vk"), r("vw", 576 * t, 576 * t + C), A.mult, A.add)
+        o = 768 * (t % 2)
+        act(r("vg", o + C, o + 768), ind(r("vs"), r("cu", 24, 48)))
+        act(r("vg", o, o + C), ind(r("vs"), r("cu", 0, 24)))
+        spread(r("land", 96 * t + 168, 96 * t + 192), r("vg", o + C, o + 768))
+        spread(r("land", 96 * t + 144, 96 * t + 168), r("vg", o, o + C))
+        cp(li(12, 48), r("land", 96 * t + 144, 96 * t + 192))
+        ts(li(18, 24), li(14, 24), 4095, A.bitwise_and)
+        tt(li(18, 24), li(18, 24), csrc, A.add)
+        cp(lu(84, 24), li(18, 24))
+        if t == 2:
+            ts(li(16, 24), li(12, 24), 12, A.arith_shift_right)
+            cp(lu(0, 24), li(16, 24))
+            act(r("wb"), ind(numc, lu(0, 24)))
+            dma(lambda: T.ot[:], lambda: T.wb[0:128:16, :], [r("wb")], [])
+        return basew, lu(36, 12), lu(84, 24)
+
+    def plane(name, b, a, n):
+        return r(name, 576 * b + a, 576 * b + a + n)
+
+    for b in range(4):
+        act(plane("xmh", b, C, E), r("mt", b, 768, 4), scale=0.5)
+        pcp(plane("hm", b, C, E), r("mt", b, 768, 4))
+
+    for t in range(ROUNDS):
+        basew, lp16, sp16 = lists(t)
+        tab = r("tab", 576 * t, 576 * t + 576)
+        quant(r("xq"), r("xp"), r("xt"))
+        mm(5, C, r("uq2"), r("up2"), r("xq"), r("xp"))
+        if t > 0:
+            mm(4, C, r("uq2"), r("up2"), r("xq"), r("xp"))
+        act(r("ssb", 0, C), ps(5, C))
+        sw = r("ssb")
+        sv = ps(4, C) if t > 0 else ind(sw, s016)
+        tt(r("sa"), sv, r("a1"), A.add)
+        scan(r("yy"), r("d0", 448 * t, 448 * t + C), r("sa"), A.max, A.min)
+        for b in range(4):
+            act(plane("xmh", b, 0, C), r("xt", b, 1536, 4), scale=0.5)
+            pcp(r("xth", C * b, C * b + C), plane("xmh", b, 0, C))
+        tt(r("ut", 0, 1536, 4), sv, r("yy"), A.is_gt)
+        scan(r("ds"), keep, r("ut", 0, 1536, 4), A.mult, A.add)
+        for k in range(6):
+            for m in range(max(4 * k - 1, 0), 4 * k + 3):
+                s = m + 1 - 4 * k
+                n = C - 16 * (m + 1)
+                o = r("ut", 1536 * k + 64 * (m + 1) + s, 1536 * k + 1536, 4)
+                src = ind(sw, r("ml", 576 * t + 24 * m, 576 * t + 24 * m + 23 - m))
+                y = r("yy", 16 * m + 15, 16 * m + 16)
+                if m in ACT_ROWS:
+                    act(r("sg", C * m, C * m + n), src, F.Sign, bias=y, scale=-1.0)
+                    act(o, r("sg", C * m, C * m + n), F.Relu, scale=-1.0, acc=r("rs", m, m + 1))
+                else:
+                    ts(o, src, y, A.is_gt)
+                    act(r("junk", C * m, C * m + n), o, F.Relu, acc=r("rs", m, m + 1))
+            lo = 64 * min(k, 4)
+            quant(r("utq", C * k + lo, C * k + C), r("utp", C * k + lo, C * k + C), r("ut", 1536 * k + 4 * lo, 1536 * k + 1536))
+            mm(6, C, r("gq"), r("gp"), r("utq", C * k, C * k + C), r("utp", C * k, C * k + C), k == 0, k == 5)
+        tt(r("pw", 0, 24), basew, r("ds", 15, C, 16), A.add)
+        tt(r("pw", 24, 48), r("pw", 0, 24), r("rs"), A.add)
+        tt(r("w1"), ps(6, C), r("dm"), A.mult)
+        scan(r("w2"), keep, r("w1"), A.mult, A.add)
+        tt(r("pw", 48, 72), r("pw", 24, 48), r("w2", 15, C, 16), A.subtract)
+        cp(r("pu", 0, 24), r("pw", 48, 72))
+        cp(ind(tab, r("pu", 0, 24)), numc if t > 0 else r("s0rep"))
+        ts(r("pu", 24, 48), r("pw", 48, 72), -4.0, A.add)
+        if t > 0:
+            tt(r("w3"), ind(tab, r("pu", 24, 48)), r("dm"), A.mult)
+        else:
+            cp(r("wa"), ind(tab, r("pu", 24, 48)))
+            tt(r("w3"), ind(r("wa"), rk16), r("dm"), A.mult)
+        scan(r("w4"), keep, r("w3"), A.mult, A.add)
+        cp(r("pu", 48, 72), r("w4", 15, C, 16))
+        act(r("srep"), ind(tab, sp16))
+        spread(r("land2", 40 * t, 40 * t + 24), r("srep"))
+        act(r("lrep"), ind(tab, lp16))
+        act(r("lrep2"), ind(r("lrep"), g1216))
+        spread(r("land2", 40 * t + 24, 40 * t + 36), r("lrep2"))
+        sk16, la16 = r("du", 40 * t, 40 * t + 24), r("du", 40 * t + 24, 40 * t + 36)
+        cp(sk16, r("land2", 40 * t, 40 * t + 24))
+        cp(la16, r("land2", 40 * t + 24, 40 * t + 36))
+        for b in range(4):
+            tt(r("zt", b, 1536, 4), ind(plane("xmh", b, 0, 576), r("pu", 48, 72)), r("xth", C * b, C * b + C), A.add)
+        quant(r("zq"), r("zp"), r("zt"))
+        for b in range(4):
+            mm(b, C, r("wq", 128 * b, 128 * b + 128), r("wp", 128 * b, 128 * b + 128), r("zq"), r("zp"))
+            act(plane("rr", b, 0, C), ps(b, C), F.Relu, scale=0.03125)
+            if t == 2:
+                act(plane("hm", b, 0, C), r("zt", b, 1536, 4))
+                cp(r("zl", E * b, E * b + E), ind(plane("hm", b, 0, 576), la16))
+                tt(r("mt", b, 768, 4), ind(plane("rr", b, 0, 576), la16), r("zl", E * b, E * b + E), A.add)
+            tt(plane("hm", b, 0, C), plane("rr", b, 0, C), r("zt", b, 1536, 4), A.add)
+        for b in range(4):
+            if t < 2:
+                act(r("mt", b, 768, 4), ind(plane("hm", b, 0, 576), la16))
+            (cp if b == 3 else act)(r("xt", b, 1536, 4), ind(plane("hm", b, 0, 576), sk16))
+        bq, bp, aq, apl = r("bq%d" % t), r("bp%d" % t), r("aq%d" % t), r("ap%d" % t)
+        quant(bq, bp, r("mt", 0, 4 * K))
+        peer = T.cores[rank ^ STEP[t]]
+        rid, pid = topo.addr(peer)[:2]
+        eng = topo.engines(core, peer)
+        half = len(eng) // 2
+        m1, m2 = sum(1 << e for e in eng[:half]), sum(1 << e for e in eng[half:])
+
+        def send(t=t, bq=bq, bp=bp, aq=aq, apl=apl, rid=rid, pid=pid, m1=m1, m2=m2):
+            g.remote_dma(u8(aq), u8(bq), T.sem["arr%d" % t], T.sem["out%d" % t], pid, rid, m1)
+            g.remote_dma(ap(apl), ap(bp), T.sem["arr%d" % t], T.sem["out%d" % t], pid, rid, m2)
+        add("pool", send, [bq, bp], [aq, apl], 600, lat=3600, kind="remote", sem=("arr%d" % t, "out%d" % t, len(eng)))
+        for b in range(4):
+            bank = 7 if b % 2 == 0 or t < 2 else 6
+            mm(bank, K, r("eq", 128 * b, 128 * b + 128), r("ep", 128 * b, 128 * b + 128), aq, apl)
+            if t < 2:
+                act(plane("hm", b, C, K), ps(bank, K))
+                act(plane("xmh", b, C, K), ps(bank, K), scale=0.5)
+                pcp(plane("hm", b, C + K, E - K), r("mt", 4 * K + b, 768, 4))
+                act(plane("xmh", b, C + K, E - K), r("mt", 4 * K + b, 768, 4), scale=0.5)
+            else:
+                (act if b % 2 == 0 else cp)(r("mt", b, 4 * K, 4), ps(bank, K))
+    quant(r("xq"), r("xp"), r("xt"))
+    mm(4, C, r("vq"), r("vp"), r("xq"), r("xp"))
+    act(r("ysb"), ps(4, C))
+    dma(lambda: T.y[:], lambda: T.ysb[:], [r("ysb")], [])
+    quant(r("mq"), r("mp"), r("mt"))
+    dma(lambda: T.oc[:], lambda: u8(r("mq")), [r("mq")], [])
+    for k in range(4):
+        dma(lambda k=k: T.osc[4 * k:4 * k + 4, :], lambda k=k: T.mp[32 * k:32 * k + 4, :], [r("mp")], [],
+            eng="sp" if k < 2 else "act")
+    return ops, Q
+
+
+def order(ops):
+    hop = 110
+    hist = {}
+    for i, o in enumerate(ops):
+        dep = set()
+        for x, w in [(x, False) for x in o["rd"]] + [(x, True) for x in o["wr"]]:
+            for y, j, wj in hist.get(x[0], []):
+                both_read = not (w or wj)
+                if j != i and _overlap(x, y) and not (both_read and (x[0] != "ps" or ops[j]["eng"] == o["eng"])):
+                    dep.add(j)
+        for x, w in [(x, False) for x in o["rd"]] + [(x, True) for x in o["wr"]]:
+            hist.setdefault(x[0], []).append((x, i, w))
+        o["dep"] = dep
+    far = [0.0] * len(ops)
+    for i in range(len(ops) - 1, -1, -1):
+        far[i] += ops[i]["dur"] + ops[i]["lat"] + ops[i]["early"]
+        for j in ops[i]["dep"]:
+            far[j] = max(far[j], far[i] + hop)
+    n = len(ops)
+    deps = [sorted(o["dep"]) for o in ops]
+    runs, key = [], {}
+    for i, o in enumerate(ops):
+        name = ((o["wr"] or o["rd"])[0][0], o["eng"])
+        if name not in key or i - key[name][1] > GAP:
+            key[name] = [len(set(runs)), i]
+        key[name][1] = i
+        runs.append(key[name][0])
+
+    def place(shift):
+        p = [far[i] + shift[runs[i]] for i in range(n)]
+        for i in range(n - 1, -1, -1):
+            for j in deps[i]:
+                if p[j] <= p[i]:
+                    p[j] = p[i] + 1
+        busy, st, en = {}, [0.0] * n, [0.0] * n
+        for i in sorted(range(n), key=lambda i: -p[i]):
+            o = ops[i]
+            s, d = 0.0, o["dur"]
+            for j in deps[i]:
+                if en[j] + hop > s:
+                    s = en[j] + hop
+            line = busy.setdefault(o["eng"], [])
+            k = len(line)
+            while k > 0 and line[k - 1][1] > s:
+                k -= 1
+            while k < len(line) and s + d > line[k][0]:
+                s = max(s, line[k][1])
+                k += 1
+            line.insert(k, (s, s + d))
+            st[i], en[i] = s, s + d + o["lat"]
+        return max(en), st, en
+
+    if "best" not in PLAN:
+        rng = np.random.default_rng(SEED)
+        shift = [0.0] * (max(runs) + 1)
+        best = place(shift)
+        for rep in range(PASSES):
+            other = list(shift)
+            for k in rng.integers(0, len(shift), 3):
+                other[int(k)] += float(rng.normal()) * SIG[rep % 3]
+            got = place(other)
+            if got[0] <= best[0]:
+                best, shift = got, other
+        PLAN["best"] = best
+    for i, o in enumerate(ops):
+        o["start"], o["end"] = PLAN["best"][1][i], PLAN["best"][2][i]
+    return sorted(range(len(ops)), key=lambda i: (ops[i]["start"], i))
+
+
+def emit(g, T, ops, Q):
+    seq = order(ops)
+    count = {"dve": 0, "act": 0, "pe": 0, "pool": 0}
+    known = {e: {} for e in Q}
+    total = {}
+    nd = 0
+    for i in seq:
+        o = ops[i]
+        e = o["eng"]
+        need = {}
+        for j in o["dep"]:
+            if o["chain"] and ops[j]["eng"] == e:
+                continue
+            s, v = ops[j]["sig"]
+            if need.get(s, (0, 0))[0] < v:
+                need[s] = (v, j)
+        for s, (v, j) in sorted(need.items(), key=lambda kv: -ops[kv[1][1]]["end"]):
+            if known[e].get(s, 0) < v:
+                Q[e].wait_ge(T.sem[s], v)
+                for s2, v2 in ops[j]["clock"].items():
+                    known[e][s2] = max(known[e].get(s2, 0), v2)
+        clock = dict(known[e])
+        if o["kind"] == "c":
+            count[e] += 1
+            o["sig"] = (e, count[e])
+            o["fn"]().then_inc(T.sem[e], 1)
+        elif o["kind"] == "dma":
+            o["sig"] = ("d%d" % nd, 16)
+            nd += 1
+            o["fn"]().then_inc(T.sem[o["sig"][0]], 16)
+        else:
+            o["fn"]()
+            o["sig"] = (o["sem"][0], o["sem"][2])
+            total[o["sem"][1]] = o["sem"][2]
+            clock = {}
+        clock[o["sig"][0]] = o["sig"][1]
+        o["clock"] = clock
+        total[o["sig"][0]] = o["sig"][1]
+    for s, v in total.items():
+        g.wait_ge(T.sem[s], v)
+
+
+def rank_program(g, core, T, topo):
+    rank = T.rank_of(core)
+    if rank is None:
+        return
+    ops, Q = build(g, core, T, topo, rank)
+    emit(g, T, ops, Q)

@@ -8,10 +8,18 @@ E = 4 * V
 STEP = [1, 2, 1]
 NB = C // 16
 BIG = 2.0 ** 80
+WHOLE = 1.5 * 2 ** 23
 F32, BF, I32, U16, F16 = "float32", "bfloat16", "int32", "uint16", "float16"
 CODE, PLANE = "float8_e4m3fn_x4", "uint8"
-ACT_ROWS = (0, 2, 4, 6, 8, 10, 12, 14, 16, 18, 20)
-SIG, GAP, PASSES, SEED, PLAN = (500, 2500, 9000), 40, 4500, 2, {}
+LO = (0, 64, 128, 192, 256, 256)
+UO = (0, 1728, 3008, 4032, 4800, 5312)
+SO = (0, 320, 576, 768, 896, 960)
+TILES = (0, 3, 4, 5, 1, 2)
+ACT_ROWS = 8
+ZG_DVE = (1,)
+ZA = 256
+MT, ZT = (1536, 2304, 4608), 3072
+SIG, SLACK, PASSES, SEED, PLAN = (100, 300, 1000), 1.01, 1500, 2, {}
 
 
 def _sb(n, d):
@@ -22,27 +30,29 @@ SCRATCH = {
     "ati": _sb(24, I32), "exi": _sb(12, I32), "ub": _sb(512, BF), "vb": _sb(512, BF),
     "wq": _sb(512, CODE), "wp": _sb(512, PLANE), "uq": _sb(128, CODE), "up": _sb(128, PLANE),
     "uq2": _sb(128, CODE), "up2": _sb(128, PLANE), "vq": _sb(128, CODE), "vp": _sb(128, PLANE),
-    "num": _sb(640, F32), "numb": _sb(2176, F32), "t512": _sb(64, F32), "e4096": _sb(E, F32),
-    "pi": _sb(8, I32), "pm": _sb(8, F32), "i16": _sb(416, BF), "dm": _sb(C, BF), "a1": _sb(C, BF), "keep": _sb(416, BF),
-    "cc": _sb(C, BF), "cc2": _sb(C, BF), "half": _sb(64, BF), "ones": _sb(512, BF), "c1": _sb(512, BF), "gb": _sb(512, BF),
+    "num": _sb(640, F32), "numb": _sb(2176, F32), "t512": _sb(64, F32), "e8192": _sb(E, F32),
+    "pi": _sb(8, I32), "pm": _sb(8, F32), "i16": _sb(2 * C, BF), "dm": _sb(C, BF), "dm4": _sb(C, BF),
+    "a1": _sb(2 * C, BF), "keep": _sb(416, BF), "keep4": _sb(C, BF),
+    "cc": _sb(C, BF), "half": _sb(64, BF), "ones": _sb(512, BF), "c1": _sb(512, BF), "gb": _sb(512, BF),
     "eb": _sb(2048, BF), "zb": _sb(1024, BF), "gq": _sb(128, CODE), "gp": _sb(128, PLANE), "eq": _sb(512, CODE),
     "ep": _sb(512, PLANE), "zq0": _sb(256, CODE), "zp0": _sb(256, PLANE),
     "ci": _sb(256, I32), "cf": _sb(256, F32), "cu": _sb(128, U16), "uo": _sb(8, U16),
-    "krep": _sb(C, F32), "ksort": _sb(C, F32), "lt": _sb(C * 3, BF), "cs": _sb(C * 3, F32), "nrp": _sb(C, BF),
+    "ksort": _sb(C, F32), "lt": _sb(C * 3, BF), "cs": _sb(C * 3, F32), "nrp": _sb(C, BF),
     "ff": _sb(416, F16), "tr": _sb(800, F16), "trs": _sb(800, F16),
-    "junk": _sb(23 * C, BF), "th": _sb(64, F32), "acc": _sb(64, F32), "su": _sb(128, U16),
-    "xrep": _sb(E, F32), "to4": _sb(E, F32), "sig": _sb(E, F32), "sig2": _sb(E, F32), "sigw": _sb(12, F32),
-    "s0rep": _sb(C, F32), "wa": _sb(C, F32), "wb": _sb(C, F32),
-    "li": _sb(3 * 256, I32), "lf": _sb(3 * 128, F32), "lu": _sb(3 * 128, U16), "land": _sb(4 * 96, F32), "ro": _sb(48, I32),
-    "landn": _sb(3 * 8, F32), "crep": _sb(E, F32), "csrt": _sb(E, F32), "pf": _sb(208, F32), "g1": _sb(272, F32),
+    "th": _sb(64, F32), "acc": _sb(64, F32), "su": _sb(128, U16),
+    "xrep": _sb(E, F32), "sig": _sb(E, F32), "sig2": _sb(E, F32), "sigw": _sb(12, F32), "wa": _sb(C, F32),
+    "li": _sb(128, I32), "lf": _sb(3 * 320, F32), "lu": _sb(3 * 128, U16), "land": _sb(4 * 48, F32), "ro": _sb(48, I32),
+    "crep": _sb(E, F32), "csrt": _sb(E, F32), "pf": _sb(208, F32), "g1": _sb(272, F32),
     "g2": _sb(2 * 704, F32), "vrep": _sb(E, F32), "vw": _sb(3 * 576, F32), "vk": _sb(C, BF), "vs": _sb(C, F32),
-    "vg": _sb(2 * 768, F32), "d0": _sb(3 * 448, BF), "ml": _sb(3 * 24 * 24, U16), "tab": _sb(3 * 576, F32),
-    "ssb": _sb(400, F32), "sa": _sb(C, F32), "yy": _sb(C, F32), "ut": _sb(6 * 1536, BF), "utq": _sb(6 * C, CODE),
-    "utp": _sb(6 * C, PLANE), "sg": _sb(23 * C, BF), "rs": _sb(24, F32), "ds": _sb(C, F16), "pw": _sb(96, F32),
-    "pu": _sb(96, U16), "w1": _sb(C, F16), "w2": _sb(C, F16), "w3": _sb(C, F16), "w4": _sb(C, F16),
-    "srep": _sb(C, F32), "lrep": _sb(E, F32), "lrep2": _sb(E, F32), "land2": _sb(3 * 40, F32), "du": _sb(3 * 40, U16),
-    "xt": _sb(1536, BF), "xq": _sb(C, CODE), "xp": _sb(C, PLANE), "zt": _sb(1536, BF), "zq": _sb(C, CODE), "zp": _sb(C, PLANE),
-    "xmh": _sb(4 * 576, BF), "hm": _sb(4 * 576, BF), "rr": _sb(4 * 576, F32), "zl": _sb(768, BF), "xth": _sb(1536, BF),
+    "vg": _sb(768, F32), "lv": _sb(96, F32), "l4": _sb(48, F32), "d0": _sb(3 * 448, BF), "ml": _sb(3 * 132, U16),
+    "bl": _sb(132, F32), "mk": _sb(120, F32), "tab": _sb(3 * 576, F32), "nd": _sb(C, BF), "sp": _sb(72, U16),
+    "ssb": _sb(800, F32), "sa": _sb(C, F32), "yy": _sb(400, F32), "st": _sb(960, F32),
+    "ut": _sb(5824, BF), "utq": _sb(6 * C, CODE), "utp": _sb(6 * C, PLANE), "sg": _sb(16 * C, BF), "rs": _sb(24, F32),
+    "ds": _sb(2 * C, F16), "jr": _sb(3200, F16), "qq": _sb(32, F32), "pw": _sb(96, F32),
+    "pu": _sb(144, U16), "w1": _sb(C, F16), "w2": _sb(C, F16), "w3": _sb(C, F16), "w4": _sb(C, F16),
+    "srep": _sb(C, F32), "lrep": _sb(2 * E, F32), "land2": _sb(180, F32), "du": _sb(180, U16),
+    "xm": _sb(5376, BF), "xmh": _sb(3840, BF), "xq": _sb(C, CODE), "xp": _sb(C, PLANE), "zq": _sb(C, CODE), "zp": _sb(C, PLANE),
+    "rr": _sb(4 * 576, F32), "zl": _sb(768, BF), "zg": _sb(1536, BF),
     "mt": _sb(768, BF), "mq": _sb(E, CODE), "mp": _sb(E, PLANE), "ysb": _sb(C, F32),
     "bq0": _sb(K, CODE), "bp0": _sb(K, PLANE), "bq1": _sb(K, CODE), "bp1": _sb(K, PLANE), "bq2": _sb(K, CODE), "bp2": _sb(K, PLANE),
     "aq0": _sb(K, CODE), "ap0": _sb(K, PLANE), "aq1": _sb(K, CODE), "ap1": _sb(K, PLANE), "aq2": _sb(K, CODE), "ap2": _sb(K, PLANE),
@@ -135,7 +145,7 @@ def build(g, core, T, topo, rank):
         add("dve", lambda: g.vector.memset(ap(out), c), [], [out], vcost(out, [out], .5 if two(out) else 1))
 
     def quant(q, p, in_):
-        add("dve", lambda: g.vector.quantize_mx(ap(q), ap(p), ap(in_)), [in_], [q, p], 25 + .265 * cnt(in_))
+        add("dve", lambda: g.vector.quantize_mx(ap(q), ap(p), ap(in_)), [in_], [q, p], 15 + .265 * cnt(in_))
 
     def act(out, in_, func=F.Copy, bias=None, scale=None, acc=None):
         def fn():
@@ -143,17 +153,17 @@ def build(g, core, T, topo, rank):
             if bias is not None:
                 kw["bias"] = val(bias)
             if scale is not None:
-                kw["scale"] = scale
+                kw["scale"] = val(scale)
             if acc is not None:
                 kw["accum_out"] = ap(acc)
             return g.scalar.activation(ap(out), ap(in_), func, **kw)
         d = 78 + 1.56 * cnt(out) if in_[0] == "ind" else 60 + cnt(out)
-        add("act", fn, [in_, bias], [out, acc], d + (24 if acc else 0))
+        add("act", fn, [in_, bias, scale], [out, acc], d + (24 if acc else 0))
 
     def mm(bank, n, lq, lp, rq, rp, start=True, stop=True):
         o = r("ps", 512 * bank, 512 * bank + n)
         add("pe", lambda: g.tensor.matmul_mx(ap(o), ap(lq), ap(lp), ap(rq), ap(rp), start, stop), [lq, lp, rq, rp], [o],
-            .7 * (n + 16), lat=80, chain=not start)
+            .7 * (n + 16), lat=60, chain=not start)
 
     def ps(bank, n):
         return r("ps", 512 * bank, 512 * bank + n)
@@ -180,13 +190,17 @@ def build(g, core, T, topo, rank):
     def spread(dst, src):
         dma(lambda: ap(dst), lambda: T[src[0]][0:128:16, src[1]:src[2]], [src], [dst])
 
+    def xm(a, n, s=1):
+        return r("xm", a, a + n, s)
+
     num, numc = r("num"), r("num", 0, C)
+    xt, zt = xm(0, 4 * C), xm(ZT, 4 * C)
     dma(lambda: T.ati[:], lambda: T.at[:], [], [r("ati")])
-    dma(lambda: T.xt[:], lambda: T.x[:], [], [r("xt")], eng="act", lat=3000)
+    dma(lambda: ap(xt), lambda: T.x[:], [], [xt], eng="act", lat=4100)
     dma(lambda: T.exi[:], lambda: T.ex[:], [], [r("exi")])
-    dma(lambda: T.ub[:], lambda: T.u[:], [], [r("ub")])
-    dma(lambda: T.mt[:], lambda: T.e[:], [], [r("mt")])
-    dma(lambda: u8(r("wq")), lambda: T.wc[:], [], [r("wq")])
+    dma(lambda: T.ub[:], lambda: T.u[:], [], [r("ub")], lat=2800)
+    dma(lambda: ap(xm(MT[0], 768)), lambda: T.e[:], [], [xm(MT[0], 768)], lat=3200)
+    dma(lambda: u8(r("wq")), lambda: T.wc[:], [], [r("wq")], lat=3500)
     dma(lambda: T.wp[:], lambda: T.ws[:], [], [r("wp")])
     dma(lambda: T.vb[:], lambda: T.v[:], [], [r("vb")])
     iota(r("pi", 0, 1), [[0, 1]], 0, 1, early=4e4)
@@ -194,22 +208,23 @@ def build(g, core, T, topo, rank):
     iota(r("t512"), [[512, 64]], early=2e4)
     iota(numc, [[1, C]], early=1e4)
     iota(r("num", C, 640), [[1, 640 - C]], C)
-    iota(r("i16"), [[0, NB + 2], [1, 16]], early=5e3)
+    iota(r("i16", 0, C), [[0, NB], [1, 16]], early=5e3)
     iota(r("numb"), [[1, 2176]])
-    iota(r("e4096"), [[4096, E]])
+    iota(r("e8192"), [[8192, E]])
+    iota(r("ones"), [[0, 512]], 1)
     ts(r("pi", 2, 3), r("pi", 0, 1), 15, A.bitwise_and)
     cp(r("pm", 0, 1), r("pi", 2, 3))
     pm, keep = r("pm", 0, 1), r("keep", 0, C)
     ts(r("dm"), r("i16", 0, C), pm, A.is_equal)
-    ts(r("a1"), r("i16", 0, C), pm, A.not_equal, BIG, A.mult)
-    ts(r("keep"), r("i16"), 0.0, A.is_gt)
-    act(r("cc2"), r("a1"), bias=BIG / 2, scale=-1.0)
-    sel(r("cc"), r("cc2"), [[0, NB], [1, 16]], A.is_gt, 0, 0, BIG / 2)
-    mset(r("half"), BIG / 2)
+    act(r("a1", 0, C), r("dm"), scale=-BIG, bias=BIG)
+    sel(r("keep"), r("ones", 0, 416), [[0, NB + 2], [1, 16]], A.is_gt, 0, 0)
+    act(r("a1", C, 2 * C), r("dm"), bias=-BIG / 2, scale=BIG)
+    sel(r("cc"), r("a1", C, 2 * C), [[0, NB], [1, 16]], A.is_gt, 0, 0, BIG / 2)
+    act(r("half"), r("num", 0, 64), scale=BIG / 128, bias=BIG / 2)
     cp(r("uo"), r("ci", 0, 8))
     jw = r("cf", 0, 24)
     ts(jw, r("ci", 0, 24), pm, A.add)
-    j12, ga = r("cf", 0, 12), r("cf", 132, 156)
+    j12, ga = r("cf", 0, 12), r("cf", 136, 160)
 
     def turn(out, x, w, t1, t2, t3):
         ts(t2, x, float(65536 // w + 1), A.mult)
@@ -220,9 +235,9 @@ def build(g, core, T, topo, rank):
 
     turn(ga, jw, 24, r("ci", 24, 48), r("ci", 48, 72), r("cf", 200, 224))
     turn(r("cu", 24, 48), ga, 24, r("ci", 72, 96), r("ci", 96, 120), r("cf", 224, 248))
-    turn(r("cu", 48, 60), j12, 12, r("ci", 120, 132), r("ci", 132, 144), r("cf", 48, 60))
+    turn(r("cu", 48, 60), j12, 12, r("ci", 120, 132), r("ci", 132, 144), r("cf", 72, 84))
     cp(r("cu", 0, 24), ga)
-    g1216, px16 = r("cu", 48, 60), r("cu", 48, 92)
+    g1216 = r("cu", 48, 60)
     ts(r("ci", 144, 156), r("ci", 120, 132), 2, A.arith_shift_right)
     ts(r("ci", 156, 168), r("ci", 120, 132), -48.0, A.mult, float(E), A.add)
     tt(r("ci", 156, 168), r("ci", 156, 168), r("ci", 144, 156), A.add)
@@ -233,29 +248,29 @@ def build(g, core, T, topo, rank):
     turn(r("cf", 192, 196), r("cf", 0, 4), 4, r("ci", 204, 208), r("ci", 208, 212), r("cf", 196, 200))
     ts(r("cu", 84, 88), r("cf", 192, 196), float(E), A.add)
     ts(r("cu", 88, 92), r("cf", 192, 196), float(E + 1), A.add)
-    csrc, e384, jw4, c4n = r("cf", 96, 120), r("cf", 120, 132), r("cf", 24, 48), r("ci", 212, 236)
-    ts(csrc, ga, 4.0, A.mult, -1536.0, A.add)
-    ts(e384, j12, float(C), A.add)
-    ts(jw4, jw, 4.0, A.add)
+    csrc, c4n = r("cf", 96, 120), r("ci", 212, 224)
+    act(csrc, ga, scale=4.0, bias=-1536.0)
+    act(r("cf", 120, 132), j12, bias=float(C))
+    act(r("cf", 132, 136), r("cf", 0, 4), bias=float(C))
+    act(r("cf", 24, 48), jw, scale=-1.0)
+    act(r("cf", 48, 72), jw, bias=4.0)
     cp(r("ci", 168, 180), j12)
     ts(r("ci", 192, 204), r("ci", 168, 180), 3, A.bitwise_and)
     ts(r("ro", 0, 12), r("ci", 192, 204), -1.0, A.mult, 3.0, A.add)
-    for k in range(2):
-        tt(r("ci", 212 + 12 * k, 224 + 12 * k), r("ci", 168, 180), r("ro", 0, 12), A.add)
-    iota(r("ones"), [[0, 512]], 1)
+    tt(c4n, r("ci", 168, 180), r("ro", 0, 12), A.add)
     sel(r("c1"), r("ones"), [[-16, 8], [0, 64]], A.is_ge, 0, 1)
     sel(r("gb"), r("c1"), [[16, 8], [0, 64]], A.is_ge, 15, -1)
     quant(r("gq"), r("gp"), r("gb"))
     for k in range(6):
-        lo = 64 * min(k, 4)
-        iota(r("ut", 1536 * k + 4 * lo, 1536 * k + 4 * (64 * k + 48)), [[0, 4 * (64 * k + 48 - lo)]])
+        n = 4 * (max(64 * k, 0) + 48 - LO[k])
+        iota(r("ut", UO[k], UO[k] + n), [[0, n]])
+    iota(r("ut", 1536, 1536 + 192), [[0, 192]])
     iota(r("zb"), [[0, 1024]])
     quant(r("zq0"), r("zp0"), r("zb"))
     for k in range(1, 6):
-        w = 64 * min(k, 4)
-        dq, dp = r("utq", C * k, C * k + w), r("utp", C * k, C * k + w)
-        dma(lambda dq=dq: u8(dq), lambda w=w: u8(r("zq0", 0, w)), [r("zq0")], [dq])
-        dma(lambda dp=dp: ap(dp), lambda w=w: ap(r("zp0", 0, w)), [r("zp0")], [dp])
+        dq, dp = r("utq", C * k, C * k + LO[k]), r("utp", C * k, C * k + LO[k])
+        dma(lambda dq=dq, w=LO[k]: u8(dq), lambda w=LO[k]: u8(r("zq0", 0, w)), [r("zq0")], [dq])
+        dma(lambda dp=dp: ap(dp), lambda w=LO[k]: ap(r("zp0", 0, w)), [r("zp0")], [dp])
     for t in range(ROUNDS):
         iota(r("tab", 576 * t, 576 * t + 576), [[0, 576]])
         iota(r("vw", 576 * t, 576 * t + 576), [[0, 576]])
@@ -264,9 +279,19 @@ def build(g, core, T, topo, rank):
         sel(r("eb", 512 * b, 512 * b + 512), r("ones"), [[-1, 512]], A.is_equal, b, 4)
         iota(r("rr", 576 * b + C, 576 * b + 576), [[0, E]])
     quant(r("eq"), r("ep"), r("eb"))
-    mset(r("ssb", C, 400), -BIG)
-    mset(r("rs", 23, 24), 0.0)
-    mset(r("pf", 0, 1), 0.0)
+    act(r("ssb", 0, 8), r("ones", 0, 8), scale=-BIG)
+    act(r("yy", C, 400), r("ones", 0, 16), scale=BIG)
+    iota(r("qq", 0, 2), [[0, 2]])
+    iota(r("bl", 0, 72), [[0, 72]])
+    iota(r("pf", 0, 2), [[0, 2]])
+    iota(r("acc", 3, 4), [[0, 1]], -C)
+    ts(r("pi", 6, 7), r("pi", 0, 1), 3, A.bitwise_and)
+    cp(r("pm", 6, 7), r("pi", 6, 7))
+    ts(r("pi", 5, 6), r("pi", 2, 3), 2, A.arith_shift_right)
+    cp(r("pm", 5, 6), r("pi", 5, 6))
+    iota(r("i16", C, 2 * C), [[0, C // 4], [1, 4]])
+    ts(r("dm4"), r("i16", C, 2 * C), r("pm", 5, 6), A.is_equal)
+    sel(r("keep4"), r("ones", 0, C), [[0, C // 4], [1, 4]], A.is_gt, 0, 0)
     iota(r("g1"), [[0, 272]], C)
     quant(r("uq"), r("up"), r("ub"))
     add("dve", lambda: g.vector.tensor_copy(T.uq2[:].bitcast(dt.uint32), T.uq[:].bitcast(dt.uint32).indirect(T.uo[:, 0:8])),
@@ -277,21 +302,20 @@ def build(g, core, T, topo, rank):
     at16, rk16, st16, s016, ex16, ln16, sg16 = (r("su", 0, 24), r("su", 24, 48), r("su", 48, 52), r("su", 52, 76),
                                                 r("su", 76, 88), r("su", 88, 104), r("su", 104, 116))
     cp(at16, r("ati"))
-    tt(r("krep"), ind(r("t512"), at16), numc, A.add)
     act(r("nrp"), ind(numc, at16))
-    ts(r("th", 0, 4), r("cf", 0, 4), -1.0, A.mult, 0.5, A.add)
-    for m in range(4):
-        act(r("junk", C * m, C * m + C), r("nrp"), F.Sign, bias=r("th", m, m + 1), acc=r("acc", m, m + 1))
+    act(r("th", 0, 3), r("cf", 0, 3), scale=-1.0, bias=0.5)
+    for m in range(3):
+        act(r("g2", C * m, C * m + C), r("nrp"), F.Sign, bias=r("th", m, m + 1), acc=r("acc", m, m + 1))
     ts(st16, r("acc", 0, 4), -0.5, A.mult, C / 2, A.add)
-    ts(r("th", 4, 8), r("acc", 0, 4), -0.5, A.mult, C / 2 - 1, A.add)
     for q in range(3):
+        act(r("th", 4 + q, 5 + q), r("acc", q, q + 1), scale=-0.5, bias=C / 2 - 1)
         ts(r("lt", C * q, C * q + C), r("nrp"), r("cf", q, q + 1), A.is_equal)
         scan(r("cs", C * q, C * q + C), r("ones", 0, C), r("lt", C * q, C * q + C), A.mult, A.add, r("th", 4 + q, 5 + q))
-    ts(r("li", 0, 24), r("ati"), 4, A.arith_shift_right)
-    ts(r("th", 8, 32), r("li", 0, 24), float(C), A.mult)
+    ts(r("li", 96, 120), r("ati"), 4, A.arith_shift_right)
+    ts(r("th", 8, 32), r("li", 96, 120), float(C), A.mult)
     tt(r("th", 8, 32), r("th", 8, 32), jw, A.add)
     cp(r("pu", 0, 24), r("th", 8, 32))
-    ts(r("vk"), ind(r("i16", 0, 64), at16), pm, A.is_equal)
+    act(r("vk"), ind(r("dm", 0, 64), at16))
     mset(r("ff", 0, 16), 0.0)
     mset(r("ff", 400, 416), 0.0)
     tt(r("ff", 16, 400), ind(r("cs"), r("pu", 0, 24)), r("vk"), A.mult)
@@ -308,17 +332,16 @@ def build(g, core, T, topo, rank):
     ts(r("pw", 25, 48, 2), r("trs", 31, C, 32), r("pm", 2, 3), A.mult)
     tt(r("pw", 48, 72), r("pw", 0, 24), r("pw", 24, 48), A.add)
     cp(rk16, r("pw", 48, 72))
-    cp(ind(r("ksort"), rk16), r("krep"))
-    tt(r("wa"), r("ksort"), r("dm"), A.mult)
-    ops[-1]["early"] = 15000
-    scan(r("wb"), keep, r("wa"), A.mult, A.add)
+    cp(ind(r("ksort"), rk16), numc)
+    tt(r("w1"), r("ksort"), r("dm"), A.mult)
+    scan(r("w2"), keep, r("w1"), A.mult, A.add)
+    cp(s016, r("w2", 15, C, 16))
     cp(ex16, r("exi"))
     tt(r("xrep"), ind(r("t512"), ex16), r("num", 0, E), A.add)
-    act(r("to4"), ind(numc, ex16), scale=4096.0)
     ts(r("cf", 160, 172), r("exi"), 512.0, A.mult)
     tt(r("cf", 160, 172), r("cf", 160, 172), j12, A.add)
-    ts(r("cf", 172, 176), r("cf", 0, 4), 512.0, A.mult)
-    ts(r("cf", 176, 192), r("cf", 160, 176), -1.0, A.mult, 0.5, A.add)
+    act(r("cf", 172, 176), r("cf", 0, 4), scale=512.0)
+    act(r("cf", 176, 192), r("cf", 160, 176), scale=-1.0, bias=0.5)
     for m in range(16):
         act(r("sg", C * m, C * m + E), r("xrep"), F.Sign, bias=r("cf", 176 + m, 177 + m), acc=r("acc", 32 + m, 33 + m))
     ts(ln16, r("acc", 32, 48), -0.5, A.mult, E / 2, A.add)
@@ -327,180 +350,224 @@ def build(g, core, T, topo, rank):
     spread(r("sigw"), r("sig2"))
     cp(sg16, r("sigw"))
 
+    def land(i, a, n):
+        return r("land", 48 * i + a, 48 * i + a + n)
+
     def expand(i):
         o = 704 * (i % 2)
-        if i == 3:
-            act(r("g2", o, o + E), ind(r("g1"), g1216))
+        a, b = {0: (12, 36), 3: (0, 12)}.get(i, (0, 44))
+        act(r("g2", o + 16 * a, o + 16 * b), ind(r("g1"), r("cu", 48 + a, 48 + b)))
+        for x, y, n in ((0, 0, 12), (12, 20, 12), (24, 32, 12), (36, 12, 4), (40, 16, 4)):
+            if a <= x < b:
+                spread(land(i, y, n), r("g2", o + 16 * x, o + 16 * (x + n)))
+
+    def lf(t, a, n, s=1):
+        return r("lf", 320 * t + a, 320 * t + a + n, s)
+
+    def lu(t, a, n):
+        return r("lu", 128 * t + a, 128 * t + a + n)
+
+    def ml(t, a, n):
+        return r("ml", 132 * t + a, 132 * t + a + n)
+
+    def starts(t, off):
+        d0 = r("d0", 448 * t, 448 * t + C)
+        pcp(d0, r("cc"))
+        cp(ind(r("d0", 448 * t, 448 * t + 448), off), r("half", 0, 48))
+        scan(r("nd"), d0, d0, A.max, A.max)
+        n512, last = lf(t, 0, 24), lf(t, 96, 24)
+        act(r("vg", 0, C), ind(r("nd"), r("cu", 0, 24)), scale=65536 / BIG, bias=-32768.0)
+        spread(n512, r("vg", 0, C))
+        act(last, r("nd", 15, C, 16), scale=65536 / BIG, bias=-32768.0)
+        act(lf(t, 24, 24), n512, scale=1.0 / 128)
+        tt(lf(t, 48, 48), lf(t, 0, 48), r("cf", 24, 72), A.add)
+        tt(lf(t, 120, 24), last, r("num", 15, C, 16), A.subtract)
+        for d in range(1, 4):
+            tt(r("bl", 24 * d - 24, 24 * d - d), lf(t, d, 24 - d), lf(t, 120, 24 - d), A.subtract)
+        act(lf(t, 144, 24), last, bias=8.0)
+        act(lf(t, 168, 24), last, scale=-1.0, bias=1.0)
+        for k in range(5):
+            act(r("bl", 72 + SO[k] // 16, 72 + SO[k + 1] // 16), lf(t, 52 + 4 * k, 20 - 4 * k), F.Relu, scale=-1.0,
+                bias=lf(t, 147 + 4 * k, 1))
+            act(r("mk", 40 * t + 4 * k, 40 * t + 4 * k + 4), lf(t, 96 + 4 * k, 4), F.Relu, bias=lf(t, 171 + 4 * k, 1))
+        act(r("mk", 40 * t + 20, 40 * t + 40), r("mk", 40 * t, 40 * t + 20), scale=-1.0)
+        ts(ml(t, 0, 132), r("bl"), 399.0, A.min)
+
+    def exits(t):
+        st, en, rot, nxt = land(t, 20, 12), land(t, 32, 12), r("ro", 12 * t, 12 * t + 12), r("ro", 12 * t + 12, 12 * t + 24)
+        w, u, c4, mp = lf(t, 192, 12), r("li", 12 * t, 12 * t + 12), lf(t, 204, 12), lf(t, 220, 12)
+        tt(w, st, rot, A.subtract)
+        tt(u, en, w, A.subtract)
+        ts(nxt, u, 3, A.bitwise_and)
+        tt(c4, u, nxt, A.subtract)
+        ts(lu(t, 24, 12), c4, 0.25, A.mult)
+        tt(mp, w, c4n, A.add)
+        if t == 2:
+            tt(lf(t, 232, 12), mp, c4, A.add)
+        cp(lu(t, 0, 24 if t == 2 else 12), lf(t, 220, 24 if t == 2 else 12))
+        cp(ind(r("tab", 576 * t, 576 * t + 576), lu(t, 0, 12)), r("num", C, C + E))
+        act(r("crep"), ind(numc, lu(t, 24, 12)))
+        act(r("csrt"), ind(r("crep"), sg16))
+        scan(r("pf", 1, 1 + E), r("ones", 0, E), r("csrt"), A.mult, A.add)
+        act(r("g1", 0, 256 if t < 2 else E), ind(r("pf", 0, 1 + E), ln16 if t < 2 else r("su", 88, 100)))
+        expand(t + 1)
+        n = 16 if t < 2 else 12
+        if t < 2:
+            tt(lf(t, 216, 4), land(t + 1, 16, 4), land(t + 1, 12, 4), A.subtract)
+        spare, b4 = lf(t, 244, n), lf(t, 260, 12)
+        act(spare, lf(t, 204, n), scale=-1000.0)
+        tt(spare, spare, r("cf", 120, 120 + n), A.add)
+        tt(lf(t, 284, n), spare, land(t + 1, 0, n), A.max)
+        act(b4, land(t + 1, 0, 12), scale=4.0, bias=-1540.0)
+        tt(lf(t, 272, 12), mp, b4, A.subtract)
+        cp(lu(t, 36, 12 + n), lf(t, 272, 12 + n))
+        if t < 2:
+            starts(t + 1, lu(t, 60, 3))
+            tt(b4, b4, c4, A.add)
+            act(lf(t, 300, 12), lf(t, 244, 12), scale=4.0, bias=float(4 + 4 * E * t - 1540))
+            tt(b4, b4, lf(t, 300, 12), A.max)
+            for b in range(4):
+                act(r("l4", 12 * b, 12 * b + 12), b4, bias=float(1536 + b))
+            cp(lu(t, 64, 48), r("l4", 0, 48))
+            act(r("vrep"), ind(r("numb"), lu(t, 36, 12)))
         else:
-            act(r("g2", o, o + 704), ind(r("g1"), px16))
-            for k in range(2):
-                spread(r("landn", 8 * i + 4 * k, 8 * i + 4 * k + 4), r("g2", o + 576 + 64 * k, o + 640 + 64 * k))
-        for k in range(3):
-            if (i, k) not in ((0, 0), (3, 1), (3, 2)):
-                spread(r("land", 96 * i + 12 * k, 96 * i + 12 * k + 12), r("g2", o + E * k, o + E * k + E))
+            tt(r("vrep"), ind(r("numb"), lu(t, 36, 12)), r("e8192"), A.add)
+        cp(ind(r("vw", 576 * t, 576 * t + 576), lu(t, 48, 12)), r("vrep"))
+        act(r("vk"), r("vw", 576 * t, 576 * t + C), F.Relu, bias=1.0, scale=-1.0)
+        scan(r("vs"), r("vk"), r("vw", 576 * t, 576 * t + C), A.mult, A.add)
+        act(r("vg", C, 2 * C), ind(r("vs"), r("cu", 24, 48)))
+        src = r("lv", 24 * t, 24 * t + 24)
+        spread(src, r("vg", C, 2 * C))
+        if t == 2:
+            act(r("wa"), r("vs"), scale=1.0 / 8192, bias=WHOLE)
+            act(r("wa"), r("wa"), bias=-WHOLE)
+            dma(lambda: T.ot[:], lambda: T.wa[0:128:16, :], [r("wa")], [])
+            cp(r("li", 40, 64), src)
+            src = r("li", 64, 88)
+            ts(src, r("li", 40, 64), 8191, A.bitwise_and)
+        tt(r("lv", 72, 96), src, csrc, A.add)
+        cp(r("sp", 24 * t, 24 * t + 24), r("lv", 72, 96))
 
     act(r("g1", E, 256), ind(num, st16))
     expand(0)
-
-    def lists(t):
-        def li(k, n=12):
-            return r("li", 256 * t + 12 * k, 256 * t + 12 * k + n)
-
-        def lu(a, n):
-            return r("lu", 128 * t + a, 128 * t + a + n)
-        keyw, basew = r("lf", 128 * t, 128 * t + 24), r("lf", 128 * t + 24, 128 * t + 48)
-        node = li(10, 24)
-        if t == 0:
-            cp(keyw, r("wb", 15, C, 16))
-            cp(li(12, 24), r("wb", 15, C, 16))
-            ts(node, li(12, 24), 9, A.arith_shift_right)
-            ts(li(18, 24), li(12, 24), 511, A.bitwise_and)
-            cp(s016, li(18, 24))
-            act(r("s0rep"), ind(numc, s016))
-        else:
-            ts(node, r("li", 256 * t - 112, 256 * t - 88), 12, A.arith_shift_right)
-            ts(keyw, node, 512.0, A.mult)
-        ts(basew, node, 4.0, A.mult)
-        o = 24 if t == 0 else 0
-        tt(r("lf", 128 * t + o, 128 * t + 48), r("lf", 128 * t + o, 128 * t + 48), r("cf", o, 48), A.add)
-        cp(li(8, 24), r("ksort" if t == 0 else "vs", 15, C, 16))
-        ts(li(16, 24), li(8, 24), 9 if t == 0 else 12, A.arith_shift_right)
-        ts(r("lf", 128 * t + 48, 128 * t + 72), li(16, 24), 512.0, A.mult)
-        for m in range(NB - 1):
-            o = 576 * t + 24 * m
-            ts(r("ml", o, o + 23 - m), r("lf", 128 * t + m + 1, 128 * t + 24), r("lf", 128 * t + 48 + m, 128 * t + 49 + m),
-               A.subtract, float(C), A.min)
-        sn = r("landn", 8 * t, 8 * t + 4)
-        pcp(r("d0", 448 * t, 448 * t + C), r("cc"))
-        tt(li(20, 4), sn, r("landn", 8 * t + 4, 8 * t + 8), A.subtract)
-        ts(li(20, 4), li(20, 4), 1000.0, A.mult)
-        tt(li(20, 4), li(20, 4), r("cf", 120, 124), A.add)
-        tt(li(20, 4), li(20, 4), sn, A.max)
-        cp(lu(108, 4), li(20, 4))
-        cp(ind(r("d0", 448 * t, 448 * t + 448), lu(108, 4)), r("half"))
-        st, en, base = (r("land", 96 * t + 12, 96 * t + 24), r("land", 96 * t + 24, 96 * t + 36),
-                        r("land", 96 * t + 96, 96 * t + 108))
-        rot, nxt = r("ro", 12 * t, 12 * t + 12), r("ro", 12 * t + 12, 12 * t + 24)
-        tt(li(1), en, st, A.subtract)
-        tt(li(2), li(1), rot, A.add)
-        ts(li(3), li(2), 2, A.arith_shift_right)
-        ts(nxt, li(2), 3, A.bitwise_and)
-        tt(li(4, 24), r("land", 96 * t + 12, 96 * t + 36), c4n, A.add)
-        tt(li(4, 24), li(4, 24), r("ro", 12 * t, 12 * t + 24), A.subtract)
-        cp(lu(24, 24), li(4, 24))
-        cp(ind(r("tab", 576 * t, 576 * t + 576), lu(24, 12)), r("num", C, C + E))
-        cp(lu(48, 12), li(3))
-        act(r("crep"), ind(numc, lu(48, 12)))
-        act(r("csrt"), ind(r("crep"), sg16))
-        scan(r("pf", 1, 1 + E), r("ones", 0, E), r("csrt"), A.mult, A.add)
-        act(r("g1", 0, 256), ind(r("pf", 0, 1 + E), ln16))
-        expand(t + 1)
-        ts(li(6), li(3), -1000.0, A.mult)
-        tt(li(6), li(6), e384, A.add)
-        tt(li(6), li(6), base, A.max)
-        ts(li(7), base, -4.0, A.mult, 1540.0, A.add)
-        tt(li(7), li(7), li(4), A.add)
-        cp(lu(60, 24), li(6, 24))
-        tt(r("vrep"), ind(r("numb"), lu(72, 12)), r("to4") if t < 2 else r("e4096"), A.add)
-        cp(ind(r("vw", 576 * t, 576 * t + 576), lu(60, 12)), r("vrep"))
-        act(r("vk"), r("vw", 576 * t, 576 * t + C), F.Relu, bias=1.0, scale=-1.0)
-        scan(r("vs"), r("vk"), r("vw", 576 * t, 576 * t + C), A.mult, A.add)
-        o = 768 * (t % 2)
-        act(r("vg", o + C, o + 768), ind(r("vs"), r("cu", 24, 48)))
-        act(r("vg", o, o + C), ind(r("vs"), r("cu", 0, 24)))
-        spread(r("land", 96 * t + 168, 96 * t + 192), r("vg", o + C, o + 768))
-        spread(r("land", 96 * t + 144, 96 * t + 168), r("vg", o, o + C))
-        cp(li(12, 48), r("land", 96 * t + 144, 96 * t + 192))
-        ts(li(18, 24), li(14, 24), 4095, A.bitwise_and)
-        tt(li(18, 24), li(18, 24), csrc, A.add)
-        cp(lu(84, 24), li(18, 24))
-        if t == 2:
-            ts(li(16, 24), li(12, 24), 12, A.arith_shift_right)
-            cp(lu(0, 24), li(16, 24))
-            act(r("wb"), ind(numc, lu(0, 24)))
-            dma(lambda: T.ot[:], lambda: T.wb[0:128:16, :], [r("wb")], [])
-        return basew, lu(36, 12), lu(84, 24)
+    act(r("th", 32, 35), r("th", 4, 7), bias=1.0)
+    tt(r("th", 36, 39), r("th", 4, 7), r("cs", C - 1, 3 * C, C), A.subtract)
+    act(r("th", 36, 39), r("th", 36, 39), scale=1000.0)
+    tt(r("th", 36, 39), r("th", 36, 39), r("cf", 120, 123), A.add)
+    tt(r("th", 36, 39), r("th", 36, 39), r("th", 32, 35), A.max)
+    cp(r("su", 116, 119), r("th", 36, 39))
+    starts(0, r("su", 116, 119))
 
     def plane(name, b, a, n):
         return r(name, 576 * b + a, 576 * b + a + n)
 
-    for b in range(4):
-        act(plane("xmh", b, C, E), r("mt", b, 768, 4), scale=0.5)
-        pcp(plane("hm", b, C, E), r("mt", b, 768, 4))
+    def ut(k, s, a, n):
+        o = UO[k] + 4 * (a - LO[k]) + s
+        return r("ut", o, o + 4 * n - 3, 4)
+
+    act(r("xmh", 4 * C, 4 * C + 768), xm(MT[0], 768), scale=0.5)
 
     for t in range(ROUNDS):
-        basew, lp16, sp16 = lists(t)
+        exits(t)
         tab = r("tab", 576 * t, 576 * t + 576)
-        quant(r("xq"), r("xp"), r("xt"))
+        quant(r("xq"), r("xp"), xt)
         mm(5, C, r("uq2"), r("up2"), r("xq"), r("xp"))
         if t > 0:
             mm(4, C, r("uq2"), r("up2"), r("xq"), r("xp"))
-        act(r("ssb", 0, C), ps(5, C))
-        sw = r("ssb")
-        sv = ps(4, C) if t > 0 else ind(sw, s016)
-        tt(r("sa"), sv, r("a1"), A.add)
-        scan(r("yy"), r("d0", 448 * t, 448 * t + C), r("sa"), A.max, A.min)
-        for b in range(4):
-            act(plane("xmh", b, 0, C), r("xt", b, 1536, 4), scale=0.5)
-            pcp(r("xth", C * b, C * b + C), plane("xmh", b, 0, C))
-        tt(r("ut", 0, 1536, 4), sv, r("yy"), A.is_gt)
-        scan(r("ds"), keep, r("ut", 0, 1536, 4), A.mult, A.add)
-        for k in range(6):
-            for m in range(max(4 * k - 1, 0), 4 * k + 3):
-                s = m + 1 - 4 * k
-                n = C - 16 * (m + 1)
-                o = r("ut", 1536 * k + 64 * (m + 1) + s, 1536 * k + 1536, 4)
-                src = ind(sw, r("ml", 576 * t + 24 * m, 576 * t + 24 * m + 23 - m))
-                y = r("yy", 16 * m + 15, 16 * m + 16)
-                if m in ACT_ROWS:
+            act(r("ssb", 8, 8 + C), ps(5, C))
+            sv = ps(4, C)
+        else:
+            act(r("ssb", 400, 400 + C), ps(5, C))
+            sv = ind(r("ssb", 400, 400 + C), s016)
+            act(r("ssb", 8, 8 + C), sv)
+        tt(r("sa"), sv, r("a1", 0, C), A.add)
+        scan(r("yy", 0, C), r("d0", 448 * t, 448 * t + C), r("sa"), A.max, A.min)
+        for a, b in ((0, 1), (1, 2), (2, 5)):
+            act(r("st", SO[a], SO[b]), ind(r("ssb", 0, 8 + C), ml(t, 72 + SO[a] // 16, (SO[b] - SO[a]) // 16)))
+        for k in range(3):
+            x, y = r("xmh", 512 * k, 512 * k + 512), r("xmh", 2304 + 512 * k, 2304 + 512 * k + 512)
+            act(x, xm(512 * k, 512), scale=0.5)
+            dma(lambda y=y: ap(y), lambda x=x: ap(x), [x], [y], lat=2900)
+        tt(ut(0, 0, 0, C), sv, r("yy", 0, C), A.is_gt)
+        for d in range(1, 4):
+            tt(ut(0, d, 16 * d, C - 16 * d), ind(r("yy"), ml(t, 24 * d - 24, 24 - d)), r("ssb", 8 + 16 * d, 8 + C), A.is_lt)
+        scan(r("ds", 0, C), ut(0, 0, 0, C), ut(0, 1, 16, C), A.add, A.add)
+        scan(r("ds", C, 2 * C), ut(0, 2, 32, C), ut(0, 3, 48, C), A.add, A.add)
+        tt(r("qq", 1, 25), r("ds", 15, C, 16), r("ds", C + 15, 2 * C, 16), A.add)
+        tt(r("pw", 0, 24), lf(t, 72, 24), r("qq", 1, 25), A.add)
+        tt(r("pw", 0, 24), r("pw", 0, 24), r("qq", 0, 24), A.subtract)
+        for k in TILES:
+            for s in range(4 if k else 0):
+                m = 4 * (k - 1) + s
+                a = 16 * (m + 4)
+                n = C - a
+                src, y = r("st", SO[k - 1] + 16 * s, SO[k]), r("yy", 16 * m + 15, 16 * m + 16)
+                if m < ACT_ROWS:
                     act(r("sg", C * m, C * m + n), src, F.Sign, bias=y, scale=-1.0)
-                    act(o, r("sg", C * m, C * m + n), F.Relu, scale=-1.0, acc=r("rs", m, m + 1))
+                    act(ut(k, s, a, n), r("sg", C * m, C * m + n), F.Relu, scale=r("mk", 40 * t + 20 + m, 40 * t + 21 + m),
+                        acc=r("rs", m, m + 1))
                 else:
-                    ts(o, src, y, A.is_gt)
-                    act(r("junk", C * m, C * m + n), o, F.Relu, acc=r("rs", m, m + 1))
-            lo = 64 * min(k, 4)
-            quant(r("utq", C * k + lo, C * k + C), r("utp", C * k + lo, C * k + C), r("ut", 1536 * k + 4 * lo, 1536 * k + 1536))
-            mm(6, C, r("gq"), r("gp"), r("utq", C * k, C * k + C), r("utp", C * k, C * k + C), k == 0, k == 5)
-        tt(r("pw", 0, 24), basew, r("ds", 15, C, 16), A.add)
-        tt(r("pw", 24, 48), r("pw", 0, 24), r("rs"), A.add)
+                    ts(ut(k, s, a, n), src, y, A.is_gt, r("mk", 40 * t + m, 40 * t + m + 1), A.mult)
+                    scan(r("jr", 160 * m + 160 - n // 2, 160 * m + 160), ut(k, s, a, n // 2), ut(k, s, a + n // 2, n // 2),
+                         A.add, A.add)
+            quant(r("utq", C * k + LO[k], C * k + C), r("utp", C * k + LO[k], C * k + C), r("ut", UO[k], UO[k] + 4 * (C - LO[k])))
+            mm(6, C, r("gq"), r("gp"), r("utq", C * k, C * k + C), r("utp", C * k, C * k + C), k == TILES[0], k == TILES[-1])
+        tt(r("pw", ACT_ROWS, 20), r("pw", ACT_ROWS, 20), r("jr", 160 * ACT_ROWS + 159, 3200, 160), A.add)
+        tt(r("pw", 0, ACT_ROWS), r("pw", 0, ACT_ROWS), r("rs", 0, ACT_ROWS), A.add)
         tt(r("w1"), ps(6, C), r("dm"), A.mult)
         scan(r("w2"), keep, r("w1"), A.mult, A.add)
-        tt(r("pw", 48, 72), r("pw", 24, 48), r("w2", 15, C, 16), A.subtract)
+        tt(r("pw", 48, 72), r("pw", 0, 24), r("w2", 15, C, 16), A.subtract)
         cp(r("pu", 0, 24), r("pw", 48, 72))
-        cp(ind(tab, r("pu", 0, 24)), numc if t > 0 else r("s0rep"))
+        cp(ind(tab, r("pu", 0, 24)), numc if t > 0 else r("ksort"))
         ts(r("pu", 24, 48), r("pw", 48, 72), -4.0, A.add)
         if t > 0:
-            tt(r("w3"), ind(tab, r("pu", 24, 48)), r("dm"), A.mult)
+            tt(r("w3"), ind(tab, r("pu", 24, 48)), r("dm4"), A.mult)
         else:
             cp(r("wa"), ind(tab, r("pu", 24, 48)))
-            tt(r("w3"), ind(r("wa"), rk16), r("dm"), A.mult)
-        scan(r("w4"), keep, r("w3"), A.mult, A.add)
-        cp(r("pu", 48, 72), r("w4", 15, C, 16))
-        act(r("srep"), ind(tab, sp16))
-        spread(r("land2", 40 * t, 40 * t + 24), r("srep"))
-        act(r("lrep"), ind(tab, lp16))
-        act(r("lrep2"), ind(r("lrep"), g1216))
-        spread(r("land2", 40 * t + 24, 40 * t + 36), r("lrep2"))
-        sk16, la16 = r("du", 40 * t, 40 * t + 24), r("du", 40 * t + 24, 40 * t + 36)
-        cp(sk16, r("land2", 40 * t, 40 * t + 24))
-        cp(la16, r("land2", 40 * t + 24, 40 * t + 36))
+            tt(r("w3"), ind(r("wa"), rk16), r("dm4"), A.mult)
+        scan(r("w4"), r("keep4"), r("w3"), A.mult, A.add)
+        ts(r("pu", 48, 144), r("w4", 3, C, 4), 4.0, A.mult, r("pm", 6, 7), A.add)
+        act(r("srep"), ind(tab, r("sp", 24 * t, 24 * t + 24)))
+        spread(r("land2", 0, 24), r("srep"))
         for b in range(4):
-            tt(r("zt", b, 1536, 4), ind(plane("xmh", b, 0, 576), r("pu", 48, 72)), r("xth", C * b, C * b + C), A.add)
-        quant(r("zq"), r("zp"), r("zt"))
+            act(r("land2", 24 + 24 * b, 48 + 24 * b), r("land2", 0, 24), scale=4.0, bias=float(b))
+        cp(r("du", 0, 120), r("land2", 0, 120))
+        sk16 = r("du", 0, 24)
+        if t == 2:
+            act(r("lrep", 0, E), ind(tab, lu(t, 12, 12)))
+            act(r("lrep", E, 2 * E), ind(r("lrep", 0, E), g1216))
+            spread(r("land2", 120, 132), r("lrep", E, 2 * E))
+            for b in range(4):
+                act(r("land2", 132 + 12 * b, 144 + 12 * b), r("land2", 120, 132), scale=4.0, bias=float(b))
+            cp(r("du", 120, 180), r("land2", 120, 180))
+        for h, (a, n) in enumerate(((0, ZA), (ZA, C - ZA))):
+            tt(xm(ZT + 4 * a, 4 * n), ind(r("xmh", 0, 2304), r("pu", 48 + a // 4, 48 + (a + n) // 4)),
+               r("xmh", 2304 + 4 * a, 2304 + 4 * (a + n)), A.add)
+            quant(r("zq", a, a + n), r("zp", a, a + n), xm(ZT + 4 * a, 4 * n))
+            for b in range(4):
+                mm(4 * h + b, n, r("wq", 128 * b, 128 * b + 128), r("wp", 128 * b, 128 * b + 128), r("zq", a, a + n),
+                   r("zp", a, a + n))
+                act(plane("rr", b, a, n), ps(4 * h + b, n), F.Relu, scale=0.03125)
+        new = r("mt") if t == 2 else xm(MT[t + 1], 768)
+
+        def mem(a, n, b=0, s=1, new=new):
+            return (new[0], new[1] + 4 * a + b, new[1] + 4 * (a + n), s)
+        if t == 2:
+            for a, n in ((0, K), (K, E - K)):
+                for b in range(4):
+                    zl = r("zl", E * b + a, E * b + a + n)
+                    act(zl, ind(xm(ZT, 4 * C + 768), r("du", 132 + 12 * b + a // 16, 132 + 12 * b + (a + n) // 16)))
+                    tt(mem(a, n, b, 4), ind(plane("rr", b, 0, 576), r("du", 120 + a // 16, 120 + (a + n) // 16)), zl, A.add)
         for b in range(4):
-            mm(b, C, r("wq", 128 * b, 128 * b + 128), r("wp", 128 * b, 128 * b + 128), r("zq"), r("zp"))
-            act(plane("rr", b, 0, C), ps(b, C), F.Relu, scale=0.03125)
-            if t == 2:
-                act(plane("hm", b, 0, C), r("zt", b, 1536, 4))
-                cp(r("zl", E * b, E * b + E), ind(plane("hm", b, 0, 576), la16))
-                tt(r("mt", b, 768, 4), ind(plane("rr", b, 0, 576), la16), r("zl", E * b, E * b + E), A.add)
-            tt(plane("hm", b, 0, C), plane("rr", b, 0, C), r("zt", b, 1536, 4), A.add)
-        for b in range(4):
-            if t < 2:
-                act(r("mt", b, 768, 4), ind(plane("hm", b, 0, 576), la16))
-            (cp if b == 3 else act)(r("xt", b, 1536, 4), ind(plane("hm", b, 0, 576), sk16))
+            zg = r("zg", C * b, C * b + C)
+            (cp if b in ZG_DVE else act)(zg, ind(zt, r("du", 24 + 24 * b, 48 + 24 * b)))
+            tt(xm(b, 4 * C - b, 4), ind(plane("rr", b, 0, C), sk16), zg, A.add)
+        if t < 2:
+            for a, n in ((0, K), (K, E - K)):
+                for b in range(4):
+                    act(mem(a, n, b, 4), ind(xm(0, MT[t] + 768), lu(t, 64 + 12 * b + a // 16, n // 16)))
         bq, bp, aq, apl = r("bq%d" % t), r("bp%d" % t), r("aq%d" % t), r("ap%d" % t)
-        quant(bq, bp, r("mt", 0, 4 * K))
+        quant(bq, bp, mem(0, K))
         peer = T.cores[rank ^ STEP[t]]
         rid, pid = topo.addr(peer)[:2]
         eng = topo.engines(core, peer)
@@ -512,21 +579,17 @@ def build(g, core, T, topo, rank):
             g.remote_dma(ap(apl), ap(bp), T.sem["arr%d" % t], T.sem["out%d" % t], pid, rid, m2)
         add("pool", send, [bq, bp], [aq, apl], 600, lat=3600, kind="remote", sem=("arr%d" % t, "out%d" % t, len(eng)))
         for b in range(4):
-            bank = 7 if b % 2 == 0 or t < 2 else 6
-            mm(bank, K, r("eq", 128 * b, 128 * b + 128), r("ep", 128 * b, 128 * b + 128), aq, apl)
-            if t < 2:
-                act(plane("hm", b, C, K), ps(bank, K))
-                act(plane("xmh", b, C, K), ps(bank, K), scale=0.5)
-                pcp(plane("hm", b, C + K, E - K), r("mt", 4 * K + b, 768, 4))
-                act(plane("xmh", b, C + K, E - K), r("mt", 4 * K + b, 768, 4), scale=0.5)
-            else:
-                (act if b % 2 == 0 else cp)(r("mt", b, 4 * K, 4), ps(bank, K))
-    quant(r("xq"), r("xp"), r("xt"))
+            mm(b, K, r("eq", 128 * b, 128 * b + 128), r("ep", 128 * b, 128 * b + 128), aq, apl)
+            (cp if t == 2 and b % 2 else act)(mem(0, K, b, 4), ps(b, K))
+        if t < 2:
+            for a, n in ((0, K), (K, E - K)):
+                act(r("xmh", 4 * (C + a), 4 * (C + a + n)), mem(a, n), scale=0.5)
+    quant(r("xq"), r("xp"), xt)
     mm(4, C, r("vq"), r("vp"), r("xq"), r("xp"))
     act(r("ysb"), ps(4, C))
-    dma(lambda: T.y[:], lambda: T.ysb[:], [r("ysb")], [])
+    dma(lambda: T.y[:], lambda: T.ysb[:], [r("ysb")], [], lat=3200)
     quant(r("mq"), r("mp"), r("mt"))
-    dma(lambda: T.oc[:], lambda: u8(r("mq")), [r("mq")], [])
+    dma(lambda: T.oc[:], lambda: u8(r("mq")), [r("mq")], [], lat=2700)
     for k in range(4):
         dma(lambda k=k: T.osc[4 * k:4 * k + 4, :], lambda k=k: T.mp[32 * k:32 * k + 4, :], [r("mp")], [],
             eng="sp" if k < 2 else "act")
@@ -553,27 +616,23 @@ def order(ops):
             far[j] = max(far[j], far[i] + hop)
     n = len(ops)
     deps = [sorted(o["dep"]) for o in ops]
-    runs, key = [], {}
-    for i, o in enumerate(ops):
-        name = ((o["wr"] or o["rd"])[0][0], o["eng"])
-        if name not in key or i - key[name][1] > GAP:
-            key[name] = [len(set(runs)), i]
-        key[name][1] = i
-        runs.append(key[name][0])
+    after = [[] for o in ops]
+    for i in range(n):
+        for j in deps[i]:
+            after[j].append(i)
 
-    def place(shift):
-        p = [far[i] + shift[runs[i]] for i in range(n)]
-        for i in range(n - 1, -1, -1):
-            for j in deps[i]:
-                if p[j] <= p[i]:
-                    p[j] = p[i] + 1
+    def place(urge, back):
+        p = list(urge)
+        for i in (range(n) if back else range(n - 1, -1, -1)):
+            for j in (after[i] if back else deps[i]):
+                p[j] = max(p[j], p[i] + 1e-3)
         busy, st, en = {}, [0.0] * n, [0.0] * n
         for i in sorted(range(n), key=lambda i: -p[i]):
             o = ops[i]
             s, d = 0.0, o["dur"]
-            for j in deps[i]:
-                if en[j] + hop > s:
-                    s = en[j] + hop
+            for j in (after[i] if back else deps[i]):
+                s = max(s, en[j] + hop)
+            s += o["lat"] if back else 0
             line = busy.setdefault(o["eng"], [])
             k = len(line)
             while k > 0 and line[k - 1][1] > s:
@@ -582,20 +641,20 @@ def order(ops):
                 s = max(s, line[k][1])
                 k += 1
             line.insert(k, (s, s + d))
-            st[i], en[i] = s, s + d + o["lat"]
+            st[i], en[i] = s, s + d + (0 if back else o["lat"])
         return max(en), st, en
 
     if "best" not in PLAN:
         rng = np.random.default_rng(SEED)
-        shift = [0.0] * (max(runs) + 1)
-        best = place(shift)
+        best = now = place(far, False)
         for rep in range(PASSES):
-            other = list(shift)
-            for k in rng.integers(0, len(shift), 3):
-                other[int(k)] += float(rng.normal()) * SIG[rep % 3]
-            got = place(other)
-            if got[0] <= best[0]:
-                best, shift = got, other
+            noise = rng.normal(size=n) * SIG[rep % len(SIG)]
+            late = place([now[2][i] + float(noise[i]) for i in range(n)], True)
+            now = place(late[2], False)
+            if now[0] <= best[0]:
+                best = now
+            elif now[0] > best[0] * SLACK:
+                now = best
         PLAN["best"] = best
     for i, o in enumerate(ops):
         o["start"], o["end"] = PLAN["best"][1][i], PLAN["best"][2][i]

@@ -16,10 +16,19 @@ UO = (0, 1728, 3008, 4032, 4800, 5312)
 SO = (0, 320, 576, 768, 896, 960)
 TILES = (0, 3, 4, 5, 1, 2)
 ACT_ROWS = 8
-ZG_DVE = (1,)
+ZG_DVE = ()
+RELU_DVE = ((1, 0), (1, 1), (1, 2), (1, 3))
+XRUNS = ((0, 128), (128, 128), (256, 128))
+SK_Q = "sp"
+LONG = 1e9
+HOP, LATE, SLOW, MORE, AC = 180, {}, {}, {}, 78
+SMALL_DVE = ()
+WIDE = 6000
+XH = ((0, 768), (768, 768))
+S0_DMA = True
 ZA = 256
 MT, ZT = (1536, 2304, 4608), 3072
-SIG, SLACK, PASSES, SEED, PLAN = (100, 300, 1000), 1.01, 1500, 2, {}
+SIG, SLACK, PASSES, SEED, PLAN = (300, 1000, 3000), 200, 5000, 2, {}
 
 
 def _sb(n, d):
@@ -34,9 +43,9 @@ SCRATCH = {
     "pi": _sb(8, I32), "pm": _sb(8, F32), "i16": _sb(2 * C, BF), "dm": _sb(C, BF), "dm4": _sb(C, BF),
     "a1": _sb(2 * C, BF), "keep": _sb(416, BF), "keep4": _sb(C, BF),
     "cc": _sb(C, BF), "half": _sb(64, BF), "ones": _sb(512, BF), "c1": _sb(512, BF), "gb": _sb(512, BF),
-    "eb": _sb(2048, BF), "zb": _sb(1024, BF), "gq": _sb(128, CODE), "gp": _sb(128, PLANE), "eq": _sb(512, CODE),
+    "eb": _sb(2048, BF), "zb": _sb(512, BF), "gq": _sb(128, CODE), "gp": _sb(128, PLANE), "eq": _sb(512, CODE),
     "ep": _sb(512, PLANE), "zq0": _sb(256, CODE), "zp0": _sb(256, PLANE),
-    "ci": _sb(256, I32), "cf": _sb(256, F32), "cu": _sb(128, U16), "uo": _sb(8, U16),
+    "ci": _sb(24, I32), "cf": _sb(504, F32), "cu": _sb(128, U16), "uo": _sb(8, U16),
     "ksort": _sb(C, F32), "lt": _sb(C * 3, BF), "cs": _sb(C * 3, F32), "nrp": _sb(C, BF),
     "ff": _sb(416, F16), "tr": _sb(800, F16), "trs": _sb(800, F16),
     "th": _sb(64, F32), "acc": _sb(64, F32), "su": _sb(128, U16),
@@ -50,7 +59,7 @@ SCRATCH = {
     "ut": _sb(5824, BF), "utq": _sb(6 * C, CODE), "utp": _sb(6 * C, PLANE), "sg": _sb(16 * C, BF), "rs": _sb(24, F32),
     "ds": _sb(2 * C, F16), "jr": _sb(3200, F16), "qq": _sb(32, F32), "pw": _sb(96, F32),
     "pu": _sb(144, U16), "w1": _sb(C, F16), "w2": _sb(C, F16), "w3": _sb(C, F16), "w4": _sb(C, F16),
-    "srep": _sb(C, F32), "lrep": _sb(2 * E, F32), "land2": _sb(180, F32), "du": _sb(180, U16),
+    "srep": _sb(C, F32), "land2": _sb(96, F32), "du": _sb(144, U16),
     "xm": _sb(5376, BF), "xmh": _sb(3840, BF), "xq": _sb(C, CODE), "xp": _sb(C, PLANE), "zq": _sb(C, CODE), "zp": _sb(C, PLANE),
     "rr": _sb(4 * 576, F32), "zl": _sb(768, BF), "zg": _sb(1536, BF),
     "mt": _sb(768, BF), "mq": _sb(E, CODE), "mp": _sb(E, PLANE), "ysb": _sb(C, F32),
@@ -157,7 +166,7 @@ def build(g, core, T, topo, rank):
             if acc is not None:
                 kw["accum_out"] = ap(acc)
             return g.scalar.activation(ap(out), ap(in_), func, **kw)
-        d = 78 + 1.56 * cnt(out) if in_[0] == "ind" else 60 + cnt(out)
+        d = 78 + 1.56 * cnt(out) if in_[0] == "ind" else AC + cnt(out)
         add("act", fn, [in_, bias, scale], [out, acc], d + (24 if acc else 0))
 
     def mm(bank, n, lq, lp, rq, rp, start=True, stop=True):
@@ -216,48 +225,50 @@ def build(g, core, T, topo, rank):
     cp(r("pm", 0, 1), r("pi", 2, 3))
     pm, keep = r("pm", 0, 1), r("keep", 0, C)
     ts(r("dm"), r("i16", 0, C), pm, A.is_equal)
-    act(r("a1", 0, C), r("dm"), scale=-BIG, bias=BIG)
+    ts(r("a1", 0, C), r("dm"), -BIG, A.mult, BIG, A.add)
     sel(r("keep"), r("ones", 0, 416), [[0, NB + 2], [1, 16]], A.is_gt, 0, 0)
-    act(r("a1", C, 2 * C), r("dm"), bias=-BIG / 2, scale=BIG)
+    ts(r("a1", C, 2 * C), r("dm"), BIG, A.mult, -BIG / 2, A.add)
     sel(r("cc"), r("a1", C, 2 * C), [[0, NB], [1, 16]], A.is_gt, 0, 0, BIG / 2)
     act(r("half"), r("num", 0, 64), scale=BIG / 128, bias=BIG / 2)
     cp(r("uo"), r("ci", 0, 8))
     jw = r("cf", 0, 24)
     ts(jw, r("ci", 0, 24), pm, A.add)
-    j12, ga = r("cf", 0, 12), r("cf", 136, 160)
+    j12, ga = r("cf", 0, 12), r("cf", 256, 280)
 
-    def turn(out, x, w, t1, t2, t3):
-        ts(t2, x, float(65536 // w + 1), A.mult)
-        ts(t1, t2, 16, A.arith_shift_right)
-        ts(t3, t1, -float(16 * w - 1) / 16, A.mult)
-        tt(t3, x, t3, A.add)
-        ts(out, t3, 16.0, A.mult)
+    def above(out, x, w):
+        act(out, x, scale=1.0 / w, bias=0.5 / w - 0.5)
+        act(out, out, bias=WHOLE)
 
-    turn(ga, jw, 24, r("ci", 24, 48), r("ci", 48, 72), r("cf", 200, 224))
-    turn(r("cu", 24, 48), ga, 24, r("ci", 72, 96), r("ci", 96, 120), r("cf", 224, 248))
-    turn(r("cu", 48, 60), j12, 12, r("ci", 120, 132), r("ci", 132, 144), r("cf", 72, 84))
+    def turn(out, x, w, t1, t2, h=16):
+        above(t1, x, w)
+        act(t2, x, scale=float(h))
+        ts(t1, t1, -WHOLE, A.add, -float(h * w - 1), A.mult)
+        tt(out, t1, t2, A.add)
+
+    turn(ga, jw, 24, r("cf", 352, 376), r("cf", 376, 400))
+    turn(r("cf", 280, 304), ga, 96, r("cf", 400, 424), r("cf", 424, 448), 4)
+    turn(r("cf", 200, 224), jw, 96, r("cf", 224, 248), r("cf", 480, 504), 4)
+    turn(r("cf", 304, 316), j12, 12, r("cf", 448, 460), r("cf", 460, 472))
+    turn(r("cf", 192, 196), r("cf", 0, 4), 4, r("cf", 472, 476), r("cf", 476, 480))
+    above(r("cf", 72, 84), r("cf", 304, 316), 4)
+    for k in range(2):
+        act(r("cf", 316 + 12 * k, 328 + 12 * k), r("cf", 72, 84), bias=E + k - WHOLE)
+        act(r("cf", 340 + 4 * k, 344 + 4 * k), r("cf", 192, 196), bias=float(E + k))
     cp(r("cu", 0, 24), ga)
+    cp(r("cu", 24, 48), r("cf", 280, 304))
+    cp(r("cu", 48, 92), r("cf", 304, 348))
     g1216 = r("cu", 48, 60)
-    ts(r("ci", 144, 156), r("ci", 120, 132), 2, A.arith_shift_right)
-    ts(r("ci", 156, 168), r("ci", 120, 132), -48.0, A.mult, float(E), A.add)
-    tt(r("ci", 156, 168), r("ci", 156, 168), r("ci", 144, 156), A.add)
-    ts(r("cf", 84, 96), j12, 4.0, A.mult)
-    tt(r("cf", 84, 96), r("cf", 84, 96), r("ci", 156, 168), A.add)
-    cp(r("cu", 60, 72), r("cf", 84, 96))
-    ts(r("cu", 72, 84), r("cf", 84, 96), 1.0, A.add)
-    turn(r("cf", 192, 196), r("cf", 0, 4), 4, r("ci", 204, 208), r("ci", 208, 212), r("cf", 196, 200))
-    ts(r("cu", 84, 88), r("cf", 192, 196), float(E), A.add)
-    ts(r("cu", 88, 92), r("cf", 192, 196), float(E + 1), A.add)
-    csrc, c4n = r("cf", 96, 120), r("ci", 212, 224)
-    act(csrc, ga, scale=4.0, bias=-1536.0)
+    csrc, c4n = r("cf", 96, 120), r("cf", 84, 96)
+    act(csrc, r("cf", 200, 224), scale=4.0, bias=-1536.0)
     act(r("cf", 120, 132), j12, bias=float(C))
     act(r("cf", 132, 136), r("cf", 0, 4), bias=float(C))
-    act(r("cf", 24, 48), jw, scale=-1.0)
+    act(r("cf", 24, 48), jw, bias=8.0)
+    iota(r("mk"), [[0, 120]], 1)
     act(r("cf", 48, 72), jw, bias=4.0)
-    cp(r("ci", 168, 180), j12)
-    ts(r("ci", 192, 204), r("ci", 168, 180), 3, A.bitwise_and)
-    ts(r("ro", 0, 12), r("ci", 192, 204), -1.0, A.mult, 3.0, A.add)
-    tt(c4n, r("ci", 168, 180), r("ro", 0, 12), A.add)
+    above(r("cf", 136, 148), j12, 4)
+    act(c4n, r("cf", 136, 148), bias=-WHOLE)
+    act(c4n, c4n, scale=4.0, bias=3.0)
+    tt(r("ro", 0, 12), c4n, j12, A.subtract)
     sel(r("c1"), r("ones"), [[-16, 8], [0, 64]], A.is_ge, 0, 1)
     sel(r("gb"), r("c1"), [[16, 8], [0, 64]], A.is_ge, 15, -1)
     quant(r("gq"), r("gp"), r("gb"))
@@ -265,8 +276,10 @@ def build(g, core, T, topo, rank):
         n = 4 * (max(64 * k, 0) + 48 - LO[k])
         iota(r("ut", UO[k], UO[k] + n), [[0, n]])
     iota(r("ut", 1536, 1536 + 192), [[0, 192]])
-    iota(r("zb"), [[0, 1024]])
-    quant(r("zq0"), r("zp0"), r("zb"))
+    iota(r("zb"), [[0, 512]])
+    quant(r("zq0", 0, 128), r("zp0", 0, 128), r("zb"))
+    dma(lambda: u8(r("zq0", 128, 256)), lambda: u8(r("zq0", 0, 128)), [r("zq0", 0, 128)], [r("zq0", 128, 256)])
+    dma(lambda: T.zp0[:, 128:256], lambda: T.zp0[:, 0:128], [r("zp0", 0, 128)], [r("zp0", 128, 256)])
     for k in range(1, 6):
         dq, dp = r("utq", C * k, C * k + LO[k]), r("utp", C * k, C * k + LO[k])
         dma(lambda dq=dq, w=LO[k]: u8(dq), lambda w=LO[k]: u8(r("zq0", 0, w)), [r("zq0")], [dq])
@@ -277,7 +290,7 @@ def build(g, core, T, topo, rank):
         iota(r("d0", 448 * t + C, 448 * t + 448), [[0, 64]])
     for b in range(4):
         sel(r("eb", 512 * b, 512 * b + 512), r("ones"), [[-1, 512]], A.is_equal, b, 4)
-        iota(r("rr", 576 * b + C, 576 * b + 576), [[0, E]])
+    iota(r("rr", 4 * C, 4 * C + 768), [[0, 768]])
     quant(r("eq"), r("ep"), r("eb"))
     act(r("ssb", 0, 8), r("ones", 0, 8), scale=-BIG)
     act(r("yy", C, 400), r("ones", 0, 16), scale=BIG)
@@ -333,16 +346,22 @@ def build(g, core, T, topo, rank):
     tt(r("pw", 48, 72), r("pw", 0, 24), r("pw", 24, 48), A.add)
     cp(rk16, r("pw", 48, 72))
     cp(ind(r("ksort"), rk16), numc)
-    tt(r("w1"), r("ksort"), r("dm"), A.mult)
-    scan(r("w2"), keep, r("w1"), A.mult, A.add)
-    cp(s016, r("w2", 15, C, 16))
+    if S0_DMA:
+        act(r("srep"), ind(r("ksort"), r("cu", 0, 24)))
+        spread(r("lv", 72, 96), r("srep"))
+        cp(s016, r("lv", 72, 96))
+    else:
+        tt(r("w1"), r("ksort"), r("dm"), A.mult)
+        scan(r("w2"), keep, r("w1"), A.mult, A.add)
+        cp(s016, r("w2", 15, C, 16))
     cp(ex16, r("exi"))
     tt(r("xrep"), ind(r("t512"), ex16), r("num", 0, E), A.add)
     ts(r("cf", 160, 172), r("exi"), 512.0, A.mult)
     tt(r("cf", 160, 172), r("cf", 160, 172), j12, A.add)
     act(r("cf", 172, 176), r("cf", 0, 4), scale=512.0)
     act(r("cf", 176, 192), r("cf", 160, 176), scale=-1.0, bias=0.5)
-    for m in range(16):
+    iota(r("acc", 47, 48), [[0, 1]], -E)
+    for m in range(15):
         act(r("sg", C * m, C * m + E), r("xrep"), F.Sign, bias=r("cf", 176 + m, 177 + m), acc=r("acc", 32 + m, 33 + m))
     ts(ln16, r("acc", 32, 48), -0.5, A.mult, E / 2, A.add)
     cp(ind(r("sig"), r("su", 88, 100)), r("num", 0, E))
@@ -379,19 +398,27 @@ def build(g, core, T, topo, rank):
         act(r("vg", 0, C), ind(r("nd"), r("cu", 0, 24)), scale=65536 / BIG, bias=-32768.0)
         spread(n512, r("vg", 0, C))
         act(last, r("nd", 15, C, 16), scale=65536 / BIG, bias=-32768.0)
-        act(lf(t, 24, 24), n512, scale=1.0 / 128)
-        tt(lf(t, 48, 48), lf(t, 0, 48), r("cf", 24, 72), A.add)
+        act(lf(t, 24, 24), n512, scale=-1.0 / 128)
+        tt(lf(t, 48, 48), r("cf", 24, 72), lf(t, 0, 48), A.subtract)
         tt(lf(t, 120, 24), last, r("num", 15, C, 16), A.subtract)
         for d in range(1, 4):
             tt(r("bl", 24 * d - 24, 24 * d - d), lf(t, d, 24 - d), lf(t, 120, 24 - d), A.subtract)
-        act(lf(t, 144, 24), last, bias=8.0)
-        act(lf(t, 168, 24), last, scale=-1.0, bias=1.0)
-        for k in range(5):
-            act(r("bl", 72 + SO[k] // 16, 72 + SO[k + 1] // 16), lf(t, 52 + 4 * k, 20 - 4 * k), F.Relu, scale=-1.0,
-                bias=lf(t, 147 + 4 * k, 1))
-            act(r("mk", 40 * t + 4 * k, 40 * t + 4 * k + 4), lf(t, 96 + 4 * k, 4), F.Relu, bias=lf(t, 171 + 4 * k, 1))
+        if "bl" in SMALL_DVE:
+            for k in range(5):
+                ts(ml(t, 72 + SO[k] // 16, 20 - 4 * k), lf(t, 52 + 4 * k, 20 - 4 * k), lf(t, 99 + 4 * k, 1), A.add, 0.0, A.max)
+            ts(ml(t, 0, 72), r("bl", 0, 72), 399.0, A.min)
+        else:
+            for k in range(5):
+                act(r("bl", 72 + SO[k] // 16, 72 + SO[k + 1] // 16), lf(t, 52 + 4 * k, 20 - 4 * k), F.Relu, bias=lf(t, 99 + 4 * k, 1))
+            ts(ml(t, 0, 132), r("bl"), 399.0, A.min)
+        if "mk" in SMALL_DVE:
+            for q in range(3):
+                tt(r("mk", 40 * t + q, 40 * t + 20, 4), lf(t, 99, 17, 4), lf(t, 96 + q, 17, 4), A.is_equal)
+        else:
+            act(lf(t, 168, 24), last, scale=-1.0, bias=1.0)
+            for k in range(5):
+                act(r("mk", 40 * t + 4 * k, 40 * t + 4 * k + 4), lf(t, 96 + 4 * k, 4), F.Relu, bias=lf(t, 171 + 4 * k, 1))
         act(r("mk", 40 * t + 20, 40 * t + 40), r("mk", 40 * t, 40 * t + 20), scale=-1.0)
-        ts(ml(t, 0, 132), r("bl"), 399.0, A.min)
 
     def exits(t):
         st, en, rot, nxt = land(t, 20, 12), land(t, 32, 12), r("ro", 12 * t, 12 * t + 12), r("ro", 12 * t + 12, 12 * t + 24)
@@ -426,9 +453,13 @@ def build(g, core, T, topo, rank):
             tt(b4, b4, c4, A.add)
             act(lf(t, 300, 12), lf(t, 244, 12), scale=4.0, bias=float(4 + 4 * E * t - 1540))
             tt(b4, b4, lf(t, 300, 12), A.max)
-            for b in range(4):
-                act(r("l4", 12 * b, 12 * b + 12), b4, bias=float(1536 + b))
-            cp(lu(t, 64, 48), r("l4", 0, 48))
+            if "l4" in SMALL_DVE:
+                for b in range(4):
+                    ts(lu(t, 64 + 12 * b, 12), b4, float(1536 + b), A.add)
+            else:
+                for b in range(4):
+                    act(r("l4", 12 * b, 12 * b + 12), b4, bias=float(1536 + b))
+                cp(lu(t, 64, 48), r("l4", 0, 48))
             act(r("vrep"), ind(r("numb"), lu(t, 36, 12)))
         else:
             tt(r("vrep"), ind(r("numb"), lu(t, 36, 12)), r("e8192"), A.add)
@@ -484,9 +515,9 @@ def build(g, core, T, topo, rank):
         scan(r("yy", 0, C), r("d0", 448 * t, 448 * t + C), r("sa"), A.max, A.min)
         for a, b in ((0, 1), (1, 2), (2, 5)):
             act(r("st", SO[a], SO[b]), ind(r("ssb", 0, 8 + C), ml(t, 72 + SO[a] // 16, (SO[b] - SO[a]) // 16)))
-        for k in range(3):
-            x, y = r("xmh", 512 * k, 512 * k + 512), r("xmh", 2304 + 512 * k, 2304 + 512 * k + 512)
-            act(x, xm(512 * k, 512), scale=0.5)
+        for a, n in XH:
+            x, y = r("xmh", a, a + n), r("xmh", 2304 + a, 2304 + a + n)
+            act(x, xm(a, n), scale=0.5)
             dma(lambda y=y: ap(y), lambda x=x: ap(x), [x], [y], lat=2900)
         tt(ut(0, 0, 0, C), sv, r("yy", 0, C), A.is_gt)
         for d in range(1, 4):
@@ -528,18 +559,14 @@ def build(g, core, T, topo, rank):
         scan(r("w4"), r("keep4"), r("w3"), A.mult, A.add)
         ts(r("pu", 48, 144), r("w4", 3, C, 4), 4.0, A.mult, r("pm", 6, 7), A.add)
         act(r("srep"), ind(tab, r("sp", 24 * t, 24 * t + 24)))
-        spread(r("land2", 0, 24), r("srep"))
         for b in range(4):
-            act(r("land2", 24 + 24 * b, 48 + 24 * b), r("land2", 0, 24), scale=4.0, bias=float(b))
-        cp(r("du", 0, 120), r("land2", 0, 120))
-        sk16 = r("du", 0, 24)
+            dma(lambda b=b: T.land2[b:128:4, :], lambda: T.srep[0:128:16, :], [r("srep")], [("land2", b, 96, 4)],
+                eng="sp" if b % 2 else SK_Q)
+        ts(r("du", 0, 96), r("land2"), 4.0, A.mult, r("pm", 6, 7), A.add)
         if t == 2:
-            act(r("lrep", 0, E), ind(tab, lu(t, 12, 12)))
-            act(r("lrep", E, 2 * E), ind(r("lrep", 0, E), g1216))
-            spread(r("land2", 120, 132), r("lrep", E, 2 * E))
-            for b in range(4):
-                act(r("land2", 132 + 12 * b, 144 + 12 * b), r("land2", 120, 132), scale=4.0, bias=float(b))
-            cp(r("du", 120, 180), r("land2", 120, 180))
+            tt(r("w1", 0, E), ind(tab, lu(t, 12, 12)), r("dm4", 0, E), A.mult)
+            scan(r("w2", 0, E), r("keep4", 0, E), r("w1", 0, E), A.mult, A.add)
+            ts(r("du", 96, 144), r("w2", 3, E, 4), 4.0, A.mult, r("pm", 6, 7), A.add)
         for h, (a, n) in enumerate(((0, ZA), (ZA, C - ZA))):
             tt(xm(ZT + 4 * a, 4 * n), ind(r("xmh", 0, 2304), r("pu", 48 + a // 4, 48 + (a + n) // 4)),
                r("xmh", 2304 + 4 * a, 2304 + 4 * (a + n)), A.add)
@@ -547,21 +574,23 @@ def build(g, core, T, topo, rank):
             for b in range(4):
                 mm(4 * h + b, n, r("wq", 128 * b, 128 * b + 128), r("wp", 128 * b, 128 * b + 128), r("zq", a, a + n),
                    r("zp", a, a + n))
-                act(plane("rr", b, a, n), ps(4 * h + b, n), F.Relu, scale=0.03125)
+                if (h, b) in RELU_DVE:
+                    ts(r("rr", 4 * a + b, 4 * (a + n), 4), ps(4 * h + b, n), 0.0, A.max, 0.03125, A.mult)
+                else:
+                    act(r("rr", 4 * a + b, 4 * (a + n), 4), ps(4 * h + b, n), F.Relu, scale=0.03125)
         new = r("mt") if t == 2 else xm(MT[t + 1], 768)
 
         def mem(a, n, b=0, s=1, new=new):
             return (new[0], new[1] + 4 * a + b, new[1] + 4 * (a + n), s)
         if t == 2:
             for a, n in ((0, K), (K, E - K)):
-                for b in range(4):
-                    zl = r("zl", E * b + a, E * b + a + n)
-                    act(zl, ind(xm(ZT, 4 * C + 768), r("du", 132 + 12 * b + a // 16, 132 + 12 * b + (a + n) // 16)))
-                    tt(mem(a, n, b, 4), ind(plane("rr", b, 0, 576), r("du", 120 + a // 16, 120 + (a + n) // 16)), zl, A.add)
-        for b in range(4):
-            zg = r("zg", C * b, C * b + C)
-            (cp if b in ZG_DVE else act)(zg, ind(zt, r("du", 24 + 24 * b, 48 + 24 * b)))
-            tt(xm(b, 4 * C - b, 4), ind(plane("rr", b, 0, C), sk16), zg, A.add)
+                zl, la = r("zl", 4 * a, 4 * (a + n)), r("du", 96 + a // 4, 96 + (a + n) // 4)
+                act(zl, ind(xm(ZT, 4 * C + 768), la))
+                tt(mem(a, n), ind(r("rr"), la), zl, A.add)
+        for h, (a, n) in enumerate(XRUNS):
+            zg, sk = r("zg", 4 * a, 4 * (a + n)), r("du", a // 4, (a + n) // 4)
+            (cp if h in ZG_DVE else act)(zg, ind(zt, sk))
+            tt(xm(4 * a, 4 * n), ind(r("rr", 0, 4 * C), sk), zg, A.add)
         if t < 2:
             for a, n in ((0, K), (K, E - K)):
                 for b in range(4):
@@ -597,7 +626,10 @@ def build(g, core, T, topo, rank):
 
 
 def order(ops):
-    hop = 110
+    hop = HOP
+    for o in ops:
+        o["lat"] += LATE.get(o["kind"], 0)
+        o["dur"] = o["dur"] * SLOW.get(o["eng"], 1) + MORE.get(o["eng"], 0)
     hist = {}
     for i, o in enumerate(ops):
         dep = set()
@@ -648,13 +680,13 @@ def order(ops):
         rng = np.random.default_rng(SEED)
         best = now = place(far, False)
         for rep in range(PASSES):
-            noise = rng.normal(size=n) * SIG[rep % len(SIG)]
-            late = place([now[2][i] + float(noise[i]) for i in range(n)], True)
-            now = place(late[2], False)
-            if now[0] <= best[0]:
-                best = now
-            elif now[0] > best[0] * SLACK:
-                now = best
+            noise, mid = rng.normal(size=n) * SIG[rep % len(SIG)], rng.random() * best[0]
+            late = place([now[2][i] + (float(noise[i]) if abs(now[2][i] - mid) < WIDE else 0) for i in range(n)], True)
+            new = place(late[2], False)
+            if new[0] <= best[0] + SLACK * (1 - rep / PASSES):
+                now = new
+            if new[0] <= best[0]:
+                best = new
         PLAN["best"] = best
     for i, o in enumerate(ops):
         o["start"], o["end"] = PLAN["best"][1][i], PLAN["best"][2][i]
@@ -663,9 +695,9 @@ def order(ops):
 
 def emit(g, T, ops, Q):
     seq = order(ops)
-    count = {"dve": 0, "act": 0, "pe": 0, "pool": 0}
+    done = {"dve": [], "act": [], "pe": [], "pool": []}
     known = {e: {} for e in Q}
-    total = {}
+    total, last, waited = {}, {}, {}
     nd = 0
     for i in seq:
         o = ops[i]
@@ -675,17 +707,21 @@ def emit(g, T, ops, Q):
             if o["chain"] and ops[j]["eng"] == e:
                 continue
             s, v = ops[j]["sig"]
+            if s in done and known[e].get(s, 0) < v:
+                while v < len(done[s]) and ops[done[s][v]]["end"] + LONG <= o["start"]:
+                    j, v = done[s][v], v + 1
             if need.get(s, (0, 0))[0] < v:
                 need[s] = (v, j)
         for s, (v, j) in sorted(need.items(), key=lambda kv: -ops[kv[1][1]]["end"]):
             if known[e].get(s, 0) < v:
                 Q[e].wait_ge(T.sem[s], v)
+                waited[s] = max(waited.get(s, 0), v)
                 for s2, v2 in ops[j]["clock"].items():
                     known[e][s2] = max(known[e].get(s2, 0), v2)
         clock = dict(known[e])
         if o["kind"] == "c":
-            count[e] += 1
-            o["sig"] = (e, count[e])
+            done[e].append(i)
+            o["sig"] = (e, len(done[e]))
             o["fn"]().then_inc(T.sem[e], 1)
         elif o["kind"] == "dma":
             o["sig"] = ("d%d" % nd, 16)
@@ -694,13 +730,14 @@ def emit(g, T, ops, Q):
         else:
             o["fn"]()
             o["sig"] = (o["sem"][0], o["sem"][2])
-            total[o["sem"][1]] = o["sem"][2]
+            total[o["sem"][1]], last[o["sem"][1]] = o["sem"][2], o["end"]
             clock = {}
         clock[o["sig"][0]] = o["sig"][1]
         o["clock"] = clock
-        total[o["sig"][0]] = o["sig"][1]
-    for s, v in total.items():
-        g.wait_ge(T.sem[s], v)
+        total[o["sig"][0]], last[o["sig"][0]] = o["sig"][1], o["end"]
+    for s, v in sorted(total.items(), key=lambda kv: last[kv[0]]):
+        if waited.get(s, 0) < v:
+            g.wait_ge(T.sem[s], v)
 
 
 def rank_program(g, core, T, topo):

@@ -15,20 +15,35 @@ LO = (0, 64, 128, 192, 256, 256)
 UO = (0, 1728, 3008, 4032, 4800, 5312)
 SO = (0, 320, 576, 768, 896, 960)
 TILES = (0, 3, 4, 5, 1, 2)
-ACT_ROWS = 8
+ACT_ROWS = (8, 6, 6)
 ZG_DVE = ()
-RELU_DVE = ((1, 0), (1, 1), (1, 2), (1, 3))
+RELU_DVE = (2, 4, 4)
 XRUNS = ((0, 128), (128, 128), (256, 128))
 SK_Q = "sp"
-LONG = 1e9
-HOP, LATE, SLOW, MORE, AC = 180, {}, {}, {}, 78
+MOVES = 22000
+GUESS = ((1, 1.56, 3.8, 85, 1.2, (190, 190), 200, 12), (1.4, 1.9, 5.2, 80, 1.6, (165, 165), 0, 10),
+         (1, 1.3, 2.6, 78, 1.5, (150, 150), 900, 10), (1, 1.56, 3.8, 100, 1.0, (60, 350), 300, 0),
+         (1, 1.56, 3.8, 78, 1.3, (250, 80), 0, 0))
+WEIGH = (0.7, 1, 1, 1)
 SMALL_DVE = ()
-WIDE = 6000
+WIDE, STARTS = 3000, 3
+XS_DVE = 3
+SHORT = 17
+AT_DVE = True
+LT_DVE = 2
+OC_SPLIT = True
+TAB = 1160
+MRUNS = ((0, E),)
+NEAR_PE = False
+INORDER = False
+ONE, TWOL, TWOZ = ((0, C),), ((0, 192), (192, C)), ((0, 256), (256, C))
+LANES = ((ONE, ONE, ONE), (ONE, ONE, ONE))
+YRUNS = ((0, 256), (256, 128))
 XH = ((0, 768), (768, 768))
 S0_DMA = True
-ZA = 256
+ZA = (256, 256, 192)
 MT, ZT = (1536, 2304, 4608), 3072
-SIG, SLACK, PASSES, SEED, PLAN = (300, 1000, 3000), 200, 5000, 2, {}
+SIG, SLACK, PASSES, SEED, PLAN = (150, 500, 1500), 300, 4800, 2, {}
 
 
 def _sb(n, d):
@@ -39,24 +54,24 @@ SCRATCH = {
     "ati": _sb(24, I32), "exi": _sb(12, I32), "ub": _sb(512, BF), "vb": _sb(512, BF),
     "wq": _sb(512, CODE), "wp": _sb(512, PLANE), "uq": _sb(128, CODE), "up": _sb(128, PLANE),
     "uq2": _sb(128, CODE), "up2": _sb(128, PLANE), "vq": _sb(128, CODE), "vp": _sb(128, PLANE),
-    "num": _sb(640, F32), "numb": _sb(2176, F32), "t512": _sb(64, F32), "e8192": _sb(E, F32),
+    "num": _sb(1200, F32), "t512": _sb(64, F32), "e8192": _sb(E, F32),
     "pi": _sb(8, I32), "pm": _sb(8, F32), "i16": _sb(2 * C, BF), "dm": _sb(C, BF), "dm4": _sb(C, BF),
-    "a1": _sb(2 * C, BF), "keep": _sb(416, BF), "keep4": _sb(C, BF),
+    "a1": _sb(2 * C, BF), "keep": _sb(C, BF), "own": _sb(416, BF), "keep4": _sb(C, BF),
     "cc": _sb(C, BF), "half": _sb(64, BF), "ones": _sb(512, BF), "c1": _sb(512, BF), "gb": _sb(512, BF),
     "eb": _sb(2048, BF), "zb": _sb(512, BF), "gq": _sb(128, CODE), "gp": _sb(128, PLANE), "eq": _sb(512, CODE),
     "ep": _sb(512, PLANE), "zq0": _sb(256, CODE), "zp0": _sb(256, PLANE),
     "ci": _sb(24, I32), "cf": _sb(504, F32), "cu": _sb(128, U16), "uo": _sb(8, U16),
-    "ksort": _sb(C, F32), "lt": _sb(C * 3, BF), "cs": _sb(C * 3, F32), "nrp": _sb(C, BF),
+    "at1": _sb(C, BF), "lt": _sb(C * 3, BF), "cs": _sb(C * 3, F32), "nrp": _sb(C, BF),
     "ff": _sb(416, F16), "tr": _sb(800, F16), "trs": _sb(800, F16),
     "th": _sb(64, F32), "acc": _sb(64, F32), "su": _sb(128, U16),
-    "xrep": _sb(E, F32), "sig": _sb(E, F32), "sig2": _sb(E, F32), "sigw": _sb(12, F32), "wa": _sb(C, F32),
+    "xrep": _sb(E, F32), "x16": _sb(E, U16), "sig": _sb(E, F32), "sig2": _sb(E, F32), "sigw": _sb(12, F32), "wa": _sb(C, F32),
     "li": _sb(128, I32), "lf": _sb(3 * 320, F32), "lu": _sb(3 * 128, U16), "land": _sb(4 * 48, F32), "ro": _sb(48, I32),
     "crep": _sb(E, F32), "csrt": _sb(E, F32), "pf": _sb(208, F32), "g1": _sb(272, F32),
-    "g2": _sb(2 * 704, F32), "vrep": _sb(E, F32), "vw": _sb(3 * 576, F32), "vk": _sb(C, BF), "vs": _sb(C, F32),
+    "g2": _sb(2 * 704, F32), "vrep": _sb(E, F32), "vw": _sb(3 * 768, F32), "vk": _sb(C, BF), "vs": _sb(C, F32),
     "vg": _sb(768, F32), "lv": _sb(96, F32), "l4": _sb(48, F32), "d0": _sb(3 * 448, BF), "ml": _sb(3 * 132, U16),
-    "bl": _sb(132, F32), "mk": _sb(120, F32), "tab": _sb(3 * 576, F32), "nd": _sb(C, BF), "sp": _sb(72, U16),
+    "bl": _sb(132, F32), "mk": _sb(120, F32), "tab": _sb(3 * TAB, F32), "nd": _sb(C, BF), "sp": _sb(72, U16),
     "ssb": _sb(800, F32), "sa": _sb(C, F32), "yy": _sb(400, F32), "st": _sb(960, F32),
-    "ut": _sb(5824, BF), "utq": _sb(6 * C, CODE), "utp": _sb(6 * C, PLANE), "sg": _sb(16 * C, BF), "rs": _sb(24, F32),
+    "ut": _sb(5824, BF), "utq": _sb(6 * C, CODE), "utp": _sb(6 * C, PLANE), "sg": _sb(20 * 320, BF), "rs": _sb(72, F32),
     "ds": _sb(2 * C, F16), "jr": _sb(3200, F16), "qq": _sb(32, F32), "pw": _sb(96, F32),
     "pu": _sb(144, U16), "w1": _sb(C, F16), "w2": _sb(C, F16), "w3": _sb(C, F16), "w4": _sb(C, F16),
     "srep": _sb(C, F32), "land2": _sb(96, F32), "du": _sb(144, U16),
@@ -67,7 +82,7 @@ SCRATCH = {
     "aq0": _sb(K, CODE), "ap0": _sb(K, PLANE), "aq1": _sb(K, CODE), "ap1": _sb(K, PLANE), "aq2": _sb(K, CODE), "ap2": _sb(K, PLANE),
     "ps": ("psum", [128, 4096], F32),
 }
-SEMAPHORES = ["dve", "act", "pe", "pool", "arr0", "arr1", "arr2", "out0", "out1", "out2"] + ["d%d" % i for i in range(80)]
+SEMAPHORES = ["dve", "act", "pe", "pool", "arr0", "arr1", "arr2", "out0", "out1", "out2"] + ["d%d" % i for i in range(100)]
 TWO = (BF, F16, U16)
 
 
@@ -119,14 +134,14 @@ def build(g, core, T, topo, rank):
         return all(SCRATCH[x[0]][2] in TWO for x in xs)
 
     def add(eng, fn, rd, wr, dur, lat=0, kind="c", chain=False, sem=None, early=0):
-        ops.append({"eng": eng, "fn": fn, "rd": regs(rd), "wr": regs(wr), "dur": dur, "lat": lat, "kind": kind,
+        ops.append({"eng": eng, "fn": fn, "rd": regs(rd), "wr": regs(wr), "cost": dur if isinstance(dur, tuple) else (dur, 0, 0, 0), "lat": lat, "kind": kind,
                     "chain": chain, "sem": sem, "early": early})
 
     def vcost(out, ins, per):
         if out[0] == "ind":
-            return 60 + 3.8 * cnt(out)
+            return (60, 0, cnt(out), 0)
         if ins[0][0] == "ind":
-            return 60 + 1.56 * cnt(out)
+            return (60, cnt(out), 0, 0)
         return max(64, per * cnt(out)) + 10
 
     def cp(out, in_):
@@ -166,8 +181,8 @@ def build(g, core, T, topo, rank):
             if acc is not None:
                 kw["accum_out"] = ap(acc)
             return g.scalar.activation(ap(out), ap(in_), func, **kw)
-        d = 78 + 1.56 * cnt(out) if in_[0] == "ind" else AC + cnt(out)
-        add("act", fn, [in_, bias, scale], [out, acc], d + (24 if acc else 0))
+        d = (78, cnt(out), 0, 0) if in_[0] == "ind" else (cnt(out) + (24 if acc else 0), 0, 0, 1)
+        add("act", fn, [in_, bias, scale], [out, acc], d)
 
     def mm(bank, n, lq, lp, rq, rp, start=True, stop=True):
         o = r("ps", 512 * bank, 512 * bank + n)
@@ -199,34 +214,38 @@ def build(g, core, T, topo, rank):
     def spread(dst, src):
         dma(lambda: ap(dst), lambda: T[src[0]][0:128:16, src[1]:src[2]], [src], [dst])
 
+    def copy(dst, src):
+        dma(lambda: ap(dst), lambda: ap(src), [src], [dst], lat=2400 + cnt(dst))
+
     def xm(a, n, s=1):
         return r("xm", a, a + n, s)
 
-    num, numc = r("num"), r("num", 0, C)
+    num, numc = r("num", 0, 400), r("num", 0, C)
     xt, zt = xm(0, 4 * C), xm(ZT, 4 * C)
     dma(lambda: T.ati[:], lambda: T.at[:], [], [r("ati")])
-    dma(lambda: ap(xt), lambda: T.x[:], [], [xt], eng="act", lat=4100)
     dma(lambda: T.exi[:], lambda: T.ex[:], [], [r("exi")])
-    dma(lambda: T.ub[:], lambda: T.u[:], [], [r("ub")], lat=2800)
-    dma(lambda: ap(xm(MT[0], 768)), lambda: T.e[:], [], [xm(MT[0], 768)], lat=3200)
-    dma(lambda: u8(r("wq")), lambda: T.wc[:], [], [r("wq")], lat=3500)
-    dma(lambda: T.wp[:], lambda: T.ws[:], [], [r("wp")])
-    dma(lambda: T.vb[:], lambda: T.v[:], [], [r("vb")])
+    dma(lambda: T.ub[:], lambda: T.u[:], [], [r("ub")], lat=3200)
+    dma(lambda: ap(xt), lambda: T.x[:], [], [xt], eng="act", lat=4800)
+    dma(lambda: ap(xm(MT[0], 768)), lambda: T.e[:], [xt], [xm(MT[0], 768)], lat=4000)
+    dma(lambda: u8(r("wq")), lambda: T.wc[:], [xt], [r("wq")], lat=5000)
+    dma(lambda: T.wp[:], lambda: T.ws[:], [xt], [r("wp")], lat=5000)
+    dma(lambda: T.vb[:], lambda: T.v[:], [xt], [r("vb")], lat=5000)
     iota(r("pi", 0, 1), [[0, 1]], 0, 1, early=4e4)
     iota(r("ci", 0, 24), [[16, 24]], early=3e4)
     iota(r("t512"), [[512, 64]], early=2e4)
     iota(numc, [[1, C]], early=1e4)
-    iota(r("num", C, 640), [[1, 640 - C]], C)
+    iota(r("num", C, 800), [[1, 800 - C]], C)
+    iota(r("num", 800, 1200), [[1, 400]], 800)
     iota(r("i16", 0, C), [[0, NB], [1, 16]], early=5e3)
-    iota(r("numb"), [[1, 2176]])
     iota(r("e8192"), [[8192, E]])
-    iota(r("ones"), [[0, 512]], 1)
+    mset(r("ones"), 1.0)
+    mset(r("zb"), 0.0)
     ts(r("pi", 2, 3), r("pi", 0, 1), 15, A.bitwise_and)
     cp(r("pm", 0, 1), r("pi", 2, 3))
     pm, keep = r("pm", 0, 1), r("keep", 0, C)
     ts(r("dm"), r("i16", 0, C), pm, A.is_equal)
     ts(r("a1", 0, C), r("dm"), -BIG, A.mult, BIG, A.add)
-    sel(r("keep"), r("ones", 0, 416), [[0, NB + 2], [1, 16]], A.is_gt, 0, 0)
+    sel(r("keep"), r("ones", 0, C), [[0, NB], [1, 16]], A.is_gt, 0, 0)
     ts(r("a1", C, 2 * C), r("dm"), BIG, A.mult, -BIG / 2, A.add)
     sel(r("cc"), r("a1", C, 2 * C), [[0, NB], [1, 16]], A.is_gt, 0, 0, BIG / 2)
     act(r("half"), r("num", 0, 64), scale=BIG / 128, bias=BIG / 2)
@@ -247,23 +266,24 @@ def build(g, core, T, topo, rank):
 
     turn(ga, jw, 24, r("cf", 352, 376), r("cf", 376, 400))
     turn(r("cf", 280, 304), ga, 96, r("cf", 400, 424), r("cf", 424, 448), 4)
-    turn(r("cf", 200, 224), jw, 96, r("cf", 224, 248), r("cf", 480, 504), 4)
     turn(r("cf", 304, 316), j12, 12, r("cf", 448, 460), r("cf", 460, 472))
     turn(r("cf", 192, 196), r("cf", 0, 4), 4, r("cf", 472, 476), r("cf", 476, 480))
     above(r("cf", 72, 84), r("cf", 304, 316), 4)
-    for k in range(2):
-        act(r("cf", 316 + 12 * k, 328 + 12 * k), r("cf", 72, 84), bias=E + k - WHOLE)
-        act(r("cf", 340 + 4 * k, 344 + 4 * k), r("cf", 192, 196), bias=float(E + k))
+    act(r("cf", 316, 328), r("cf", 72, 84), bias=E - WHOLE)
+    act(r("cf", 328, 331), r("cf", 72, 75), bias=E + 4 - WHOLE)
+    act(r("cf", 331, 335), r("cf", 192, 196), bias=float(E))
+    act(r("cf", 335, 336), r("cf", 192, 193), bias=float(E + 16))
     cp(r("cu", 0, 24), ga)
     cp(r("cu", 24, 48), r("cf", 280, 304))
-    cp(r("cu", 48, 92), r("cf", 304, 348))
+    cp(r("cu", 48, 80), r("cf", 304, 336))
     g1216 = r("cu", 48, 60)
-    csrc, c4n = r("cf", 96, 120), r("cf", 84, 96)
-    act(csrc, r("cf", 200, 224), scale=4.0, bias=-1536.0)
+    c4n = r("cf", 84, 96)
     act(r("cf", 120, 132), j12, bias=float(C))
     act(r("cf", 132, 136), r("cf", 0, 4), bias=float(C))
+    act(r("cf", 200, 212), j12, bias=float(C + E))
+    act(r("cf", 212, 216), r("cf", 0, 4), bias=float(C))
     act(r("cf", 24, 48), jw, bias=8.0)
-    iota(r("mk"), [[0, 120]], 1)
+    iota(r("mk", 0, 20), [[0, 20]], 1)
     act(r("cf", 48, 72), jw, bias=4.0)
     above(r("cf", 136, 148), j12, 4)
     act(c4n, r("cf", 136, 148), bias=-WHOLE)
@@ -273,10 +293,8 @@ def build(g, core, T, topo, rank):
     sel(r("gb"), r("c1"), [[16, 8], [0, 64]], A.is_ge, 15, -1)
     quant(r("gq"), r("gp"), r("gb"))
     for k in range(6):
-        n = 4 * (max(64 * k, 0) + 48 - LO[k])
-        iota(r("ut", UO[k], UO[k] + n), [[0, n]])
-    iota(r("ut", 1536, 1536 + 192), [[0, 192]])
-    iota(r("zb"), [[0, 512]])
+        copy(r("ut", UO[k], UO[k] + 4 * (64 * k + 48 - LO[k])), r("zb", 0, 4 * (64 * k + 48 - LO[k])))
+    copy(r("ut", 1536, 1536 + 192), r("zb", 0, 192))
     quant(r("zq0", 0, 128), r("zp0", 0, 128), r("zb"))
     dma(lambda: u8(r("zq0", 128, 256)), lambda: u8(r("zq0", 0, 128)), [r("zq0", 0, 128)], [r("zq0", 128, 256)])
     dma(lambda: T.zp0[:, 128:256], lambda: T.zp0[:, 0:128], [r("zp0", 0, 128)], [r("zp0", 128, 256)])
@@ -285,9 +303,10 @@ def build(g, core, T, topo, rank):
         dma(lambda dq=dq, w=LO[k]: u8(dq), lambda w=LO[k]: u8(r("zq0", 0, w)), [r("zq0")], [dq])
         dma(lambda dp=dp: ap(dp), lambda w=LO[k]: ap(r("zp0", 0, w)), [r("zp0")], [dp])
     for t in range(ROUNDS):
-        iota(r("tab", 576 * t, 576 * t + 576), [[0, 576]])
-        iota(r("vw", 576 * t, 576 * t + 576), [[0, 576]])
-        iota(r("d0", 448 * t + C, 448 * t + 448), [[0, 64]])
+        iota(r("tab", TAB * t, TAB * t + TAB), [[0, TAB]])
+        iota(r("vw", 768 * t, 768 * t + 768), [[0, 768]], 8)
+        if t:
+            copy(r("d0", 448 * t + C, 448 * t + 448), r("zb", 0, 64))
     for b in range(4):
         sel(r("eb", 512 * b, 512 * b + 512), r("ones"), [[-1, 512]], A.is_equal, b, 4)
     iota(r("rr", 4 * C, 4 * C + 768), [[0, 768]])
@@ -295,6 +314,7 @@ def build(g, core, T, topo, rank):
     act(r("ssb", 0, 8), r("ones", 0, 8), scale=-BIG)
     act(r("yy", C, 400), r("ones", 0, 16), scale=BIG)
     iota(r("qq", 0, 2), [[0, 2]])
+    iota(r("rs"), [[0, 72]])
     iota(r("bl", 0, 72), [[0, 72]])
     iota(r("pf", 0, 2), [[0, 2]])
     iota(r("acc", 3, 4), [[0, 1]], -C)
@@ -305,7 +325,7 @@ def build(g, core, T, topo, rank):
     iota(r("i16", C, 2 * C), [[0, C // 4], [1, 4]])
     ts(r("dm4"), r("i16", C, 2 * C), r("pm", 5, 6), A.is_equal)
     sel(r("keep4"), r("ones", 0, C), [[0, C // 4], [1, 4]], A.is_gt, 0, 0)
-    iota(r("g1"), [[0, 272]], C)
+    iota(r("g1", 256, 272), [[0, 16]], C)
     quant(r("uq"), r("up"), r("ub"))
     add("dve", lambda: g.vector.tensor_copy(T.uq2[:].bitcast(dt.uint32), T.uq[:].bitcast(dt.uint32).indirect(T.uo[:, 0:8])),
         [r("uq"), r("uo")], [r("uq2")], 260)
@@ -318,42 +338,48 @@ def build(g, core, T, topo, rank):
     act(r("nrp"), ind(numc, at16))
     act(r("th", 0, 3), r("cf", 0, 3), scale=-1.0, bias=0.5)
     for m in range(3):
-        act(r("g2", C * m, C * m + C), r("nrp"), F.Sign, bias=r("th", m, m + 1), acc=r("acc", m, m + 1))
+        if AT_DVE:
+            ts(r("lt", C * m, C * m + C), r("nrp"), r("cf", m, m + 1), A.is_lt, -2.0, A.mult)
+            scan(r("tr", E * m, E * m + E), r("lt", C * m, C * m + E), r("lt", C * m + E, C * m + C), A.add, A.add, float(C))
+        else:
+            act(r("g2", C * m, C * m + C), r("nrp"), F.Sign, bias=r("th", m, m + 1), acc=r("acc", m, m + 1))
+    if AT_DVE:
+        cp(r("acc", 0, 3), r("tr", E - 1, 3 * E, E))
     ts(st16, r("acc", 0, 4), -0.5, A.mult, C / 2, A.add)
-    for q in range(3):
-        act(r("th", 4 + q, 5 + q), r("acc", q, q + 1), scale=-0.5, bias=C / 2 - 1)
-        ts(r("lt", C * q, C * q + C), r("nrp"), r("cf", q, q + 1), A.is_equal)
-        scan(r("cs", C * q, C * q + C), r("ones", 0, C), r("lt", C * q, C * q + C), A.mult, A.add, r("th", 4 + q, 5 + q))
+    act(r("th", 4, 7), r("cf", 0, 3), scale=8.0, bias=8.0)
+    tt(r("th", 4, 7), r("acc", 0, 3), r("th", 4, 7), A.subtract)
     ts(r("li", 96, 120), r("ati"), 4, A.arith_shift_right)
-    ts(r("th", 8, 32), r("li", 96, 120), float(C), A.mult)
-    tt(r("th", 8, 32), r("th", 8, 32), jw, A.add)
-    cp(r("pu", 0, 24), r("th", 8, 32))
-    act(r("vk"), ind(r("dm", 0, 64), at16))
+    act(r("at1"), ind(r("dm", 0, 64), at16))
     mset(r("ff", 0, 16), 0.0)
     mset(r("ff", 400, 416), 0.0)
-    tt(r("ff", 16, 400), ind(r("cs"), r("pu", 0, 24)), r("vk"), A.mult)
-    for o, a, n in ((0, 16, C), (C, 0, 416)):
-        x, y = r("tr", o, o + n), r("ff", a, a + n)
-        add("dve", lambda x=x, y=y: g.vector.transpose(ap(x), ap(y)), [y], [x], 10 + n / 2)
-        scan(r("trs", o, o + n), r("keep", 0, n), x, A.mult, A.add)
     ts(r("pi", 4, 5), r("pi", 0, 1), 4, A.arith_shift_right, 1, A.bitwise_and)
     cp(r("pm", 2, 3), r("pi", 4, 5))
-    ts(r("pm", 4, 5), r("pm", 2, 3), -1.0, A.mult, 1.0, A.add)
-    ts(r("pw", 0, 24, 2), r("trs", 15, C, 32), r("pm", 4, 5), A.mult)
-    ts(r("pw", 1, 24, 2), r("trs", C + 47, 800, 32), r("pm", 4, 5), A.mult)
-    ts(r("pw", 24, 48, 2), r("trs", C + 31, 768, 32), r("pm", 2, 3), A.mult)
-    ts(r("pw", 25, 48, 2), r("trs", 31, C, 32), r("pm", 2, 3), A.mult)
-    tt(r("pw", 48, 72), r("pw", 0, 24), r("pw", 24, 48), A.add)
-    cp(rk16, r("pw", 48, 72))
-    cp(ind(r("ksort"), rk16), numc)
-    if S0_DMA:
-        act(r("srep"), ind(r("ksort"), r("cu", 0, 24)))
-        spread(r("lv", 72, 96), r("srep"))
-        cp(s016, r("lv", 72, 96))
-    else:
-        tt(r("w1"), r("ksort"), r("dm"), A.mult)
-        scan(r("w2"), keep, r("w1"), A.mult, A.add)
-        cp(s016, r("w2", 15, C, 16))
+    iota(r("own"), [[0, 13], [1, 2], [0, 16]])
+    ts(r("own"), r("own"), r("pm", 2, 3), A.is_equal)
+
+    def by_node():
+        cp(rk16, r("pw", 48, 72))
+        cp(ind(r("nd"), rk16), r("nrp"))
+        for q in range(3):
+            if q < LT_DVE:
+                ts(r("lt", C * q, C * q + C), r("nd"), r("cf", q, q + 1), A.is_equal, -2.0, A.mult)
+                scan(r("cs", q, 3 * C, 3), r("ones", 0, C), r("lt", C * q, C * q + C), A.mult, A.add, r("th", 4 + q, 5 + q))
+            else:
+                act(r("lt", C * q, C * q + C), r("nd"), F.Abs, scale=-1.0, bias=r("cf", q, q + 1))
+                act(r("lt", C * q, C * q + C), r("lt", C * q, C * q + C), F.Relu, scale=-2.0, bias=2.0)
+                scan(r("cs", q, 3 * C, 3), r("zb", 0, C), r("lt", C * q, C * q + C), A.add, A.subtract, r("th", 4 + q, 5 + q))
+        act(r("th", 40, 64), r("pw", 48, 72), scale=3.0)
+        tt(r("th", 8, 32), r("li", 96, 120), r("th", 40, 64), A.add)
+        cp(s016, r("th", 8, 32))
+        tt(r("ff", 16, 400), ind(r("cs"), s016), r("at1"), A.mult)
+        for o, a, n in ((0, 16, C), (C, 0, 416)):
+            x, y = r("tr", o, o + n), r("ff", a, a + n)
+            add("dve", lambda x=x, y=y: g.vector.transpose(ap(x), ap(y)), [y], [x], 10 + n / 2)
+            scan(r("trs", o, o + n), x, r("own", 0, n), A.add, A.mult)
+        tt(r("pw", 72, 96, 2), r("trs", 15, C, 32), r("trs", C + 31, 768, 32), A.add)
+        tt(r("pw", 73, 96, 2), r("trs", 31, C, 32), r("trs", C + 47, 800, 32), A.add)
+        ts(r("pu", 0, 24), r("pw", 72, 96), -1.0, A.mult, C - 2.0, A.add)
+
     cp(ex16, r("exi"))
     tt(r("xrep"), ind(r("t512"), ex16), r("num", 0, E), A.add)
     ts(r("cf", 160, 172), r("exi"), 512.0, A.mult)
@@ -361,9 +387,15 @@ def build(g, core, T, topo, rank):
     act(r("cf", 172, 176), r("cf", 0, 4), scale=512.0)
     act(r("cf", 176, 192), r("cf", 160, 176), scale=-1.0, bias=0.5)
     iota(r("acc", 47, 48), [[0, 1]], -E)
-    for m in range(15):
+    for m in range(XS_DVE, 15):
         act(r("sg", C * m, C * m + E), r("xrep"), F.Sign, bias=r("cf", 176 + m, 177 + m), acc=r("acc", 32 + m, 33 + m))
-    ts(ln16, r("acc", 32, 48), -0.5, A.mult, E / 2, A.add)
+    ts(r("su", 88 + XS_DVE, 104), r("acc", 32 + XS_DVE, 48), -0.5, A.mult, E / 2, A.add)
+    if XS_DVE:
+        cp(r("x16"), r("xrep"))
+        for m in range(XS_DVE):
+            ts(r("sg", C * m, C * m + E), r("x16"), r("cf", 160 + m, 161 + m), A.is_lt)
+            scan(r("jr", 160 * m + 64, 160 * m + 160), r("sg", C * m, C * m + 96), r("sg", C * m + 96, C * m + E), A.add, A.add)
+        cp(r("su", 88, 88 + XS_DVE), r("jr", 159, 160 * XS_DVE, 160))
     cp(ind(r("sig"), r("su", 88, 100)), r("num", 0, E))
     act(r("sig2"), ind(r("sig"), g1216))
     spread(r("sigw"), r("sig2"))
@@ -374,11 +406,11 @@ def build(g, core, T, topo, rank):
 
     def expand(i):
         o = 704 * (i % 2)
-        a, b = {0: (12, 36), 3: (0, 12)}.get(i, (0, 44))
+        a, b = {0: (12, 27), 3: (0, 12)}.get(i, (0, 32))
         act(r("g2", o + 16 * a, o + 16 * b), ind(r("g1"), r("cu", 48 + a, 48 + b)))
-        for x, y, n in ((0, 0, 12), (12, 20, 12), (24, 32, 12), (36, 12, 4), (40, 16, 4)):
-            if a <= x < b:
-                spread(land(i, y, n), r("g2", o + 16 * x, o + 16 * (x + n)))
+        for x, y, n in ((0, 0, 12), (192, 20, 12), (240, 32, 12), (432, 12, 4), (436, 16, 4)):
+            if 16 * a <= x < 16 * b:
+                spread(land(i, y, n), r("g2", o + x, o + x + 16 * n))
 
     def lf(t, a, n, s=1):
         return r("lf", 320 * t + a, 320 * t + a + n, s)
@@ -422,18 +454,18 @@ def build(g, core, T, topo, rank):
 
     def exits(t):
         st, en, rot, nxt = land(t, 20, 12), land(t, 32, 12), r("ro", 12 * t, 12 * t + 12), r("ro", 12 * t + 12, 12 * t + 24)
-        w, u, c4, mp = lf(t, 192, 12), r("li", 12 * t, 12 * t + 12), lf(t, 204, 12), lf(t, 220, 12)
+        w, u, mp, c4 = lf(t, 220, 12), r("li", 12 * t, 12 * t + 12), lf(t, 192, 12), lf(t, 204, 12)
         tt(w, st, rot, A.subtract)
         tt(u, en, w, A.subtract)
         ts(nxt, u, 3, A.bitwise_and)
         tt(c4, u, nxt, A.subtract)
-        ts(lu(t, 24, 12), c4, 0.25, A.mult)
         tt(mp, w, c4n, A.add)
+        ts(lu(t, 0, 24), lf(t, 192, 24), 2.0, A.mult)
         if t == 2:
             tt(lf(t, 232, 12), mp, c4, A.add)
-        cp(lu(t, 0, 24 if t == 2 else 12), lf(t, 220, 24 if t == 2 else 12))
-        cp(ind(r("tab", 576 * t, 576 * t + 576), lu(t, 0, 12)), r("num", C, C + E))
-        act(r("crep"), ind(numc, lu(t, 24, 12)))
+            ts(lu(t, 24, 12), lf(t, 232, 12), 2.0, A.mult)
+        cp(ind(r("tab", TAB * t + 8, TAB * t + TAB), lu(t, 0, 12)), r("num", C, C + E))
+        act(r("crep"), ind(r("num", 0, 800), lu(t, 12, 12)), scale=0.125)
         act(r("csrt"), ind(r("crep"), sg16))
         scan(r("pf", 1, 1 + E), r("ones", 0, E), r("csrt"), A.mult, A.add)
         act(r("g1", 0, 256 if t < 2 else E), ind(r("pf", 0, 1 + E), ln16 if t < 2 else r("su", 88, 100)))
@@ -443,29 +475,22 @@ def build(g, core, T, topo, rank):
             tt(lf(t, 216, 4), land(t + 1, 16, 4), land(t + 1, 12, 4), A.subtract)
         spare, b4 = lf(t, 244, n), lf(t, 260, 12)
         act(spare, lf(t, 204, n), scale=-1000.0)
-        tt(spare, spare, r("cf", 120, 120 + n), A.add)
+        tt(spare, spare, r("cf", 200, 216) if t == 1 else r("cf", 120, 120 + n), A.add)
         tt(lf(t, 284, n), spare, land(t + 1, 0, n), A.max)
-        act(b4, land(t + 1, 0, 12), scale=4.0, bias=-1540.0)
-        tt(lf(t, 272, 12), mp, b4, A.subtract)
-        cp(lu(t, 36, 12 + n), lf(t, 272, 12 + n))
+        cp(lu(t, 48, n), lf(t, 284, n))
         if t < 2:
             starts(t + 1, lu(t, 60, 3))
-            tt(b4, b4, c4, A.add)
-            act(lf(t, 300, 12), lf(t, 244, 12), scale=4.0, bias=float(4 + 4 * E * t - 1540))
-            tt(b4, b4, lf(t, 300, 12), A.max)
-            if "l4" in SMALL_DVE:
-                for b in range(4):
-                    ts(lu(t, 64 + 12 * b, 12), b4, float(1536 + b), A.add)
-            else:
-                for b in range(4):
-                    act(r("l4", 12 * b, 12 * b + 12), b4, bias=float(1536 + b))
-                cp(lu(t, 64, 48), r("l4", 0, 48))
-            act(r("vrep"), ind(r("numb"), lu(t, 36, 12)))
+            act(b4, c4, F.Relu, scale=0.25, bias=-1.0)
+            tt(b4, b4, lf(t, 284, 12), A.add)
+            for b in range(4):
+                act(r("l4", 12 * b, 12 * b + 12), b4, scale=4.0, bias=float(b))
+            cp(lu(t, 64, 48), r("l4", 0, 48))
+            act(r("vrep"), ind(r("num", 16, 1200), lu(t, 0, 12)))
         else:
-            tt(r("vrep"), ind(r("numb"), lu(t, 36, 12)), r("e8192"), A.add)
-        cp(ind(r("vw", 576 * t, 576 * t + 576), lu(t, 48, 12)), r("vrep"))
-        act(r("vk"), r("vw", 576 * t, 576 * t + C), F.Relu, bias=1.0, scale=-1.0)
-        scan(r("vs"), r("vk"), r("vw", 576 * t, 576 * t + C), A.mult, A.add)
+            tt(r("vrep"), ind(r("num", 16, 1200), lu(t, 0, 12)), r("e8192"), A.add)
+        cp(ind(r("vw", 768 * t, 768 * t + 768), lu(t, 48, 12)), r("vrep"))
+        act(r("vk"), r("vw", 768 * t, 768 * t + C), F.Relu, bias=9.0, scale=-1.0)
+        scan(r("vs"), r("vk"), r("vw", 768 * t, 768 * t + C), A.mult, A.add)
         act(r("vg", C, 2 * C), ind(r("vs"), r("cu", 24, 48)))
         src = r("lv", 24 * t, 24 * t + 24)
         spread(src, r("vg", C, 2 * C))
@@ -476,18 +501,13 @@ def build(g, core, T, topo, rank):
             cp(r("li", 40, 64), src)
             src = r("li", 64, 88)
             ts(src, r("li", 40, 64), 8191, A.bitwise_and)
-        tt(r("lv", 72, 96), src, csrc, A.add)
-        cp(r("sp", 24 * t, 24 * t + 24), r("lv", 72, 96))
+        cp(r("sp", 24 * t, 24 * t + 24), src)
 
     act(r("g1", E, 256), ind(num, st16))
+    copy(r("g1", 0, E), r("num", 0, E))
     expand(0)
-    act(r("th", 32, 35), r("th", 4, 7), bias=1.0)
-    tt(r("th", 36, 39), r("th", 4, 7), r("cs", C - 1, 3 * C, C), A.subtract)
-    act(r("th", 36, 39), r("th", 36, 39), scale=1000.0)
-    tt(r("th", 36, 39), r("th", 36, 39), r("cf", 120, 123), A.add)
-    tt(r("th", 36, 39), r("th", 36, 39), r("th", 32, 35), A.max)
-    cp(r("su", 116, 119), r("th", 36, 39))
-    starts(0, r("su", 116, 119))
+    ts(ml(0, 0, 24), r("ci", 0, 24), 15.0, A.add)
+    iota(r("mk", 20, 40), [[0, 20]], -1)
 
     def plane(name, b, a, n):
         return r(name, 576 * b + a, 576 * b + a + n)
@@ -500,20 +520,16 @@ def build(g, core, T, topo, rank):
 
     for t in range(ROUNDS):
         exits(t)
-        tab = r("tab", 576 * t, 576 * t + 576)
+        rows = ACT_ROWS[t]
+        tab, before = r("tab", TAB * t + 8, TAB * t + TAB), r("tab", TAB * t, TAB * t + TAB)
         quant(r("xq"), r("xp"), xt)
         mm(5, C, r("uq2"), r("up2"), r("xq"), r("xp"))
-        if t > 0:
-            mm(4, C, r("uq2"), r("up2"), r("xq"), r("xp"))
-            act(r("ssb", 8, 8 + C), ps(5, C))
-            sv = ps(4, C)
-        else:
-            act(r("ssb", 400, 400 + C), ps(5, C))
-            sv = ind(r("ssb", 400, 400 + C), s016)
-            act(r("ssb", 8, 8 + C), sv)
+        mm(4, C, r("uq2"), r("up2"), r("xq"), r("xp"))
+        act(r("ssb", 8, 8 + C), ps(5, C))
+        sv = ps(4, C)
         tt(r("sa"), sv, r("a1", 0, C), A.add)
-        scan(r("yy", 0, C), r("d0", 448 * t, 448 * t + C), r("sa"), A.max, A.min)
-        for a, b in ((0, 1), (1, 2), (2, 5)):
+        scan(r("yy", 0, C), r("d0", 448 * t, 448 * t + C) if t else r("cc"), r("sa"), A.max, A.min)
+        for a, b in ((0, 1), (1, 2), (2, 5)) if t else ():
             act(r("st", SO[a], SO[b]), ind(r("ssb", 0, 8 + C), ml(t, 72 + SO[a] // 16, (SO[b] - SO[a]) // 16)))
         for a, n in XH:
             x, y = r("xmh", a, a + n), r("xmh", 2304 + a, 2304 + a + n)
@@ -521,60 +537,73 @@ def build(g, core, T, topo, rank):
             dma(lambda y=y: ap(y), lambda x=x: ap(x), [x], [y], lat=2900)
         tt(ut(0, 0, 0, C), sv, r("yy", 0, C), A.is_gt)
         for d in range(1, 4):
-            tt(ut(0, d, 16 * d, C - 16 * d), ind(r("yy"), ml(t, 24 * d - 24, 24 - d)), r("ssb", 8 + 16 * d, 8 + C), A.is_lt)
-        scan(r("ds", 0, C), ut(0, 0, 0, C), ut(0, 1, 16, C), A.add, A.add)
-        scan(r("ds", C, 2 * C), ut(0, 2, 32, C), ut(0, 3, 48, C), A.add, A.add)
-        tt(r("qq", 1, 25), r("ds", 15, C, 16), r("ds", C + 15, 2 * C, 16), A.add)
-        tt(r("pw", 0, 24), lf(t, 72, 24), r("qq", 1, 25), A.add)
-        tt(r("pw", 0, 24), r("pw", 0, 24), r("qq", 0, 24), A.subtract)
+            tt(ut(0, d, 16 * d, C - 16 * d), ind(r("yy"), ml(t, 24 * d - 24 if t else 0, 24 - d)), r("ssb", 8 + 16 * d, 8 + C), A.is_lt)
+        if not NEAR_PE:
+            scan(r("ds", 0, C), ut(0, 0, 0, C), ut(0, 1, 16, C), A.add, A.add)
+            scan(r("ds", C, 2 * C), ut(0, 2, 32, C), ut(0, 3, 48, C), A.add, A.add)
+            tt(r("qq", 1, 25), r("ds", 15, C, 16), r("ds", C + 15, 2 * C, 16), A.add)
+            tt(r("pw", 0, 24), lf(t, 72, 24) if t else jw, r("qq", 1, 25), A.add)
+            tt(r("pw", 0, 24), r("pw", 0, 24), r("qq", 0, 24), A.subtract)
         for k in TILES:
             for s in range(4 if k else 0):
                 m = 4 * (k - 1) + s
                 a = 16 * (m + 4)
                 n = C - a
-                src, y = r("st", SO[k - 1] + 16 * s, SO[k]), r("yy", 16 * m + 15, 16 * m + 16)
-                if m < ACT_ROWS:
-                    act(r("sg", C * m, C * m + n), src, F.Sign, bias=y, scale=-1.0)
-                    act(ut(k, s, a, n), r("sg", C * m, C * m + n), F.Relu, scale=r("mk", 40 * t + 20 + m, 40 * t + 21 + m),
-                        acc=r("rs", m, m + 1))
+                src = r("st", SO[k - 1] + 16 * s, SO[k]) if t else r("ssb", 8 + a, 8 + C)
+                y = r("yy", 16 * m + 15, 16 * m + 16)
+                if m < rows or m >= SHORT:
+                    act(r("sg", 320 * m, 320 * m + n), src, F.Sign, bias=y, scale=-1.0)
+                    act(ut(k, s, a, n), r("sg", 320 * m, 320 * m + n), F.Relu, scale=r("mk", 40 * t + 20 + m, 40 * t + 21 + m),
+                        acc=r("rs", 24 * t + m, 24 * t + m + 1))
                 else:
                     ts(ut(k, s, a, n), src, y, A.is_gt, r("mk", 40 * t + m, 40 * t + m + 1), A.mult)
                     scan(r("jr", 160 * m + 160 - n // 2, 160 * m + 160), ut(k, s, a, n // 2), ut(k, s, a + n // 2, n // 2),
                          A.add, A.add)
             quant(r("utq", C * k + LO[k], C * k + C), r("utp", C * k + LO[k], C * k + C), r("ut", UO[k], UO[k] + 4 * (C - LO[k])))
-            mm(6, C, r("gq"), r("gp"), r("utq", C * k, C * k + C), r("utp", C * k, C * k + C), k == TILES[0], k == TILES[-1])
-        tt(r("pw", ACT_ROWS, 20), r("pw", ACT_ROWS, 20), r("jr", 160 * ACT_ROWS + 159, 3200, 160), A.add)
-        tt(r("pw", 0, ACT_ROWS), r("pw", 0, ACT_ROWS), r("rs", 0, ACT_ROWS), A.add)
-        tt(r("w1"), ps(6, C), r("dm"), A.mult)
-        scan(r("w2"), keep, r("w1"), A.mult, A.add)
-        tt(r("pw", 48, 72), r("pw", 0, 24), r("w2", 15, C, 16), A.subtract)
-        cp(r("pu", 0, 24), r("pw", 48, 72))
-        cp(ind(tab, r("pu", 0, 24)), numc if t > 0 else r("ksort"))
-        ts(r("pu", 24, 48), r("pw", 48, 72), -4.0, A.add)
-        if t > 0:
-            tt(r("w3"), ind(tab, r("pu", 24, 48)), r("dm4"), A.mult)
-        else:
-            cp(r("wa"), ind(tab, r("pu", 24, 48)))
-            tt(r("w3"), ind(r("wa"), rk16), r("dm4"), A.mult)
-        scan(r("w4"), r("keep4"), r("w3"), A.mult, A.add)
-        ts(r("pu", 48, 144), r("w4", 3, C, 4), 4.0, A.mult, r("pm", 6, 7), A.add)
-        act(r("srep"), ind(tab, r("sp", 24 * t, 24 * t + 24)))
+            for h, (a, b) in enumerate(LANES[0][t]):
+                mine = [x for x in TILES if LO[x] < b]
+                if k in mine:
+                    mm(6 + h, b - a, r("gq"), r("gp"), r("utq", C * k + a, C * k + b), r("utp", C * k + a, C * k + b),
+                       k == mine[0], k == mine[-1])
+            if k == 0 and NEAR_PE:
+                for d in range(4):
+                    mm(7, C, r("eq", 128 * d, 128 * d + 128), r("ep", 128 * d, 128 * d + 128), r("utq", 16 * d, 16 * d + C),
+                       r("utp", 16 * d, 16 * d + C), d == 0, d == 3)
+                scan(r("ds", 0, C), keep, ps(7, C), A.mult, A.add)
+                tt(r("pw", 0, 24), lf(t, 72, 24), r("ds", 15, C, 16), A.add)
+        tt(r("pw", rows, SHORT), r("pw", rows, SHORT), r("jr", 160 * rows + 159, 160 * SHORT, 160), A.add)
+        tt(r("pw", 0, 20), r("pw", 0, 20), r("rs", 24 * t, 24 * t + 20), A.add)
+        for h, (a, b) in enumerate(LANES[0][t]):
+            tt(r("w1", a, b), ps(6 + h, b - a), r("dm", a, b), A.mult)
+            scan(r("w2", a, b), r("keep", a, b), r("w1", a, b), A.mult, A.add)
+            tt(r("pw", 48 + a // 16, 48 + b // 16), r("pw", a // 16, b // 16), r("w2", a + 15, b, 16), A.subtract)
+            if t:
+                ts(r("pu", a // 16, b // 16), r("pw", 48 + a // 16, 48 + b // 16), 2.0, A.mult)
+                cp(ind(tab, r("pu", a // 16, b // 16)), r("num", a, b))
+        if t == 0:
+            by_node()
+            cp(ind(tab, r("pu", 0, 24)), numc)
+        for a, b in LANES[1][t]:
+            tt(r("w3", a, b), ind(before, r("pu", a // 16, b // 16)), r("dm4", a, b), A.mult)
+            scan(r("w4", a, b), r("keep4", a, b), r("w3", a, b), A.mult, A.add)
+            ts(r("pu", 48 + a // 4, 48 + b // 4), r("w4", a + 3, b, 4), 4.0, A.mult, r("pm", 6, 7), A.add)
+        act(r("srep"), ind(before, r("sp", 24 * t, 24 * t + 24)))
         for b in range(4):
             dma(lambda b=b: T.land2[b:128:4, :], lambda: T.srep[0:128:16, :], [r("srep")], [("land2", b, 96, 4)],
                 eng="sp" if b % 2 else SK_Q)
         ts(r("du", 0, 96), r("land2"), 4.0, A.mult, r("pm", 6, 7), A.add)
         if t == 2:
-            tt(r("w1", 0, E), ind(tab, lu(t, 12, 12)), r("dm4", 0, E), A.mult)
+            tt(r("w1", 0, E), ind(tab, lu(t, 24, 12)), r("dm4", 0, E), A.mult)
             scan(r("w2", 0, E), r("keep4", 0, E), r("w1", 0, E), A.mult, A.add)
             ts(r("du", 96, 144), r("w2", 3, E, 4), 4.0, A.mult, r("pm", 6, 7), A.add)
-        for h, (a, n) in enumerate(((0, ZA), (ZA, C - ZA))):
+        for h, (a, n) in enumerate(((0, ZA[t]), (ZA[t], C - ZA[t]))):
             tt(xm(ZT + 4 * a, 4 * n), ind(r("xmh", 0, 2304), r("pu", 48 + a // 4, 48 + (a + n) // 4)),
                r("xmh", 2304 + 4 * a, 2304 + 4 * (a + n)), A.add)
             quant(r("zq", a, a + n), r("zp", a, a + n), xm(ZT + 4 * a, 4 * n))
             for b in range(4):
                 mm(4 * h + b, n, r("wq", 128 * b, 128 * b + 128), r("wp", 128 * b, 128 * b + 128), r("zq", a, a + n),
                    r("zp", a, a + n))
-                if (h, b) in RELU_DVE:
+                if h == 1 and b < RELU_DVE[t]:
                     ts(r("rr", 4 * a + b, 4 * (a + n), 4), ps(4 * h + b, n), 0.0, A.max, 0.03125, A.mult)
                 else:
                     act(r("rr", 4 * a + b, 4 * (a + n), 4), ps(4 * h + b, n), F.Relu, scale=0.03125)
@@ -592,105 +621,167 @@ def build(g, core, T, topo, rank):
             (cp if h in ZG_DVE else act)(zg, ind(zt, sk))
             tt(xm(4 * a, 4 * n), ind(r("rr", 0, 4 * C), sk), zg, A.add)
         if t < 2:
-            for a, n in ((0, K), (K, E - K)):
+            for a, n in MRUNS:
                 for b in range(4):
                     act(mem(a, n, b, 4), ind(xm(0, MT[t] + 768), lu(t, 64 + 12 * b + a // 16, n // 16)))
         bq, bp, aq, apl = r("bq%d" % t), r("bp%d" % t), r("aq%d" % t), r("ap%d" % t)
         quant(bq, bp, mem(0, K))
+        if t == 2 and OC_SPLIT:
+            quant(r("zq", 0, K), r("zp", 0, K), mem(E - K, K))
         peer = T.cores[rank ^ STEP[t]]
         rid, pid = topo.addr(peer)[:2]
         eng = topo.engines(core, peer)
-        half = len(eng) // 2
-        m1, m2 = sum(1 << e for e in eng[:half]), sum(1 << e for e in eng[half:])
 
-        def send(t=t, bq=bq, bp=bp, aq=aq, apl=apl, rid=rid, pid=pid, m1=m1, m2=m2):
-            g.remote_dma(u8(aq), u8(bq), T.sem["arr%d" % t], T.sem["out%d" % t], pid, rid, m1)
-            g.remote_dma(ap(apl), ap(bp), T.sem["arr%d" % t], T.sem["out%d" % t], pid, rid, m2)
-        add("pool", send, [bq, bp], [aq, apl], 600, lat=3600, kind="remote", sem=("arr%d" % t, "out%d" % t, len(eng)))
+        def send(t=t, bq=bq, bp=bp, aq=aq, apl=apl, rid=rid, pid=pid, m=topo.mask(core, peer)):
+            g.remote_dma(u8(aq), u8(bq), T.sem["arr%d" % t], T.sem["out%d" % t], pid, rid, m)
+            g.remote_dma(ap(apl), ap(bp), T.sem["arr%d" % t], T.sem["out%d" % t], pid, rid, m)
+        add("pool", send, [bq, bp], [aq, apl], 600, lat=3600, kind="remote", sem=("arr%d" % t, "out%d" % t, 2 * len(eng)))
         for b in range(4):
             mm(b, K, r("eq", 128 * b, 128 * b + 128), r("ep", 128 * b, 128 * b + 128), aq, apl)
             (cp if t == 2 and b % 2 else act)(mem(0, K, b, 4), ps(b, K))
         if t < 2:
-            for a, n in ((0, K), (K, E - K)):
+            for a, n in MRUNS:
                 act(r("xmh", 4 * (C + a), 4 * (C + a + n)), mem(a, n), scale=0.5)
-    quant(r("xq"), r("xp"), xt)
-    mm(4, C, r("vq"), r("vp"), r("xq"), r("xp"))
-    act(r("ysb"), ps(4, C))
-    dma(lambda: T.y[:], lambda: T.ysb[:], [r("ysb")], [], lat=3200)
-    quant(r("mq"), r("mp"), r("mt"))
-    dma(lambda: T.oc[:], lambda: u8(r("mq")), [r("mq")], [], lat=2700)
-    for k in range(4):
-        dma(lambda k=k: T.osc[4 * k:4 * k + 4, :], lambda k=k: T.mp[32 * k:32 * k + 4, :], [r("mp")], [],
-            eng="sp" if k < 2 else "act")
+    for h, (a, n) in enumerate(YRUNS):
+        quant(r("xq", a, a + n), r("xp", a, a + n), xm(4 * a, 4 * n))
+        mm(4 + h, n, r("vq"), r("vp"), r("xq", a, a + n), r("xp", a, a + n))
+        act(r("ysb", a, a + n), ps(4 + h, n))
+        dma(lambda a=a, n=n: T.y[:, a:a + n], lambda a=a, n=n: T.ysb[:, a:a + n], [r("ysb", a, a + n)], [], lat=2200 + 2.6 * n)
+    def store(q, p, a, b, o):
+        dma(lambda: T.oc[:, 4 * a:4 * b], lambda: u8(r(q, a - o, b - o)), [r(q)], [], lat=2200 + 2.6 * (b - a))
+        for k in range(4):
+            dma(lambda k=k: T.osc[4 * k:4 * k + 4, a:b], lambda k=k: T[p][32 * k:32 * k + 4, a - o:b - o], [r(p)], [],
+                eng="sp" if k < 2 else "act", lat=2300)
+
+    if OC_SPLIT:
+        store("zq", "zp", K, E, E - K)
+        quant(r("mq", 0, K), r("mp", 0, K), r("mt", 0, 4 * K))
+        store("mq", "mp", 0, K, 0)
+    else:
+        quant(r("mq"), r("mp"), r("mt"))
+        store("mq", "mp", 0, E, 0)
     return ops, Q
 
 
 def order(ops):
-    hop = HOP
-    for o in ops:
-        o["lat"] += LATE.get(o["kind"], 0)
-        o["dur"] = o["dur"] * SLOW.get(o["eng"], 1) + MORE.get(o["eng"], 0)
+    def costs(slow, gather, scatter, fixed, pe, hop, late, more=0):
+        dur = [(c + gather * x + scatter * y + fixed * z + (more if o["eng"] == "dve" else 0)) * (pe if o["eng"] == "pe" else 1)
+               * (slow if o["kind"] == "c" else 1) for o in ops for c, x, y, z in [o["cost"]]]
+        return dur, [o["lat"] + (late if o["kind"] != "c" else 0) for o in ops], hop
+
+    guess = [costs(*x) for x in GUESS]
+    dur, lat, hop = guess[0]
     hist = {}
     for i, o in enumerate(ops):
-        dep = set()
+        dep = {}
         for x, w in [(x, False) for x in o["rd"]] + [(x, True) for x in o["wr"]]:
             for y, j, wj in hist.get(x[0], []):
                 both_read = not (w or wj)
+                same = ops[j]["eng"] == o["eng"] and ops[j]["kind"] == o["kind"] == "c"
                 if j != i and _overlap(x, y) and not (both_read and (x[0] != "ps" or ops[j]["eng"] == o["eng"])):
-                    dep.add(j)
+                    dep[j] = dep.get(j, False) or not (same and (o["chain"] or (INORDER and w)))
         for x, w in [(x, False) for x in o["rd"]] + [(x, True) for x in o["wr"]]:
             hist.setdefault(x[0], []).append((x, i, w))
         o["dep"] = dep
     far = [0.0] * len(ops)
     for i in range(len(ops) - 1, -1, -1):
-        far[i] += ops[i]["dur"] + ops[i]["lat"] + ops[i]["early"]
+        far[i] += dur[i] + lat[i] + ops[i]["early"]
         for j in ops[i]["dep"]:
-            far[j] = max(far[j], far[i] + hop)
+            far[j] = max(far[j], far[i] + hop[1])
     n = len(ops)
-    deps = [sorted(o["dep"]) for o in ops]
-    after = [[] for o in ops]
-    for i in range(n):
-        for j in deps[i]:
-            after[j].append(i)
+    eng = [o["eng"] for o in ops]
+    behind, links = [], ([[] for o in ops], [[] for o in ops])
+    for i, o in enumerate(ops):
+        seen = 0
+        for j in sorted(o["dep"], reverse=True):
+            if not seen >> j & 1:
+                gap = hop[eng[i] != eng[j]] + lat[j] if o["dep"][j] else 0
+                links[0][i].append((j, gap))
+                links[1][j].append((i, gap))
+            seen |= (behind[j] if o["dep"][j] else 0) | 1 << j
+        behind.append(seen)
 
     def place(urge, back):
-        p = list(urge)
+        p, link = list(urge), links[back]
         for i in (range(n) if back else range(n - 1, -1, -1)):
-            for j in (after[i] if back else deps[i]):
-                p[j] = max(p[j], p[i] + 1e-3)
-        busy, st, en = {}, [0.0] * n, [0.0] * n
+            for j, gap in link[i]:
+                if p[j] <= p[i]:
+                    p[j] = p[i] + 1e-3
+        busy, en = {e: [] for e in eng}, [0.0] * n
         for i in sorted(range(n), key=lambda i: -p[i]):
-            o = ops[i]
-            s, d = 0.0, o["dur"]
-            for j in (after[i] if back else deps[i]):
-                s = max(s, en[j] + hop)
-            s += o["lat"] if back else 0
-            line = busy.setdefault(o["eng"], [])
+            s, d, line = lat[i] if back else 0.0, dur[i], busy[eng[i]]
+            for j, gap in link[i]:
+                if en[j] + gap > s:
+                    s = en[j] + gap
             k = len(line)
             while k > 0 and line[k - 1][1] > s:
                 k -= 1
             while k < len(line) and s + d > line[k][0]:
-                s = max(s, line[k][1])
+                if line[k][1] > s:
+                    s = line[k][1]
                 k += 1
             line.insert(k, (s, s + d))
-            st[i], en[i] = s, s + d + (0 if back else o["lat"])
-        return max(en), st, en
+            en[i] = s + d
+        if back:
+            return max(en), None, en
+        end = [en[i] + lat[i] for i in range(n)]
+        seq = sorted(range(n), key=lambda i: (en[i] - dur[i], i))
+        return (max(end) + sum(w * replay(seq, *x) for w, x in zip(WEIGH, guess[1:]))) / len(guess), \
+            [en[i] - dur[i] for i in range(n)], end
+
+    def replay(seq, dur, lat, hop):
+        free, en = {e: 0.0 for e in eng}, [0.0] * n
+        for i in seq:
+            s = free[eng[i]]
+            for j, gap in links[0][i]:
+                x = en[j] + hop[eng[i] != eng[j]] if gap else en[j] - lat[j]
+                if x > s:
+                    s = x
+            free[eng[i]] = s + dur[i]
+            en[i] = s + dur[i] + lat[i]
+        return max(en)
 
     if "best" not in PLAN:
         rng = np.random.default_rng(SEED)
-        best = now = place(far, False)
-        for rep in range(PASSES):
-            noise, mid = rng.normal(size=n) * SIG[rep % len(SIG)], rng.random() * best[0]
-            late = place([now[2][i] + (float(noise[i]) if abs(now[2][i] - mid) < WIDE else 0) for i in range(n)], True)
-            new = place(late[2], False)
-            if new[0] <= best[0] + SLACK * (1 - rep / PASSES):
-                now = new
-            if new[0] <= best[0]:
-                best = new
-        PLAN["best"] = best
+
+        def improve(best, passes):
+            now = best
+            for rep in range(passes):
+                noise, mid = rng.normal(size=n) * SIG[rep % len(SIG)], rng.random() * best[0]
+                late = place([now[2][i] + (float(noise[i]) if abs(now[2][i] - mid) < WIDE else 0) for i in range(n)], True)
+                new = place(late[2], False)
+                if new[0] <= best[0] + SLACK * (1 - rep / passes):
+                    now = new
+                if new[0] <= best[0]:
+                    best = new
+            return best
+
+        tries = [improve(place(far, False), PASSES // 8) for k in range(STARTS)]
+        best = improve(min(tries, key=lambda x: x[0]), PASSES - STARTS * (PASSES // 8))
+        seq = sorted(range(n), key=lambda i: (best[1][i], i))
+
+        def worth(seq):
+            return sum(w * replay(seq, *x) for w, x in zip((1,) + WEIGH, guess)) / len(guess)
+
+        now = worth(seq)
+        for rep in range(MOVES):
+            a = int(rng.integers(n))
+            i, step, left, b = seq[a], 1 if rng.random() < 0.5 else -1, int(rng.integers(1, 5)), a
+            tied = {j for j, gap in links[step > 0][i]}
+            while left and 0 <= b + step < n and seq[b + step] not in tied:
+                b += step
+                left -= eng[seq[b]] == eng[i]
+            if left:
+                continue
+            other = seq[:a] + seq[a + 1:]
+            other.insert(b, i)
+            new = worth(other)
+            if new <= now:
+                seq, now = other, new
+        PLAN["best"] = (now, seq, best[2])
     for i, o in enumerate(ops):
-        o["start"], o["end"] = PLAN["best"][1][i], PLAN["best"][2][i]
-    return sorted(range(len(ops)), key=lambda i: (ops[i]["start"], i))
+        o["end"] = PLAN["best"][2][i]
+    return PLAN["best"][1]
 
 
 def emit(g, T, ops, Q):
@@ -704,12 +795,9 @@ def emit(g, T, ops, Q):
         e = o["eng"]
         need = {}
         for j in o["dep"]:
-            if o["chain"] and ops[j]["eng"] == e:
+            if not o["dep"][j]:
                 continue
             s, v = ops[j]["sig"]
-            if s in done and known[e].get(s, 0) < v:
-                while v < len(done[s]) and ops[done[s][v]]["end"] + LONG <= o["start"]:
-                    j, v = done[s][v], v + 1
             if need.get(s, (0, 0))[0] < v:
                 need[s] = (v, j)
         for s, (v, j) in sorted(need.items(), key=lambda kv: -ops[kv[1][1]]["end"]):

import numpy as np
from concourse.mybir import dt, AluOpType, ActivationFunctionType

A = AluOpType
F = ActivationFunctionType
C, V, K, ROUNDS = 384, 48, 128, 3
E = 4 * V
STEP = [1, 2, 1]
NB = C // 16
BIG = 2.0 ** 80
WHOLE = 1.5 * 2 ** 23
F32, BF, I32, U16, F16 = "float32", "bfloat16", "int32", "uint16", "float16"
CODE, PLANE = "float8_e4m3fn_x4", "uint8"
LO = (0, 64, 128, 192, 256, 256)
UO = (0, 1728, 3008, 4032, 4800, 5312)
SO = (0, 320, 576, 768, 896, 960)
TILES = (0, 3, 4, 5, 1, 2)
ACT_ROWS = (8, 6, 6)
ZG_DVE = ()
RELU_DVE = (2, 4, 4)
XRUNS = ((0, 128), (128, 128), (256, 128))
SK_Q = "sp"
MOVES = 22000
GUESS = ((1, 1.56, 3.8, 85, 1.2, (190, 190), 200, 12), (1.4, 1.9, 5.2, 80, 1.6, (165, 165), 0, 10),
         (1, 1.3, 2.6, 78, 1.5, (150, 150), 900, 10), (1, 1.56, 3.8, 100, 1.0, (60, 350), 300, 0),
         (1, 1.56, 3.8, 78, 1.3, (250, 80), 0, 0))
WEIGH = (0.7, 1, 1, 1)
SMALL_DVE = ()
WIDE, STARTS = 3000, 3
XS_DVE = 3
SHORT = 17
AT_DVE = True
LT_DVE = 2
OC_SPLIT = True
TAB = 1160
MRUNS = ((0, E),)
NEAR_PE = False
INORDER = False
ONE, TWOL, TWOZ = ((0, C),), ((0, 192), (192, C)), ((0, 256), (256, C))
LANES = ((ONE, ONE, ONE), (ONE, ONE, ONE))
YRUNS = ((0, 256), (256, 128))
XH = ((0, 768), (768, 768))
S0_DMA = True
ZA = (256, 256, 192)
MT, ZT = (1536, 2304, 4608), 3072
SIG, SLACK, PASSES, SEED, PLAN = (150, 500, 1500), 300, 4800, 2, {}


def _sb(n, d):
    return ("sbuf", [128, n], d)


SCRATCH = {
    "ati": _sb(24, I32), "exi": _sb(12, I32), "ub": _sb(512, BF), "vb": _sb(512, BF),
    "wq": _sb(512, CODE), "wp": _sb(512, PLANE), "uq": _sb(128, CODE), "up": _sb(128, PLANE),
    "uq2": _sb(128, CODE), "up2": _sb(128, PLANE), "vq": _sb(128, CODE), "vp": _sb(128, PLANE),
    "num": _sb(1200, F32), "t512": _sb(64, F32), "e8192": _sb(E, F32),
    "pi": _sb(8, I32), "pm": _sb(8, F32), "i16": _sb(2 * C, BF), "dm": _sb(C, BF), "dm4": _sb(C, BF),
    "a1": _sb(2 * C, BF), "keep": _sb(C, BF), "own": _sb(416, BF), "keep4": _sb(C, BF),
    "cc": _sb(C, BF), "half": _sb(64, BF), "ones": _sb(512, BF), "c1": _sb(512, BF), "gb": _sb(512, BF),
    "eb": _sb(2048, BF), "zb": _sb(512, BF), "gq": _sb(128, CODE), "gp": _sb(128, PLANE), "eq": _sb(512, CODE),
    "ep": _sb(512, PLANE), "zq0": _sb(256, CODE), "zp0": _sb(256, PLANE),
    "ci": _sb(24, I32), "cf": _sb(504, F32), "cu": _sb(128, U16), "uo": _sb(8, U16),
    "at1": _sb(C, BF), "lt": _sb(C * 3, BF), "cs": _sb(C * 3, F32), "nrp": _sb(C, BF),
    "ff": _sb(416, F16), "tr": _sb(800, F16), "trs": _sb(800, F16),
    "th": _sb(64, F32), "acc": _sb(64, F32), "su": _sb(128, U16),
    "xrep": _sb(E, F32), "x16": _sb(E, U16), "sig": _sb(E, F32), "sig2": _sb(E, F32), "sigw": _sb(12, F32), "wa": _sb(C, F32),
    "li": _sb(128, I32), "lf": _sb(3 * 320, F32), "lu": _sb(3 * 128, U16), "land": _sb(4 * 48, F32), "ro": _sb(48, I32),
    "crep": _sb(E, F32), "csrt": _sb(E, F32), "pf": _sb(208, F32), "g1": _sb(272, F32),
    "g2": _sb(2 * 704, F32), "vrep": _sb(E, F32), "vw": _sb(3 * 768, F32), "vk": _sb(C, BF), "vs": _sb(C, F32),
    "vg": _sb(768, F32), "lv": _sb(96, F32), "l4": _sb(48, F32), "d0": _sb(3 * 448, BF), "ml": _sb(3 * 132, U16),
    "bl": _sb(132, F32), "mk": _sb(120, F32), "tab": _sb(3 * TAB, F32), "nd": _sb(C, BF), "sp": _sb(72, U16),
    "ssb": _sb(800, F32), "sa": _sb(C, F32), "yy": _sb(400, F32), "st": _sb(960, F32),
    "ut": _sb(5824, BF), "utq": _sb(6 * C, CODE), "utp": _sb(6 * C, PLANE), "sg": _sb(20 * 320, BF), "rs": _sb(72, F32),
    "ds": _sb(2 * C, F16), "jr": _sb(3200, F16), "qq": _sb(32, F32), "pw": _sb(96, F32),
    "pu": _sb(144, U16), "w1": _sb(C, F16), "w2": _sb(C, F16), "w3": _sb(C, F16), "w4": _sb(C, F16),
    "srep": _sb(C, F32), "land2": _sb(96, F32), "du": _sb(144, U16),
    "xm": _sb(5376, BF), "xmh": _sb(3840, BF), "xq": _sb(C, CODE), "xp": _sb(C, PLANE), "zq": _sb(C, CODE), "zp": _sb(C, PLANE),
    "rr": _sb(4 * 576, F32), "zl": _sb(768, BF), "zg": _sb(1536, BF),
    "mt": _sb(768, BF), "mq": _sb(E, CODE), "mp": _sb(E, PLANE), "ysb": _sb(C, F32),
    "bq0": _sb(K, CODE), "bp0": _sb(K, PLANE), "bq1": _sb(K, CODE), "bp1": _sb(K, PLANE), "bq2": _sb(K, CODE), "bp2": _sb(K, PLANE),
    "aq0": _sb(K, CODE), "ap0": _sb(K, PLANE), "aq1": _sb(K, CODE), "ap1": _sb(K, PLANE), "aq2": _sb(K, CODE), "ap2": _sb(K, PLANE),
    "ps": ("psum", [128, 4096], F32),
}
SEMAPHORES = ["dve", "act", "pe", "pool", "arr0", "arr1", "arr2", "out0", "out1", "out2"] + ["d%d" % i for i in range(100)]
TWO = (BF, F16, U16)


def _overlap(a, b):
    if a[0] != b[0]:
        return False
    if a[0] == "ps":
        return a[1] // 512 == b[1] // 512
    if a[1] >= b[2] or b[1] >= a[2]:
        return False
    if a[3] == b[3] and a[3] > 1:
        return (a[1] - b[1]) % a[3] == 0
    return True


def build(g, core, T, topo, rank):
    ops = []
    Q = {"dve": g.vector, "act": g.scalar, "pe": g.tensor, "pool": g, "sp": g.sync}

    def r(name, a=0, b=None, s=1):
        return (name, a, SCRATCH[name][1][1] if b is None else b, s)

    def ind(win, off):
        return ("ind", win, off)

    def ap(x):
        if x[0] == "ind":
            return ap(x[1]).indirect(ap(x[2]))
        if x[3] == 1:
            return T[x[0]][:, x[1]:x[2]]
        return T[x[0]][:, x[1]:x[2]:x[3]]

    def regs(xs):
        o = []
        for x in xs:
            if isinstance(x, tuple):
                o += [x[1], x[2]] if x[0] == "ind" else [x]
        return o

    def cnt(x):
        if x[0] == "ind":
            return 16 * (x[2][2] - x[2][1])
        return len(range(x[1], x[2], x[3]))

    def val(x):
        return ap(x) if isinstance(x, tuple) else x

    def two(*xs):
        return all(SCRATCH[x[0]][2] in TWO for x in xs)

    def add(eng, fn, rd, wr, dur, lat=0, kind="c", chain=False, sem=None, early=0):
        ops.append({"eng": eng, "fn": fn, "rd": regs(rd), "wr": regs(wr), "cost": dur if isinstance(dur, tuple) else (dur, 0, 0, 0), "lat": lat, "kind": kind,
                    "chain": chain, "sem": sem, "early": early})

    def vcost(out, ins, per):
        if out[0] == "ind":
            return (60, 0, cnt(out), 0)
        if ins[0][0] == "ind":
            return (60, cnt(out), 0, 0)
        return max(64, per * cnt(out)) + 10

    def cp(out, in_):
        per = 1 if out[0] == "ind" or in_[0] == "ind" or not two(out, in_) else .5
        add("dve", lambda: g.vector.tensor_copy(ap(out), ap(in_)), [in_] + ([out[2]] if out[0] == "ind" else []),
            [out[1] if out[0] == "ind" else out], vcost(out, [in_], per))

    def tt(out, a, b, op):
        per = 1 if "ps" in (a[0], b[0]) else 2
        add("dve", lambda: g.vector.tensor_tensor(ap(out), ap(a), ap(b), op), [a, b], [out], vcost(out, [a], per))

    def ts(out, a, s1, op0, s2=None, op1=None):
        per = 1 if a[0] == "ind" or not two(out, a) else .5
        if op1 is None:
            fn = lambda: g.vector.tensor_scalar(ap(out), ap(a), val(s1), None, op0)
        else:
            fn = lambda: g.vector.tensor_scalar(ap(out), ap(a), val(s1), val(s2), op0, op1)
        add("dve", fn, [a, s1, s2], [out], vcost(out, [a], per))

    def scan(out, d0, d1, op0, op1, init=0.0):
        add("dve", lambda: g.vector.tensor_tensor_scan(ap(out), ap(d0), ap(d1), val(init), op0, op1), [d0, d1, init], [out],
            vcost(out, [d0], .5 if two(out, d0, d1) else 1))

    def mset(out, c):
        add("dve", lambda: g.vector.memset(ap(out), c), [], [out], vcost(out, [out], .5 if two(out) else 1))

    def quant(q, p, in_):
        add("dve", lambda: g.vector.quantize_mx(ap(q), ap(p), ap(in_)), [in_], [q, p], 15 + .265 * cnt(in_))

    def act(out, in_, func=F.Copy, bias=None, scale=None, acc=None):
        def fn():
            kw = {}
            if bias is not None:
                kw["bias"] = val(bias)
            if scale is not None:
                kw["scale"] = val(scale)
            if acc is not None:
                kw["accum_out"] = ap(acc)
            return g.scalar.activation(ap(out), ap(in_), func, **kw)
        d = (78, cnt(out), 0, 0) if in_[0] == "ind" else (cnt(out) + (24 if acc else 0), 0, 0, 1)
        add("act", fn, [in_, bias, scale], [out, acc], d)

    def mm(bank, n, lq, lp, rq, rp, start=True, stop=True):
        o = r("ps", 512 * bank, 512 * bank + n)
        add("pe", lambda: g.tensor.matmul_mx(ap(o), ap(lq), ap(lp), ap(rq), ap(rp), start, stop), [lq, lp, rq, rp], [o],
            .7 * (n + 16), lat=60, chain=not start)

    def ps(bank, n):
        return r("ps", 512 * bank, 512 * bank + n)

    def iota(out, pat, base=0, cm=0, early=0):
        if SCRATCH[out[0]][2] == I32:
            fn = lambda: g.iota(ap(out), pat, base, cm)
        else:
            fn = lambda: g.iota(ap(out), pat, base, cm, allow_small_or_imprecise_dtypes=True)
        add("pool", fn, [], [out], 160 + 2 * cnt(out), early=early)

    def sel(out, in_, pat, op, base, cm, fill=0.0):
        add("pool", lambda: g.affine_select(ap(out), ap(in_), pat, op, fill, base, cm), [in_], [out], 200 + 2 * cnt(out))

    def pcp(out, in_):
        sel(out, in_, [[0, cnt(out)]], A.is_ge, 0, 0)

    def dma(o, i, rd, wr, eng="sp", lat=2400):
        add(eng, lambda: Q[eng].dma_start(o(), i()), rd, wr, 70, lat=lat, kind="dma")

    def u8(x):
        return ap(x).bitcast(dt.uint8)

    def spread(dst, src):
        dma(lambda: ap(dst), lambda: T[src[0]][0:128:16, src[1]:src[2]], [src], [dst])

    def copy(dst, src):
        dma(lambda: ap(dst), lambda: ap(src), [src], [dst], lat=2400 + cnt(dst))

    def xm(a, n, s=1):
        return r("xm", a, a + n, s)

    num, numc = r("num", 0, 400), r("num", 0, C)
    xt, zt = xm(0, 4 * C), xm(ZT, 4 * C)
    dma(lambda: T.ati[:], lambda: T.at[:], [], [r("ati")])
    dma(lambda: T.exi[:], lambda: T.ex[:], [], [r("exi")])
    dma(lambda: T.ub[:], lambda: T.u[:], [], [r("ub")], lat=3200)
    dma(lambda: ap(xt), lambda: T.x[:], [], [xt], eng="act", lat=4800)
    dma(lambda: ap(xm(MT[0], 768)), lambda: T.e[:], [xt], [xm(MT[0], 768)], lat=4000)
    dma(lambda: u8(r("wq")), lambda: T.wc[:], [xt], [r("wq")], lat=5000)
    dma(lambda: T.wp[:], lambda: T.ws[:], [xt], [r("wp")], lat=5000)
    dma(lambda: T.vb[:], lambda: T.v[:], [xt], [r("vb")], lat=5000)
    iota(r("pi", 0, 1), [[0, 1]], 0, 1, early=4e4)
    iota(r("ci", 0, 24), [[16, 24]], early=3e4)
    iota(r("t512"), [[512, 64]], early=2e4)
    iota(numc, [[1, C]], early=1e4)
    iota(r("num", C, 800), [[1, 800 - C]], C)
    iota(r("num", 800, 1200), [[1, 400]], 800)
    iota(r("i16", 0, C), [[0, NB], [1, 16]], early=5e3)
    iota(r("e8192"), [[8192, E]])
    mset(r("ones"), 1.0)
    mset(r("zb"), 0.0)
    ts(r("pi", 2, 3), r("pi", 0, 1), 15, A.bitwise_and)
    cp(r("pm", 0, 1), r("pi", 2, 3))
    pm, keep = r("pm", 0, 1), r("keep", 0, C)
    ts(r("dm"), r("i16", 0, C), pm, A.is_equal)
    ts(r("a1", 0, C), r("dm"), -BIG, A.mult, BIG, A.add)
    sel(r("keep"), r("ones", 0, C), [[0, NB], [1, 16]], A.is_gt, 0, 0)
    ts(r("a1", C, 2 * C), r("dm"), BIG, A.mult, -BIG / 2, A.add)
    sel(r("cc"), r("a1", C, 2 * C), [[0, NB], [1, 16]], A.is_gt, 0, 0, BIG / 2)
    act(r("half"), r("num", 0, 64), scale=BIG / 128, bias=BIG / 2)
    cp(r("uo"), r("ci", 0, 8))
    jw = r("cf", 0, 24)
    ts(jw, r("ci", 0, 24), pm, A.add)
    j12, ga = r("cf", 0, 12), r("cf", 256, 280)

    def above(out, x, w):
        act(out, x, scale=1.0 / w, bias=0.5 / w - 0.5)
        act(out, out, bias=WHOLE)

    def turn(out, x, w, t1, t2, h=16):
        above(t1, x, w)
        act(t2, x, scale=float(h))
        ts(t1, t1, -WHOLE, A.add, -float(h * w - 1), A.mult)
        tt(out, t1, t2, A.add)

    turn(ga, jw, 24, r("cf", 352, 376), r("cf", 376, 400))
    turn(r("cf", 280, 304), ga, 96, r("cf", 400, 424), r("cf", 424, 448), 4)
    turn(r("cf", 304, 316), j12, 12, r("cf", 448, 460), r("cf", 460, 472))
    turn(r("cf", 192, 196), r("cf", 0, 4), 4, r("cf", 472, 476), r("cf", 476, 480))
    above(r("cf", 72, 84), r("cf", 304, 316), 4)
    act(r("cf", 316, 328), r("cf", 72, 84), bias=E - WHOLE)
    act(r("cf", 328, 331), r("cf", 72, 75), bias=E + 4 - WHOLE)
    act(r("cf", 331, 335), r("cf", 192, 196), bias=float(E))
    act(r("cf", 335, 336), r("cf", 192, 193), bias=float(E + 16))
    cp(r("cu", 0, 24), ga)
    cp(r("cu", 24, 48), r("cf", 280, 304))
    cp(r("cu", 48, 80), r("cf", 304, 336))
    g1216 = r("cu", 48, 60)
    c4n = r("cf", 84, 96)
    act(r("cf", 120, 132), j12, bias=float(C))
    act(r("cf", 132, 136), r("cf", 0, 4), bias=float(C))
    act(r("cf", 200, 212), j12, bias=float(C + E))
    act(r("cf", 212, 216), r("cf", 0, 4), bias=float(C))
    act(r("cf", 24, 48), jw, bias=8.0)
    iota(r("mk", 0, 20), [[0, 20]], 1)
    act(r("cf", 48, 72), jw, bias=4.0)
    above(r("cf", 136, 148), j12, 4)
    act(c4n, r("cf", 136, 148), bias=-WHOLE)
    act(c4n, c4n, scale=4.0, bias=3.0)
    tt(r("ro", 0, 12), c4n, j12, A.subtract)
    sel(r("c1"), r("ones"), [[-16, 8], [0, 64]], A.is_ge, 0, 1)
    sel(r("gb"), r("c1"), [[16, 8], [0, 64]], A.is_ge, 15, -1)
    quant(r("gq"), r("gp"), r("gb"))
    for k in range(6):
        copy(r("ut", UO[k], UO[k] + 4 * (64 * k + 48 - LO[k])), r("zb", 0, 4 * (64 * k + 48 - LO[k])))
    copy(r("ut", 1536, 1536 + 192), r("zb", 0, 192))
    quant(r("zq0", 0, 128), r("zp0", 0, 128), r("zb"))
    dma(lambda: u8(r("zq0", 128, 256)), lambda: u8(r("zq0", 0, 128)), [r("zq0", 0, 128)], [r("zq0", 128, 256)])
    dma(lambda: T.zp0[:, 128:256], lambda: T.zp0[:, 0:128], [r("zp0", 0, 128)], [r("zp0", 128, 256)])
    for k in range(1, 6):
        dq, dp = r("utq", C * k, C * k + LO[k]), r("utp", C * k, C * k + LO[k])
        dma(lambda dq=dq, w=LO[k]: u8(dq), lambda w=LO[k]: u8(r("zq0", 0, w)), [r("zq0")], [dq])
        dma(lambda dp=dp: ap(dp), lambda w=LO[k]: ap(r("zp0", 0, w)), [r("zp0")], [dp])
    for t in range(ROUNDS):
        iota(r("tab", TAB * t, TAB * t + TAB), [[0, TAB]])
        iota(r("vw", 768 * t, 768 * t + 768), [[0, 768]], 8)
        if t:
            copy(r("d0", 448 * t + C, 448 * t + 448), r("zb", 0, 64))
    for b in range(4):
        sel(r("eb", 512 * b, 512 * b + 512), r("ones"), [[-1, 512]], A.is_equal, b, 4)
    iota(r("rr", 4 * C, 4 * C + 768), [[0, 768]])
    quant(r("eq"), r("ep"), r("eb"))
    act(r("ssb", 0, 8), r("ones", 0, 8), scale=-BIG)
    act(r("yy", C, 400), r("ones", 0, 16), scale=BIG)
    iota(r("qq", 0, 2), [[0, 2]])
    iota(r("rs"), [[0, 72]])
    iota(r("bl", 0, 72), [[0, 72]])
    iota(r("pf", 0, 2), [[0, 2]])
    iota(r("acc", 3, 4), [[0, 1]], -C)
    ts(r("pi", 6, 7), r("pi", 0, 1), 3, A.bitwise_and)
    cp(r("pm", 6, 7), r("pi", 6, 7))
    ts(r("pi", 5, 6), r("pi", 2, 3), 2, A.arith_shift_right)
    cp(r("pm", 5, 6), r("pi", 5, 6))
    iota(r("i16", C, 2 * C), [[0, C // 4], [1, 4]])
    ts(r("dm4"), r("i16", C, 2 * C), r("pm", 5, 6), A.is_equal)
    sel(r("keep4"), r("ones", 0, C), [[0, C // 4], [1, 4]], A.is_gt, 0, 0)
    iota(r("g1", 256, 272), [[0, 16]], C)
    quant(r("uq"), r("up"), r("ub"))
    add("dve", lambda: g.vector.tensor_copy(T.uq2[:].bitcast(dt.uint32), T.uq[:].bitcast(dt.uint32).indirect(T.uo[:, 0:8])),
        [r("uq"), r("uo")], [r("uq2")], 260)
    add("act", lambda: g.scalar.activation(T.up2[:], T.up[:].indirect(T.uo[:, 0:8]), F.Copy), [r("up"), r("uo")], [r("up2")], 280)
    quant(r("vq"), r("vp"), r("vb"))

    at16, rk16, st16, s016, ex16, ln16, sg16 = (r("su", 0, 24), r("su", 24, 48), r("su", 48, 52), r("su", 52, 76),
                                                r("su", 76, 88), r("su", 88, 104), r("su", 104, 116))
    cp(at16, r("ati"))
    act(r("nrp"), ind(numc, at16))
    act(r("th", 0, 3), r("cf", 0, 3), scale=-1.0, bias=0.5)
    for m in range(3):
        if AT_DVE:
            ts(r("lt", C * m, C * m + C), r("nrp"), r("cf", m, m + 1), A.is_lt, -2.0, A.mult)
            scan(r("tr", E * m, E * m + E), r("lt", C * m, C * m + E), r("lt", C * m + E, C * m + C), A.add, A.add, float(C))
        else:
            act(r("g2", C * m, C * m + C), r("nrp"), F.Sign, bias=r("th", m, m + 1), acc=r("acc", m, m + 1))
    if AT_DVE:
        cp(r("acc", 0, 3), r("tr", E - 1, 3 * E, E))
    ts(st16, r("acc", 0, 4), -0.5, A.mult, C / 2, A.add)
    act(r("th", 4, 7), r("cf", 0, 3), scale=8.0, bias=8.0)
    tt(r("th", 4, 7), r("acc", 0, 3), r("th", 4, 7), A.subtract)
    ts(r("li", 96, 120), r("ati"), 4, A.arith_shift_right)
    act(r("at1"), ind(r("dm", 0, 64), at16))
    mset(r("ff", 0, 16), 0.0)
    mset(r("ff", 400, 416), 0.0)
    ts(r("pi", 4, 5), r("pi", 0, 1), 4, A.arith_shift_right, 1, A.bitwise_and)
    cp(r("pm", 2, 3), r("pi", 4, 5))
    iota(r("own"), [[0, 13], [1, 2], [0, 16]])
    ts(r("own"), r("own"), r("pm", 2, 3), A.is_equal)

    def by_node():
        cp(rk16, r("pw", 48, 72))
        cp(ind(r("nd"), rk16), r("nrp"))
        for q in range(3):
            if q < LT_DVE:
                ts(r("lt", C * q, C * q + C), r("nd"), r("cf", q, q + 1), A.is_equal, -2.0, A.mult)
                scan(r("cs", q, 3 * C, 3), r("ones", 0, C), r("lt", C * q, C * q + C), A.mult, A.add, r("th", 4 + q, 5 + q))
            else:
                act(r("lt", C * q, C * q + C), r("nd"), F.Abs, scale=-1.0, bias=r("cf", q, q + 1))
                act(r("lt", C * q, C * q + C), r("lt", C * q, C * q + C), F.Relu, scale=-2.0, bias=2.0)
                scan(r("cs", q, 3 * C, 3), r("zb", 0, C), r("lt", C * q, C * q + C), A.add, A.subtract, r("th", 4 + q, 5 + q))
        act(r("th", 40, 64), r("pw", 48, 72), scale=3.0)
        tt(r("th", 8, 32), r("li", 96, 120), r("th", 40, 64), A.add)
        cp(s016, r("th", 8, 32))
        tt(r("ff", 16, 400), ind(r("cs"), s016), r("at1"), A.mult)
        for o, a, n in ((0, 16, C), (C, 0, 416)):
            x, y = r("tr", o, o + n), r("ff", a, a + n)
            add("dve", lambda x=x, y=y: g.vector.transpose(ap(x), ap(y)), [y], [x], 10 + n / 2)
            scan(r("trs", o, o + n), x, r("own", 0, n), A.add, A.mult)
        tt(r("pw", 72, 96, 2), r("trs", 15, C, 32), r("trs", C + 31, 768, 32), A.add)
        tt(r("pw", 73, 96, 2), r("trs", 31, C, 32), r("trs", C + 47, 800, 32), A.add)
        ts(r("pu", 0, 24), r("pw", 72, 96), -1.0, A.mult, C - 2.0, A.add)

    cp(ex16, r("exi"))
    tt(r("xrep"), ind(r("t512"), ex16), r("num", 0, E), A.add)
    ts(r("cf", 160, 172), r("exi"), 512.0, A.mult)
    tt(r("cf", 160, 172), r("cf", 160, 172), j12, A.add)
    act(r("cf", 172, 176), r("cf", 0, 4), scale=512.0)
    act(r("cf", 176, 192), r("cf", 160, 176), scale=-1.0, bias=0.5)
    iota(r("acc", 47, 48), [[0, 1]], -E)
    for m in range(XS_DVE, 15):
        act(r("sg", C * m, C * m + E), r("xrep"), F.Sign, bias=r("cf", 176 + m, 177 + m), acc=r("acc", 32 + m, 33 + m))
    ts(r("su", 88 + XS_DVE, 104), r("acc", 32 + XS_DVE, 48), -0.5, A.mult, E / 2, A.add)
    if XS_DVE:
        cp(r("x16"), r("xrep"))
        for m in range(XS_DVE):
            ts(r("sg", C * m, C * m + E), r("x16"), r("cf", 160 + m, 161 + m), A.is_lt)
            scan(r("jr", 160 * m + 64, 160 * m + 160), r("sg", C * m, C * m + 96), r("sg", C * m + 96, C * m + E), A.add, A.add)
        cp(r("su", 88, 88 + XS_DVE), r("jr", 159, 160 * XS_DVE, 160))
    cp(ind(r("sig"), r("su", 88, 100)), r("num", 0, E))
    act(r("sig2"), ind(r("sig"), g1216))
    spread(r("sigw"), r("sig2"))
    cp(sg16, r("sigw"))

    def land(i, a, n):
        return r("land", 48 * i + a, 48 * i + a + n)

    def expand(i):
        o = 704 * (i % 2)
        a, b = {0: (12, 27), 3: (0, 12)}.get(i, (0, 32))
        act(r("g2", o + 16 * a, o + 16 * b), ind(r("g1"), r("cu", 48 + a, 48 + b)))
        for x, y, n in ((0, 0, 12), (192, 20, 12), (240, 32, 12), (432, 12, 4), (436, 16, 4)):
            if 16 * a <= x < 16 * b:
                spread(land(i, y, n), r("g2", o + x, o + x + 16 * n))

    def lf(t, a, n, s=1):
        return r("lf", 320 * t + a, 320 * t + a + n, s)

    def lu(t, a, n):
        return r("lu", 128 * t + a, 128 * t + a + n)

    def ml(t, a, n):
        return r("ml", 132 * t + a, 132 * t + a + n)

    def starts(t, off):
        d0 = r("d0", 448 * t, 448 * t + C)
        pcp(d0, r("cc"))
        cp(ind(r("d0", 448 * t, 448 * t + 448), off), r("half", 0, 48))
        scan(r("nd"), d0, d0, A.max, A.max)
        n512, last = lf(t, 0, 24), lf(t, 96, 24)
        act(r("vg", 0, C), ind(r("nd"), r("cu", 0, 24)), scale=65536 / BIG, bias=-32768.0)
        spread(n512, r("vg", 0, C))
        act(last, r("nd", 15, C, 16), scale=65536 / BIG, bias=-32768.0)
        act(lf(t, 24, 24), n512, scale=-1.0 / 128)
        tt(lf(t, 48, 48), r("cf", 24, 72), lf(t, 0, 48), A.subtract)
        tt(lf(t, 120, 24), last, r("num", 15, C, 16), A.subtract)
        for d in range(1, 4):
            tt(r("bl", 24 * d - 24, 24 * d - d), lf(t, d, 24 - d), lf(t, 120, 24 - d), A.subtract)
        if "bl" in SMALL_DVE:
            for k in range(5):
                ts(ml(t, 72 + SO[k] // 16, 20 - 4 * k), lf(t, 52 + 4 * k, 20 - 4 * k), lf(t, 99 + 4 * k, 1), A.add, 0.0, A.max)
            ts(ml(t, 0, 72), r("bl", 0, 72), 399.0, A.min)
        else:
            for k in range(5):
                act(r("bl", 72 + SO[k] // 16, 72 + SO[k + 1] // 16), lf(t, 52 + 4 * k, 20 - 4 * k), F.Relu, bias=lf(t, 99 + 4 * k, 1))
            ts(ml(t, 0, 132), r("bl"), 399.0, A.min)
        if "mk" in SMALL_DVE:
            for q in range(3):
                tt(r("mk", 40 * t + q, 40 * t + 20, 4), lf(t, 99, 17, 4), lf(t, 96 + q, 17, 4), A.is_equal)
        else:
            act(lf(t, 168, 24), last, scale=-1.0, bias=1.0)
            for k in range(5):
                act(r("mk", 40 * t + 4 * k, 40 * t + 4 * k + 4), lf(t, 96 + 4 * k, 4), F.Relu, bias=lf(t, 171 + 4 * k, 1))
        act(r("mk", 40 * t + 20, 40 * t + 40), r("mk", 40 * t, 40 * t + 20), scale=-1.0)

    def exits(t):
        st, en, rot, nxt = land(t, 20, 12), land(t, 32, 12), r("ro", 12 * t, 12 * t + 12), r("ro", 12 * t + 12, 12 * t + 24)
        w, u, mp, c4 = lf(t, 220, 12), r("li", 12 * t, 12 * t + 12), lf(t, 192, 12), lf(t, 204, 12)
        tt(w, st, rot, A.subtract)
        tt(u, en, w, A.subtract)
        ts(nxt, u, 3, A.bitwise_and)
        tt(c4, u, nxt, A.subtract)
        tt(mp, w, c4n, A.add)
        ts(lu(t, 0, 24), lf(t, 192, 24), 2.0, A.mult)
        if t == 2:
            tt(lf(t, 232, 12), mp, c4, A.add)
            ts(lu(t, 24, 12), lf(t, 232, 12), 2.0, A.mult)
        cp(ind(r("tab", TAB * t + 8, TAB * t + TAB), lu(t, 0, 12)), r("num", C, C + E))
        act(r("crep"), ind(r("num", 0, 800), lu(t, 12, 12)), scale=0.125)
        act(r("csrt"), ind(r("crep"), sg16))
        scan(r("pf", 1, 1 + E), r("ones", 0, E), r("csrt"), A.mult, A.add)
        act(r("g1", 0, 256 if t < 2 else E), ind(r("pf", 0, 1 + E), ln16 if t < 2 else r("su", 88, 100)))
        expand(t + 1)
        n = 16 if t < 2 else 12
        if t < 2:
            tt(lf(t, 216, 4), land(t + 1, 16, 4), land(t + 1, 12, 4), A.subtract)
        spare, b4 = lf(t, 244, n), lf(t, 260, 12)
        act(spare, lf(t, 204, n), scale=-1000.0)
        tt(spare, spare, r("cf", 200, 216) if t == 1 else r("cf", 120, 120 + n), A.add)
        tt(lf(t, 284, n), spare, land(t + 1, 0, n), A.max)
        cp(lu(t, 48, n), lf(t, 284, n))
        if t < 2:
            starts(t + 1, lu(t, 60, 3))
            act(b4, c4, F.Relu, scale=0.25, bias=-1.0)
            tt(b4, b4, lf(t, 284, 12), A.add)
            for b in range(4):
                act(r("l4", 12 * b, 12 * b + 12), b4, scale=4.0, bias=float(b))
            cp(lu(t, 64, 48), r("l4", 0, 48))
            act(r("vrep"), ind(r("num", 16, 1200), lu(t, 0, 12)))
        else:
            tt(r("vrep"), ind(r("num", 16, 1200), lu(t, 0, 12)), r("e8192"), A.add)
        cp(ind(r("vw", 768 * t, 768 * t + 768), lu(t, 48, 12)), r("vrep"))
        act(r("vk"), r("vw", 768 * t, 768 * t + C), F.Relu, bias=9.0, scale=-1.0)
        scan(r("vs"), r("vk"), r("vw", 768 * t, 768 * t + C), A.mult, A.add)
        act(r("vg", C, 2 * C), ind(r("vs"), r("cu", 24, 48)))
        src = r("lv", 24 * t, 24 * t + 24)
        spread(src, r("vg", C, 2 * C))
        if t == 2:
            act(r("wa"), r("vs"), scale=1.0 / 8192, bias=WHOLE)
            act(r("wa"), r("wa"), bias=-WHOLE)
            dma(lambda: T.ot[:], lambda: T.wa[0:128:16, :], [r("wa")], [])
            cp(r("li", 40, 64), src)
            src = r("li", 64, 88)
            ts(src, r("li", 40, 64), 8191, A.bitwise_and)
        cp(r("sp", 24 * t, 24 * t + 24), src)

    act(r("g1", E, 256), ind(num, st16))
    copy(r("g1", 0, E), r("num", 0, E))
    expand(0)
    ts(ml(0, 0, 24), r("ci", 0, 24), 15.0, A.add)
    iota(r("mk", 20, 40), [[0, 20]], -1)

    def plane(name, b, a, n):
        return r(name, 576 * b + a, 576 * b + a + n)

    def ut(k, s, a, n):
        o = UO[k] + 4 * (a - LO[k]) + s
        return r("ut", o, o + 4 * n - 3, 4)

    act(r("xmh", 4 * C, 4 * C + 768), xm(MT[0], 768), scale=0.5)

    for t in range(ROUNDS):
        exits(t)
        rows = ACT_ROWS[t]
        tab, before = r("tab", TAB * t + 8, TAB * t + TAB), r("tab", TAB * t, TAB * t + TAB)
        quant(r("xq"), r("xp"), xt)
        mm(5, C, r("uq2"), r("up2"), r("xq"), r("xp"))
        mm(4, C, r("uq2"), r("up2"), r("xq"), r("xp"))
        act(r("ssb", 8, 8 + C), ps(5, C))
        sv = ps(4, C)
        tt(r("sa"), sv, r("a1", 0, C), A.add)
        scan(r("yy", 0, C), r("d0", 448 * t, 448 * t + C) if t else r("cc"), r("sa"), A.max, A.min)
        for a, b in ((0, 1), (1, 2), (2, 5)) if t else ():
            act(r("st", SO[a], SO[b]), ind(r("ssb", 0, 8 + C), ml(t, 72 + SO[a] // 16, (SO[b] - SO[a]) // 16)))
        for a, n in XH:
            x, y = r("xmh", a, a + n), r("xmh", 2304 + a, 2304 + a + n)
            act(x, xm(a, n), scale=0.5)
            dma(lambda y=y: ap(y), lambda x=x: ap(x), [x], [y], lat=2900)
        tt(ut(0, 0, 0, C), sv, r("yy", 0, C), A.is_gt)
        for d in range(1, 4):
            tt(ut(0, d, 16 * d, C - 16 * d), ind(r("yy"), ml(t, 24 * d - 24 if t else 0, 24 - d)), r("ssb", 8 + 16 * d, 8 + C), A.is_lt)
        if not NEAR_PE:
            scan(r("ds", 0, C), ut(0, 0, 0, C), ut(0, 1, 16, C), A.add, A.add)
            scan(r("ds", C, 2 * C), ut(0, 2, 32, C), ut(0, 3, 48, C), A.add, A.add)
            tt(r("qq", 1, 25), r("ds", 15, C, 16), r("ds", C + 15, 2 * C, 16), A.add)
            tt(r("pw", 0, 24), lf(t, 72, 24) if t else jw, r("qq", 1, 25), A.add)
            tt(r("pw", 0, 24), r("pw", 0, 24), r("qq", 0, 24), A.subtract)
        for k in TILES:
            for s in range(4 if k else 0):
                m = 4 * (k - 1) + s
                a = 16 * (m + 4)
                n = C - a
                src = r("st", SO[k - 1] + 16 * s, SO[k]) if t else r("ssb", 8 + a, 8 + C)
                y = r("yy", 16 * m + 15, 16 * m + 16)
                if m < rows or m >= SHORT:
                    act(r("sg", 320 * m, 320 * m + n), src, F.Sign, bias=y, scale=-1.0)
                    act(ut(k, s, a, n), r("sg", 320 * m, 320 * m + n), F.Relu, scale=r("mk", 40 * t + 20 + m, 40 * t + 21 + m),
                        acc=r("rs", 24 * t + m, 24 * t + m + 1))
                else:
                    ts(ut(k, s, a, n), src, y, A.is_gt, r("mk", 40 * t + m, 40 * t + m + 1), A.mult)
                    scan(r("jr", 160 * m + 160 - n // 2, 160 * m + 160), ut(k, s, a, n // 2), ut(k, s, a + n // 2, n // 2),
                         A.add, A.add)
            quant(r("utq", C * k + LO[k], C * k + C), r("utp", C * k + LO[k], C * k + C), r("ut", UO[k], UO[k] + 4 * (C - LO[k])))
            for h, (a, b) in enumerate(LANES[0][t]):
                mine = [x for x in TILES if LO[x] < b]
                if k in mine:
                    mm(6 + h, b - a, r("gq"), r("gp"), r("utq", C * k + a, C * k + b), r("utp", C * k + a, C * k + b),
                       k == mine[0], k == mine[-1])
            if k == 0 and NEAR_PE:
                for d in range(4):
                    mm(7, C, r("eq", 128 * d, 128 * d + 128), r("ep", 128 * d, 128 * d + 128), r("utq", 16 * d, 16 * d + C),
                       r("utp", 16 * d, 16 * d + C), d == 0, d == 3)
                scan(r("ds", 0, C), keep, ps(7, C), A.mult, A.add)
                tt(r("pw", 0, 24), lf(t, 72, 24), r("ds", 15, C, 16), A.add)
        tt(r("pw", rows, SHORT), r("pw", rows, SHORT), r("jr", 160 * rows + 159, 160 * SHORT, 160), A.add)
        tt(r("pw", 0, 20), r("pw", 0, 20), r("rs", 24 * t, 24 * t + 20), A.add)
        for h, (a, b) in enumerate(LANES[0][t]):
            tt(r("w1", a, b), ps(6 + h, b - a), r("dm", a, b), A.mult)
            scan(r("w2", a, b), r("keep", a, b), r("w1", a, b), A.mult, A.add)
            tt(r("pw", 48 + a // 16, 48 + b // 16), r("pw", a // 16, b // 16), r("w2", a + 15, b, 16), A.subtract)
            if t:
                ts(r("pu", a // 16, b // 16), r("pw", 48 + a // 16, 48 + b // 16), 2.0, A.mult)
                cp(ind(tab, r("pu", a // 16, b // 16)), r("num", a, b))
        if t == 0:
            by_node()
            cp(ind(tab, r("pu", 0, 24)), numc)
        for a, b in LANES[1][t]:
            tt(r("w3", a, b), ind(before, r("pu", a // 16, b // 16)), r("dm4", a, b), A.mult)
            scan(r("w4", a, b), r("keep4", a, b), r("w3", a, b), A.mult, A.add)
            ts(r("pu", 48 + a // 4, 48 + b // 4), r("w4", a + 3, b, 4), 4.0, A.mult, r("pm", 6, 7), A.add)
        act(r("srep"), ind(before, r("sp", 24 * t, 24 * t + 24)))
        for b in range(4):
            dma(lambda b=b: T.land2[b:128:4, :], lambda: T.srep[0:128:16, :], [r("srep")], [("land2", b, 96, 4)],
                eng="sp" if b % 2 else SK_Q)
        ts(r("du", 0, 96), r("land2"), 4.0, A.mult, r("pm", 6, 7), A.add)
        if t == 2:
            tt(r("w1", 0, E), ind(tab, lu(t, 24, 12)), r("dm4", 0, E), A.mult)
            scan(r("w2", 0, E), r("keep4", 0, E), r("w1", 0, E), A.mult, A.add)
            ts(r("du", 96, 144), r("w2", 3, E, 4), 4.0, A.mult, r("pm", 6, 7), A.add)
        for h, (a, n) in enumerate(((0, ZA[t]), (ZA[t], C - ZA[t]))):
            tt(xm(ZT + 4 * a, 4 * n), ind(r("xmh", 0, 2304), r("pu", 48 + a // 4, 48 + (a + n) // 4)),
               r("xmh", 2304 + 4 * a, 2304 + 4 * (a + n)), A.add)
            quant(r("zq", a, a + n), r("zp", a, a + n), xm(ZT + 4 * a, 4 * n))
            for b in range(4):
                mm(4 * h + b, n, r("wq", 128 * b, 128 * b + 128), r("wp", 128 * b, 128 * b + 128), r("zq", a, a + n),
                   r("zp", a, a + n))
                if h == 1 and b < RELU_DVE[t]:
                    ts(r("rr", 4 * a + b, 4 * (a + n), 4), ps(4 * h + b, n), 0.0, A.max, 0.03125, A.mult)
                else:
                    act(r("rr", 4 * a + b, 4 * (a + n), 4), ps(4 * h + b, n), F.Relu, scale=0.03125)
        new = r("mt") if t == 2 else xm(MT[t + 1], 768)

        def mem(a, n, b=0, s=1, new=new):
            return (new[0], new[1] + 4 * a + b, new[1] + 4 * (a + n), s)
        if t == 2:
            for a, n in ((0, K), (K, E - K)):
                zl, la = r("zl", 4 * a, 4 * (a + n)), r("du", 96 + a // 4, 96 + (a + n) // 4)
                act(zl, ind(xm(ZT, 4 * C + 768), la))
                tt(mem(a, n), ind(r("rr"), la), zl, A.add)
        for h, (a, n) in enumerate(XRUNS):
            zg, sk = r("zg", 4 * a, 4 * (a + n)), r("du", a // 4, (a + n) // 4)
            (cp if h in ZG_DVE else act)(zg, ind(zt, sk))
            tt(xm(4 * a, 4 * n), ind(r("rr", 0, 4 * C), sk), zg, A.add)
        if t < 2:
            for a, n in MRUNS:
                for b in range(4):
                    act(mem(a, n, b, 4), ind(xm(0, MT[t] + 768), lu(t, 64 + 12 * b + a // 16, n // 16)))
        bq, bp, aq, apl = r("bq%d" % t), r("bp%d" % t), r("aq%d" % t), r("ap%d" % t)
        quant(bq, bp, mem(0, K))
        if t == 2 and OC_SPLIT:
            quant(r("zq", 0, K), r("zp", 0, K), mem(E - K, K))
        peer = T.cores[rank ^ STEP[t]]
        rid, pid = topo.addr(peer)[:2]
        eng = topo.engines(core, peer)

        def send(t=t, bq=bq, bp=bp, aq=aq, apl=apl, rid=rid, pid=pid, m=topo.mask(core, peer)):
            g.remote_dma(u8(aq), u8(bq), T.sem["arr%d" % t], T.sem["out%d" % t], pid, rid, m)
            g.remote_dma(ap(apl), ap(bp), T.sem["arr%d" % t], T.sem["out%d" % t], pid, rid, m)
        add("pool", send, [bq, bp], [aq, apl], 600, lat=3600, kind="remote", sem=("arr%d" % t, "out%d" % t, 2 * len(eng)))
        for b in range(4):
            mm(b, K, r("eq", 128 * b, 128 * b + 128), r("ep", 128 * b, 128 * b + 128), aq, apl)
            (cp if t == 2 and b % 2 else act)(mem(0, K, b, 4), ps(b, K))
        if t < 2:
            for a, n in MRUNS:
                act(r("xmh", 4 * (C + a), 4 * (C + a + n)), mem(a, n), scale=0.5)
    for h, (a, n) in enumerate(YRUNS):
        quant(r("xq", a, a + n), r("xp", a, a + n), xm(4 * a, 4 * n))
        mm(4 + h, n, r("vq"), r("vp"), r("xq", a, a + n), r("xp", a, a + n))
        act(r("ysb", a, a + n), ps(4 + h, n))
        dma(lambda a=a, n=n: T.y[:, a:a + n], lambda a=a, n=n: T.ysb[:, a:a + n], [r("ysb", a, a + n)], [], lat=2200 + 2.6 * n)
    def store(q, p, a, b, o):
        dma(lambda: T.oc[:, 4 * a:4 * b], lambda: u8(r(q, a - o, b - o)), [r(q)], [], lat=2200 + 2.6 * (b - a))
        for k in range(4):
            dma(lambda k=k: T.osc[4 * k:4 * k + 4, a:b], lambda k=k: T[p][32 * k:32 * k + 4, a - o:b - o], [r(p)], [],
                eng="sp" if k < 2 else "act", lat=2300)

    if OC_SPLIT:
        store("zq", "zp", K, E, E - K)
        quant(r("mq", 0, K), r("mp", 0, K), r("mt", 0, 4 * K))
        store("mq", "mp", 0, K, 0)
    else:
        quant(r("mq"), r("mp"), r("mt"))
        store("mq", "mp", 0, E, 0)
    return ops, Q


def order(ops):
    def costs(slow, gather, scatter, fixed, pe, hop, late, more=0):
        dur = [(c + gather * x + scatter * y + fixed * z + (more if o["eng"] == "dve" else 0)) * (pe if o["eng"] == "pe" else 1)
               * (slow if o["kind"] == "c" else 1) for o in ops for c, x, y, z in [o["cost"]]]
        return dur, [o["lat"] + (late if o["kind"] != "c" else 0) for o in ops], hop

    guess = [costs(*x) for x in GUESS]
    dur, lat, hop = guess[0]
    hist = {}
    for i, o in enumerate(ops):
        dep = {}
        for x, w in [(x, False) for x in o["rd"]] + [(x, True) for x in o["wr"]]:
            for y, j, wj in hist.get(x[0], []):
                both_read = not (w or wj)
                same = ops[j]["eng"] == o["eng"] and ops[j]["kind"] == o["kind"] == "c"
                if j != i and _overlap(x, y) and not (both_read and (x[0] != "ps" or ops[j]["eng"] == o["eng"])):
                    dep[j] = dep.get(j, False) or not (same and (o["chain"] or (INORDER and w)))
        for x, w in [(x, False) for x in o["rd"]] + [(x, True) for x in o["wr"]]:
            hist.setdefault(x[0], []).append((x, i, w))
        o["dep"] = dep
    far = [0.0] * len(ops)
    for i in range(len(ops) - 1, -1, -1):
        far[i] += dur[i] + lat[i] + ops[i]["early"]
        for j in ops[i]["dep"]:
            far[j] = max(far[j], far[i] + hop[1])
    n = len(ops)
    eng = [o["eng"] for o in ops]
    behind, links = [], ([[] for o in ops], [[] for o in ops])
    for i, o in enumerate(ops):
        seen = 0
        for j in sorted(o["dep"], reverse=True):
            if not seen >> j & 1:
                gap = hop[eng[i] != eng[j]] + lat[j] if o["dep"][j] else 0
                links[0][i].append((j, gap))
                links[1][j].append((i, gap))
            seen |= (behind[j] if o["dep"][j] else 0) | 1 << j
        behind.append(seen)

    def place(urge, back):
        p, link = list(urge), links[back]
        for i in (range(n) if back else range(n - 1, -1, -1)):
            for j, gap in link[i]:
                if p[j] <= p[i]:
                    p[j] = p[i] + 1e-3
        busy, en = {e: [] for e in eng}, [0.0] * n
        for i in sorted(range(n), key=lambda i: -p[i]):
            s, d, line = lat[i] if back else 0.0, dur[i], busy[eng[i]]
            for j, gap in link[i]:
                if en[j] + gap > s:
                    s = en[j] + gap
            k = len(line)
            while k > 0 and line[k - 1][1] > s:
                k -= 1
            while k < len(line) and s + d > line[k][0]:
                if line[k][1] > s:
                    s = line[k][1]
                k += 1
            line.insert(k, (s, s + d))
            en[i] = s + d
        if back:
            return max(en), None, en
        end = [en[i] + lat[i] for i in range(n)]
        seq = sorted(range(n), key=lambda i: (en[i] - dur[i], i))
        return (max(end) + sum(w * replay(seq, *x) for w, x in zip(WEIGH, guess[1:]))) / len(guess), \
            [en[i] - dur[i] for i in range(n)], end

    def replay(seq, dur, lat, hop):
        free, en = {e: 0.0 for e in eng}, [0.0] * n
        for i in seq:
            s = free[eng[i]]
            for j, gap in links[0][i]:
                x = en[j] + hop[eng[i] != eng[j]] if gap else en[j] - lat[j]
                if x > s:
                    s = x
            free[eng[i]] = s + dur[i]
            en[i] = s + dur[i] + lat[i]
        return max(en)

    if "best" not in PLAN:
        rng = np.random.default_rng(SEED)

        def improve(best, passes):
            now = best
            for rep in range(passes):
                noise, mid = rng.normal(size=n) * SIG[rep % len(SIG)], rng.random() * best[0]
                late = place([now[2][i] + (float(noise[i]) if abs(now[2][i] - mid) < WIDE else 0) for i in range(n)], True)
                new = place(late[2], False)
                if new[0] <= best[0] + SLACK * (1 - rep / passes):
                    now = new
                if new[0] <= best[0]:
                    best = new
            return best

        tries = [improve(place(far, False), PASSES // 8) for k in range(STARTS)]
        best = improve(min(tries, key=lambda x: x[0]), PASSES - STARTS * (PASSES // 8))
        seq = sorted(range(n), key=lambda i: (best[1][i], i))

        def worth(seq):
            return sum(w * replay(seq, *x) for w, x in zip((1,) + WEIGH, guess)) / len(guess)

        now = worth(seq)
        for rep in range(MOVES):
            a = int(rng.integers(n))
            i, step, left, b = seq[a], 1 if rng.random() < 0.5 else -1, int(rng.integers(1, 5)), a
            tied = {j for j, gap in links[step > 0][i]}
            while left and 0 <= b + step < n and seq[b + step] not in tied:
                b += step
                left -= eng[seq[b]] == eng[i]
            if left:
                continue
            other = seq[:a] + seq[a + 1:]
            other.insert(b, i)
            new = worth(other)
            if new <= now:
                seq, now = other, new
        PLAN["best"] = (now, seq, best[2])
    for i, o in enumerate(ops):
        o["end"] = PLAN["best"][2][i]
    return PLAN["best"][1]


def emit(g, T, ops, Q):
    seq = order(ops)
    done = {"dve": [], "act": [], "pe": [], "pool": []}
    known = {e: {} for e in Q}
    total, last, waited = {}, {}, {}
    nd = 0
    for i in seq:
        o = ops[i]
        e = o["eng"]
        need = {}
        for j in o["dep"]:
            if not o["dep"][j]:
                continue
            s, v = ops[j]["sig"]
            if need.get(s, (0, 0))[0] < v:
                need[s] = (v, j)
        for s, (v, j) in sorted(need.items(), key=lambda kv: -ops[kv[1][1]]["end"]):
            if known[e].get(s, 0) < v:
                Q[e].wait_ge(T.sem[s], v)
                waited[s] = max(waited.get(s, 0), v)
                for s2, v2 in ops[j]["clock"].items():
                    known[e][s2] = max(known[e].get(s2, 0), v2)
        clock = dict(known[e])
        if o["kind"] == "c":
            done[e].append(i)
            o["sig"] = (e, len(done[e]))
            o["fn"]().then_inc(T.sem[e], 1)
        elif o["kind"] == "dma":
            o["sig"] = ("d%d" % nd, 16)
            nd += 1
            o["fn"]().then_inc(T.sem[o["sig"][0]], 16)
        else:
            o["fn"]()
            o["sig"] = (o["sem"][0], o["sem"][2])
            total[o["sem"][1]], last[o["sem"][1]] = o["sem"][2], o["end"]
            clock = {}
        clock[o["sig"][0]] = o["sig"][1]
        o["clock"] = clock
        total[o["sig"][0]], last[o["sig"][0]] = o["sig"][1], o["end"]
    for s, v in sorted(total.items(), key=lambda kv: last[kv[0]]):
        if waited.get(s, 0) < v:
            g.wait_ge(T.sem[s], v)


def rank_program(g, core, T, topo):
    rank = T.rank_of(core)
    if rank is None:
        return
    ops, Q = build(g, core, T, topo, rank)
    emit(g, T, ops, Q)
